import numpy as np
import ml_dtypes


def mxq(x, axis, fmt="e4m3"):
    dtype, down = {"e4m3": (ml_dtypes.float8_e4m3fn, 7), "e5m2": (ml_dtypes.float8_e5m2, 14)}[fmt]
    v = np.moveaxis(np.asarray(x, np.float32).astype(ml_dtypes.bfloat16).astype(np.float64), axis, -1)
    blocks = v.reshape(v.shape[:-1] + (-1, 32))
    amax = np.abs(blocks).max(-1, keepdims=True)
    byte = np.maximum(np.where(amax > 0, np.frexp(amax)[1] - 1 + 127, 0) - down, 1)
    scale = np.exp2(byte - 127.0)
    codes = (blocks / scale).astype(np.float32).astype(dtype).astype(np.float64)
    return np.moveaxis((codes * scale).reshape(v.shape), -1, axis)


WIDE = False


def mx_kscale(k):
    if not WIDE:
        return np.ones(k)
    levels = np.array([10, -10, 5, -5, 0])
    if k % 512:
        return np.exp2(np.random.permutation(np.resize(levels, k // 32))).repeat(32)
    a = np.empty((k // 512, 16))
    for p in range(k // 512):
        a[p, :8] = np.random.permutation(np.resize(levels, 8))
        for g in range(8):
            far = levels[np.abs(levels - a[p, g]) >= 10]
            a[p, g + 8] = far[np.random.randint(len(far))]
    return np.exp2(a.ravel()).repeat(32)


def f64(x):
    return np.asarray(x).astype(np.float64)


def striped(idx):
    return np.tile(idx.reshape(-1, 16).T, (8, 1)).astype(np.uint16)


def unstriped(offs):
    return offs[:16].T.reshape(-1).astype(np.int64)


E2M1 = np.array([0.0, 0.5, 1.0, 1.5, 2.0, 3.0, 4.0, 6.0, -0.0, -0.5, -1.0, -1.5, -2.0, -3.0, -4.0, -6.0])


def pack_weight(w, fmt):
    k, n = w.shape
    w = f64(np.asarray(w, np.float32).astype(ml_dtypes.bfloat16)).reshape(k // 32, 32, n)
    amax = np.abs(w).max(1)
    if fmt == "e4m3":
        byte = np.frexp(amax)[1] - 1 + 127 - 7
    else:
        mant, ex = np.frexp(amax / 6.0)
        byte = np.where(mant > 0.5, ex, ex - 1) + 127
    byte = np.clip(np.where(amax > 0, byte, 1), 1, 254)
    scaled = (w * np.exp2(127.0 - byte)[:, None, :]).reshape(k, n).astype(np.float32)
    by_word = np.ascontiguousarray(scaled.reshape(k // 512, 128, 4, n).transpose(0, 1, 3, 2))
    if fmt == "e4m3":
        words = by_word.astype(ml_dtypes.float8_e4m3fn).view(np.uint8)
    else:
        c = by_word.astype(ml_dtypes.float4_e2m1fn).view(np.uint8) & 0xF
        words = (c[..., 0::2] | (c[..., 1::2] << 4)).reshape(k // 512, 128, 2 * n)
    return np.ascontiguousarray(words), np.ascontiguousarray(byte.astype(np.uint8).reshape(k // 512, 16, n))


def unpack_weight(words, scales, fmt):
    g, _, n = scales.shape
    words = np.ascontiguousarray(words).reshape(g, 128, n, -1)
    if fmt == "e4m3":
        vals = words.view(ml_dtypes.float8_e4m3fn).astype(np.float64)
    else:
        nib = np.empty((g, 128, n, 4), np.uint8)
        nib[..., 0::2] = words & 0xF
        nib[..., 1::2] = words >> 4
        vals = E2M1[nib]
    vals = vals * np.repeat(np.exp2(scales.astype(np.float64) - 127.0), 8, axis=1)[..., None]
    return vals.transpose(0, 1, 3, 2).reshape(g * 512, n)


def gelu(v):
    return 0.5 * v * (1.0 + np.tanh(np.sqrt(2.0 / np.pi) * (v + 0.044715 * v**3)))


def bf(x):
    return np.asarray(x, np.float32).astype(ml_dtypes.bfloat16)


def planes(Y):
    n, m = Y.shape
    b = f64(bf(Y)).reshape(n // 32, 32, m)
    amax = np.abs(b).max(1)
    byte = np.clip(np.where(amax > 0, np.frexp(amax)[1] - 1 + 127 - 7, 1), 1, 254)
    codes = (b * np.exp2(127.0 - byte)[:, None, :]).reshape(n, m).astype(np.float32).astype(ml_dtypes.float8_e4m3fn).view(np.uint8)
    words = codes.reshape(n // 512, 128, 4, m).transpose(0, 1, 3, 2)
    return np.ascontiguousarray(words), np.ascontiguousarray(byte.astype(np.uint8).reshape(n // 512, 16, m))


K, N, T, S = 1024, 1024, 2048, 512

def setup_inputs():
    n = np.random.standard_normal
    s = mx_kscale(K)[:, None]
    u = mx_kscale(N)[:, None]
    size = np.exp(0.8 * n(N))
    tab_words, tab_scales = pack_weight(n((K, T)) * s, "e4m3")
    w1_words, w1_scales = pack_weight(n((K, N)) / np.sqrt(K) / s, "e2m1")
    w3 = 0.5 * n((N, N)) / np.sqrt(N) / u * size
    w4_words, w4_scales = pack_weight(0.5 * n((N, N)) / np.sqrt(N) / u * size, "e4m3")
    gain = np.exp(0.3 * n(N)) * u[:, 0]
    gT = n((N, T)) * size[:, None]
    offs = striped(np.random.permutation(T)[:S])
    return {"tab_words": tab_words, "tab_scales": tab_scales,
            "w1_words": w1_words, "w1_scales": w1_scales,
            "w3": w3.astype(np.float32),
            "w4_words": w4_words, "w4_scales": w4_scales,
            "gain": gain.astype(np.float32),
            "gT": gT.astype(np.float32), "offs": offs}

def reference(tab_words, tab_scales, w1_words, w1_scales, w3, w4_words, w4_scales, gain, gT, offs):
    v = unpack_weight(tab_words, tab_scales, "e4m3")[:, unstriped(offs)]
    w1 = unpack_weight(w1_words, w1_scales, "e2m1")
    w4 = unpack_weight(w4_words, w4_scales, "e4m3")
    g = f64(gT)[:, unstriped(offs)]
    draft = np.tanh(w1.T @ v)
    z = (g - draft) * f64(gain)[:, None]
    zq = mxq(z, 0, "e4m3")
    y3 = mxq(f64(w3), 0, "e4m3").T @ zq
    y4 = w4.T @ zq
    new = g + (np.abs(y3) + y4)
    y = f64(gT).copy()
    y[:, unstriped(offs)] = new
    words, scales = planes(y)
    return y, words, scales

@@ -1,0 +1,352 @@
+from contextlib import ExitStack
+
+import concourse.mybir as mybir
+from concourse.masks import make_identity
+
+K, N, T, S = 1024, 1024, 2048, 512
+FLOPS = 3 * 2 * 1024 * 1024 * 512
+
+F32 = mybir.dt.float32
+BF16 = mybir.dt.bfloat16
+I32 = mybir.dt.int32
+U32 = mybir.dt.uint32
+U16 = mybir.dt.uint16
+U8 = mybir.dt.uint8
+FP8X4 = mybir.dt.float8_e4m3fn_x4
+FP4X4 = mybir.dt.float4_e2m1fn_x4
+ACT = mybir.ActivationFunctionType
+ALU = mybir.AluOpType
+
+P = 128
+PACK = 4
+GROUPS = 2
+PAGES = GROUPS * PACK
+CHUNK = 512
+CHUNKS = T // CHUNK
+HALF = 256
+
+
+def tile_list_tablet_sign_correction_kernel(
+    tc, tab_words, tab_scales, w1_words, w1_scales, w3, w4_words, w4_scales, gain, gT, offs, out_0, out_1, out_2
+):
+    nc = tc.nc
+    with ExitStack() as ctx:
+        keep = ctx.enter_context(tc.tile_pool(name="keep", bufs=1))
+        work = ctx.enter_context(tc.tile_pool(name="work", bufs=1))
+        psum = ctx.enter_context(tc.psum_pool(name="psum", bufs=1))
+
+        offsets = keep.tile([P, S // 16], U16, name="offsets")
+        gains = keep.tile([P, GROUPS, PACK], F32, name="gains")
+        pages = [keep.tile([P, T], F32, name="page%d" % u) for u in range(PAGES)]
+        picked = [keep.tile([P, S], F32, name="picked%d" % u, align_bytes=64)[:] for u in range(2)]
+
+        tab_sc = keep.tile([P, GROUPS, T], U8, name="tab_sc", align_bytes=64)
+        w4_sc_raw = keep.tile([P, N], U8, name="w4_sc_raw", align_bytes=64)
+        w1_sc = keep.tile([P, GROUPS, N], U8, name="w1_sc", align_bytes=64)
+        w4_sc = keep.tile([P, N], U8, name="w4_sc", align_bytes=64)
+        ident = keep.tile([P, P], F32, name="ident")
+        v_q = [keep.tile([P, S], I32, name="v_q%d" % a, align_bytes=64) for a in range(GROUPS)]
+        v_sc = [keep.tile([P, S], U8, name="v_sc%d" % a, align_bytes=64) for a in range(GROUPS)]
+        z_q = [keep.tile([P, S], I32, name="z_q%d" % a, align_bytes=64) for a in range(GROUPS)]
+        z_sc = [keep.tile([P, S], U8, name="z_sc%d" % a, align_bytes=64) for a in range(GROUPS)]
+        w4_q = [keep.tile([P, CHUNK], I32, name="w4_q%d" % a, align_bytes=64) for a in range(GROUPS)]
+        w3_q = {}
+        w3_sc = {}
+        for g in range(GROUPS):
+            for a in range(GROUPS):
+                for h in range(2):
+                    w3_q[g, a, h] = keep.tile([P, HALF], I32, name="w3_q%d%d%d" % (g, a, h), align_bytes=64)
+                    if g == 0 and a == 0 and h == 0:
+                        w3_sc[g, a, h] = z_sc[1][4:P, 0:HALF]
+                    else:
+                        w3_sc[g, a, h] = keep.tile([P, HALF], U8, name="w3_sc%d%d%d" % (g, a, h), align_bytes=64)[:]
+        z_woven = [keep.tile([P, S * PACK], BF16, name="z_woven%d" % g, align_bytes=64) for g in range(GROUPS)]
+        y_sc = [keep.tile([P, CHUNK], U8, name="y_sc%d" % g, align_bytes=64) for g in range(GROUPS)]
+
+        def bank(b, name):
+            return psum.tile([P, S], F32, name=name, tag="bank%d" % b)
+
+        nc.vector.memset(tab_sc[:].rearrange("p a n -> p (a n)").bitcast(I32), 0)
+        nc.gpsimd.memset(w1_sc[:].rearrange("p a n -> p (a n)").bitcast(I32), 0)
+        nc.gpsimd.memset(w4_sc_raw[:].bitcast(I32), 0)
+        make_identity(nc, ident[:])
+
+        g_rows = gT.rearrange("(g p t) c -> g t p c", g=GROUPS, t=PACK)
+        out_rows = out_0.rearrange("(g p t) c -> g t p c", g=GROUPS, t=PACK)
+
+        def load_scales(dst, src):
+            for q in range(4):
+                nc.sync.dma_start(
+                    out=dst[32 * q : 32 * q + 4, :, :].bitcast(I32),
+                    in_=src[:, 4 * q : 4 * q + 4, :].bitcast(I32).rearrange("a r n -> r a n"),
+                )
+
+        def load_table(a):
+            words = work.tile([P, T], I32, name="tab%d" % a, align_bytes=64)
+            nc.sync.dma_start(out=words[:], in_=tab_words[a].rearrange("p n t -> p (n t)").bitcast(I32))
+            return words
+
+        def load_w3(g, a):
+            raw = work.tile([P, PACK, CHUNK], F32, name="w3raw%d%d" % (g, a), align_bytes=64)
+            nc.sync.dma_start(
+                out=raw[:],
+                in_=w3[512 * a : 512 * (a + 1), CHUNK * g : CHUNK * (g + 1)].rearrange("(p j) c -> p j c", j=PACK),
+            )
+            return raw
+
+        def load_w4(g):
+            raw = work.tile([P, GROUPS, CHUNK], I32, name="w4raw%d" % g, align_bytes=64)
+            nc.sync.dma_start(
+                out=raw[:],
+                in_=w4_words.rearrange("a p n t -> p a (n t)").bitcast(I32)[:, :, CHUNK * g : CHUNK * (g + 1)],
+            )
+            return raw
+
+        nc.sync.dma_start(offsets[:], offs)
+        tab = [load_table(0)]
+        load_scales(tab_sc, tab_scales)
+        w1_q = keep.tile([P, GROUPS, 2 * N], U8, name="w1_q", align_bytes=64)
+        nc.sync.dma_start(out=w1_q[:].bitcast(I32), in_=w1_words.bitcast(I32).rearrange("a p c -> p a c"))
+        load_scales(w1_sc, w1_scales)
+        tab.append(load_table(1))
+        w4_raw = [load_w4(0)]
+        for q in range(4):
+            nc.sync.dma_start(
+                out=w4_sc_raw[32 * q + 4 : 32 * q + 12, :].bitcast(I32),
+                in_=w4_scales[:, 4 * q : 4 * q + 4, :].bitcast(I32),
+            )
+        for u in range(PAGES):
+            nc.sync.dma_start(out=pages[u][:], in_=g_rows[u // PACK, u % PACK])
+            if u == 0:
+                nc.sync.dma_start(out=gains[:], in_=gain.rearrange("(g p t) -> p g t", g=GROUPS, t=PACK))
+        w3_raw = {(0, 0): load_w3(0, 0)}
+        w3_raw[0, 1] = load_w3(0, 1)
+        w3_raw[1, 0] = load_w3(1, 0)
+        w3_raw[1, 1] = load_w3(1, 1)
+        w4_raw.append(load_w4(1))
+
+        nc.vector.tensor_copy(v_q[0][:].bitcast(U32), tab[0][:].bitcast(U32).indirect(offsets[:]))
+        for a in range(GROUPS):
+            nc.vector.tensor_copy(v_sc[a][:], tab_sc[:, a, :].indirect(offsets[:]))
+        nc.vector.tensor_copy(v_q[1][:].bitcast(U32), tab[1][:].bitcast(U32).indirect(offsets[:]))
+
+        gd = []
+        for g in range(GROUPS):
+            turned = []
+            for jb in range(S // P):
+                cols = slice(P * jb, P * (jb + 1))
+                acc = bank(PACK * g + jb, "draft%d%d" % (g, jb))
+                for a in range(GROUPS):
+                    nc.tensor.matmul_mx(
+                        out=acc[:],
+                        lhsT=v_q[a][:, cols].bitcast(FP8X4),
+                        lhsT_scale=v_sc[a][:, cols],
+                        rhs=w1_q[:, a, 1024 * g : 1024 * (g + 1)].bitcast(FP4X4),
+                        rhs_scale=w1_sc[:, a, 512 * g : 512 * (g + 1)],
+                        start=(a == 0),
+                        stop=(a == GROUPS - 1),
+                    )
+                draft_t = work.tile([P, PACK, P], F32, name="draft_t%d%d" % (g, jb), tag="tmp", bufs=8)
+                nc.scalar.activation(draft_t[:], acc[:].rearrange("p (m t) -> p t m", t=PACK), ACT.Tanh)
+                turned.append(draft_t)
+            for t in range(PACK):
+                draft = bank(PACK * (1 - g) + t, "draft_page%d%d" % (g, t))
+                for jb in range(S // P):
+                    nc.tensor.transpose(draft[:, P * jb : P * (jb + 1)], turned[jb][:, t, :], ident[:])
+                scaled = keep.tile([P, S], F32, name="gd%d%d" % (g, t), align_bytes=64)
+                nc.scalar.activation(scaled[:], draft[:], ACT.Copy, scale=gains[:, g, t : t + 1])
+                gd.append(scaled[:])
+        for u in range(2, PAGES):
+            picked.append(z_woven[0][:].bitcast(F32)[:, 0:S] if u == 7 else gd[u - 2])
+
+        def quantise_z(g):
+            rows = work.tile([P, PACK, S], BF16, name="z_rows%d" % g, tag="bf", bufs=4, align_bytes=64)
+            for t in range(PACK):
+                u = PACK * g + t
+                nc.vector.tensor_copy(picked[u], pages[u][:].indirect(offsets[:]))
+                nc.vector.scalar_tensor_tensor(
+                    rows[:, t, :], picked[u], gains[:, g, t : t + 1], gd[u], ALU.mult, ALU.subtract
+                )
+            dst = z_woven[g][:].rearrange("p (c i t) -> p c t i", i=4, t=PACK)
+            src = rows[:].rearrange("p t (c i) -> p c t i", i=4)
+            if g == 0:
+                nc.scalar.copy(dst, src)
+            else:
+                nc.vector.tensor_copy(dst, src)
+            nc.vector.quantize_mx(out=z_q[g][:].bitcast(FP8X4), scales=z_sc[g][:], in_=z_woven[g][:])
+
+        def weave_w3(g, a, h, on_vector, woven):
+            dst = woven.rearrange("p (t m j) -> p m j t", t=2, j=PACK)
+            src = w3_raw[g, a][:].rearrange("p j (m t) -> p m j t", t=PACK)[:, :, :, 2 * h : 2 * h + 2]
+            if on_vector:
+                nc.vector.tensor_copy(dst, src)
+            else:
+                nc.scalar.copy(dst, src)
+            nc.vector.quantize_mx(out=w3_q[g, a, h][:].bitcast(FP8X4), scales=w3_sc[g, a, h], in_=woven)
+
+        def deal_w4(g):
+            for a in range(GROUPS):
+                nc.vector.tensor_copy(
+                    out=w4_q[a][:].rearrange("p (t m) -> p m t", t=PACK),
+                    in_=w4_raw[g][:, a, :].rearrange("p (m t) -> p m t", t=PACK),
+                )
+
+        def y3_pass(acc, u, a):
+            g, t = divmod(u, PACK)
+            cols = slice(P * (t % 2), P * (t % 2 + 1))
+            nc.tensor.matmul_mx(
+                out=acc[:],
+                lhsT=w3_q[g, a, t // 2][:, cols].bitcast(FP8X4),
+                lhsT_scale=w3_sc[g, a, t // 2][:, cols],
+                rhs=z_q[a][:].bitcast(FP8X4),
+                rhs_scale=z_sc[a][:],
+                start=(a == 0),
+                stop=(a == GROUPS - 1),
+            )
+
+        def y4_pass(acc, u, a):
+            g, t = divmod(u, PACK)
+            nc.tensor.matmul_mx(
+                out=acc[:],
+                lhsT=w4_q[a][:, P * t : P * (t + 1)].bitcast(FP8X4),
+                lhsT_scale=w4_sc[4 + 4 * a : P, P * u : P * (u + 1)],
+                rhs=z_q[a][:].bitcast(FP8X4),
+                rhs_scale=z_sc[a][:],
+                start=(a == 0),
+                stop=(a == GROUPS - 1),
+            )
+
+        deal_w4(0)
+        nc.vector.tensor_copy(
+            out=w4_sc[:].rearrange("p (g t m) -> p g m t", g=GROUPS, t=PACK),
+            in_=w4_sc_raw[:].rearrange("p (g m t) -> p g m t", g=GROUPS, t=PACK),
+        )
+        quantise_z(0)
+        quantise_z(1)
+        for h in range(2):
+            weave_w3(0, 0, h, False, gd[6 + h].bitcast(BF16))
+            weave_w3(0, 1, h, h == 0, z_woven[1][:, 1024 * h : 1024 * (h + 1)])
+
+        y3 = {}
+        y4 = {}
+
+        def products(u, bank3, bank4):
+            y3[u] = bank(bank3, "y3_%d" % u)
+            y4[u] = bank(bank4, "y4_%d" % u)
+            for a in range(GROUPS):
+                y3_pass(y3[u], u, a)
+            for a in range(GROUPS):
+                y4_pass(y4[u], u, a)
+
+        mag = {}
+        base = {}
+
+        def take_abs(u):
+            if u == 0:
+                mag[u] = gd[5]
+            else:
+                mag[u] = work.tile([P, S], F32, name="mag%d" % u, tag="tmp", bufs=8)[:]
+            nc.scalar.activation(mag[u], y3[u][:], ACT.Abs)
+
+        def add_state(u):
+            if u in (0, 2):
+                base[u] = z_woven[0][:].bitcast(F32)[:, S : 2 * S]
+            elif u == 3:
+                base[u] = mag[0]
+            else:
+                base[u] = work.tile([P, S], F32, name="base%d" % u, tag="tmp", bufs=8)[:]
+            nc.vector.tensor_tensor(base[u], y4[u][:], picked[u], ALU.add)
+
+        def scatter(u):
+            nc.vector.tensor_tensor(pages[u][:].indirect(offsets[:]), base[u], mag[u], ALU.add)
+            nc.sync.dma_start(out=out_rows[u // PACK, u % PACK], in_=pages[u][:])
+
+        def round_page(u, first, count, on_vector):
+            g, t = divmod(u, PACK)
+            raw = w3_raw[1 - g, 1 - first // 2][:].bitcast(BF16).rearrange("p (c u) (m e) -> p c u m e", u=2, e=2)
+            dst = raw[:, first % 2 : first % 2 + count, t // 2, :, t % 2]
+            src = pages[u][:, CHUNK * first : CHUNK * (first + count)].rearrange("p (c m) -> p c m", c=count)
+            if on_vector:
+                nc.vector.tensor_copy(dst, src)
+            else:
+                nc.scalar.copy(dst, src)
+
+        def finish_chunk(g, c, on_vector):
+            woven = work.tile([P, CHUNK * PACK], BF16, name="y_woven%d%d" % (g, c), tag="bf", bufs=4, align_bytes=64)
+            dst = woven[:].bitcast(F32).rearrange("p (m u) -> p m u", u=2)
+            src = w3_raw[1 - g, 1 - c // 2][:, 2 * (c % 2) : 2 * (c % 2) + 2, :].rearrange("p u m -> p m u")
+            if on_vector:
+                nc.vector.tensor_copy(dst, src)
+            else:
+                nc.scalar.copy(dst, src)
+            codes = work.tile([P, CHUNK], I32, name="y_q%d%d" % (g, c), tag="y_q", bufs=8, align_bytes=64)
+            nc.vector.quantize_mx(out=codes[:].bitcast(FP8X4), scales=y_sc[g][4 * c : P, :], in_=woven[:])
+            nc.sync.dma_start(
+                out=out_1[g].rearrange("p m t -> p (m t)").bitcast(I32)[:, CHUNK * c : CHUNK * (c + 1)], in_=codes[:]
+            )
+
+        def store_scales(g):
+            for q in range(4):
+                nc.sync.dma_start(
+                    out=out_2[g, 4 * q : 4 * q + 4, :].bitcast(I32).rearrange("r (c m) -> c r m", c=CHUNKS),
+                    in_=y_sc[g][32 * q : 32 * q + 16, :].bitcast(I32),
+                )
+
+        products(0, 1, 0)
+        take_abs(0)
+        add_state(0)
+        products(1, 0, 1)
+        take_abs(1)
+        scatter(0)
+        add_state(1)
+        products(2, 0, 1)
+        scatter(1)
+        weave_w3(1, 0, 0, False, picked[0].bitcast(BF16))
+        weave_w3(1, 0, 1, False, z_woven[1][:, 1024:2048])
+        take_abs(2)
+        weave_w3(1, 1, 0, False, mag[0].bitcast(BF16))
+        weave_w3(1, 1, 1, False, base[0].bitcast(BF16))
+        add_state(2)
+        products(3, 0, 1)
+        take_abs(3)
+        deal_w4(1)
+        add_state(3)
+        for u in range(PACK, PAGES - 1):
+            products(u, 2 * (u - PACK) + 2, 2 * (u - PACK) + 3)
+        products(PAGES - 1, 0, 1)
+        scatter(2)
+        add_state(4)
+        scatter(3)
+
+        def round_whole(u):
+            for first in (0, 2):
+                round_page(u, first, 2, False)
+
+        round_whole(0)
+        round_whole(1)
+        take_abs(4)
+        add_state(5)
+        scatter(4)
+        round_whole(2)
+        take_abs(5)
+        add_state(6)
+        scatter(5)
+        round_whole(3)
+        take_abs(6)
+        add_state(7)
+        scatter(6)
+        for c in range(CHUNKS):
+            finish_chunk(0, c, False)
+        store_scales(0)
+        take_abs(7)
+        scatter(7)
+        round_whole(4)
+        round_whole(5)
+        round_page(6, 0, 2, False)
+        round_page(6, 2, 1, False)
+        round_page(6, 3, 1, True)
+        for c in (3, 2, 0, 1):
+            round_page(7, c, 1, c == CHUNKS - 1)
+        for c in (3, 2, 0, 1):
+            finish_chunk(1, c, c != 1)
+        store_scales(1)

@@ -86,13 +86,14 @@ def tile_list_tablet_sign_correction_kernel(
             nc.sync.dma_start(out=words[:], in_=tab_words[a].rearrange("p n t -> p (n t)").bitcast(I32))
             return words
 
+        w3_raw = [keep.tile([P, PACK, CHUNK], F32, name="w3_raw%d" % a, align_bytes=64) for a in range(GROUPS)]
+        pair_tiles = [keep.tile([P, PACK, CHUNK], F32, name="pairs%d" % a, align_bytes=64) for a in range(2)]
+
         def load_w3(g, a):
-            raw = work.tile([P, PACK, CHUNK], F32, name="w3raw%d%d" % (g, a), align_bytes=64)
             nc.sync.dma_start(
-                out=raw[:],
+                out=w3_raw[a][:],
                 in_=w3[512 * a : 512 * (a + 1), CHUNK * g : CHUNK * (g + 1)].rearrange("(p j) c -> p j c", j=PACK),
             )
-            return raw
 
         def load_w4(g):
             raw = work.tile([P, GROUPS, CHUNK], I32, name="w4raw%d" % g, align_bytes=64)
@@ -119,10 +120,8 @@ def tile_list_tablet_sign_correction_kernel(
             nc.sync.dma_start(out=pages[u][:], in_=g_rows[u // PACK, u % PACK])
             if u == 0:
                 nc.sync.dma_start(out=gains[:], in_=gain.rearrange("(g p t) -> p g t", g=GROUPS, t=PACK))
-        w3_raw = {(0, 0): load_w3(0, 0)}
-        w3_raw[0, 1] = load_w3(0, 1)
-        w3_raw[1, 0] = load_w3(1, 0)
-        w3_raw[1, 1] = load_w3(1, 1)
+        load_w3(0, 0)
+        load_w3(0, 1)
         w4_raw.append(load_w4(1))
 
         nc.vector.tensor_copy(v_q[0][:].bitcast(U32), tab[0][:].bitcast(U32).indirect(offsets[:]))
@@ -146,7 +145,7 @@ def tile_list_tablet_sign_correction_kernel(
                         start=(a == 0),
                         stop=(a == GROUPS - 1),
                     )
-                draft_t = work.tile([P, PACK, P], F32, name="draft_t%d%d" % (g, jb), tag="tmp", bufs=8)
+                draft_t = work.tile([P, PACK, P], F32, name="draft_t%d%d" % (g, jb), tag="tmp", bufs=10)
                 nc.scalar.activation(draft_t[:], acc[:].rearrange("p (m t) -> p t m", t=PACK), ACT.Tanh)
                 turned.append(draft_t)
             for t in range(PACK):
@@ -172,12 +171,13 @@ def tile_list_tablet_sign_correction_kernel(
             if g == 0:
                 nc.scalar.copy(dst, src)
             else:
-                nc.vector.tensor_copy(dst, src)
+                nc.scalar.copy(dst[:, :, 0:2, :], src[:, :, 0:2, :])
+                nc.vector.tensor_copy(dst[:, :, 2:4, :], src[:, :, 2:4, :])
             nc.vector.quantize_mx(out=z_q[g][:].bitcast(FP8X4), scales=z_sc[g][:], in_=z_woven[g][:])
 
-        def weave_w3(g, a, h, on_vector, woven):
+        def weave_w3(g, a, h, woven, on_vector=False):
             dst = woven.rearrange("p (t m j) -> p m j t", t=2, j=PACK)
-            src = w3_raw[g, a][:].rearrange("p j (m t) -> p m j t", t=PACK)[:, :, :, 2 * h : 2 * h + 2]
+            src = w3_raw[a][:].rearrange("p j (m t) -> p m j t", t=PACK)[:, :, :, 2 * h : 2 * h + 2]
             if on_vector:
                 nc.vector.tensor_copy(dst, src)
             else:
@@ -223,9 +223,8 @@ def tile_list_tablet_sign_correction_kernel(
         )
         quantise_z(0)
         quantise_z(1)
-        for h in range(2):
-            weave_w3(0, 0, h, False, gd[6 + h].bitcast(BF16))
-            weave_w3(0, 1, h, h == 0, z_woven[1][:, 1024 * h : 1024 * (h + 1)])
+        weave_w3(0, 0, 0, gd[6].bitcast(BF16))
+        weave_w3(0, 1, 0, z_woven[1][:, 0:1024], on_vector=True)
 
         y3 = {}
         y4 = {}
@@ -242,28 +241,28 @@ def tile_list_tablet_sign_correction_kernel(
         base = {}
 
         def take_abs(u):
-            if u == 0:
-                mag[u] = gd[5]
-            else:
-                mag[u] = work.tile([P, S], F32, name="mag%d" % u, tag="tmp", bufs=8)[:]
+            mag[u] = work.tile([P, S], F32, name="mag%d" % u, tag="tmp", bufs=10)[:]
             nc.scalar.activation(mag[u], y3[u][:], ACT.Abs)
 
         def add_state(u):
-            if u in (0, 2):
+            if u == 2:
                 base[u] = z_woven[0][:].bitcast(F32)[:, S : 2 * S]
             elif u == 3:
-                base[u] = mag[0]
+                base[u] = gd[5]
             else:
-                base[u] = work.tile([P, S], F32, name="base%d" % u, tag="tmp", bufs=8)[:]
+                base[u] = work.tile([P, S], F32, name="base%d" % u, tag="tmp", bufs=10)[:]
             nc.vector.tensor_tensor(base[u], y4[u][:], picked[u], ALU.add)
 
         def scatter(u):
             nc.vector.tensor_tensor(pages[u][:].indirect(offsets[:]), base[u], mag[u], ALU.add)
             nc.sync.dma_start(out=out_rows[u // PACK, u % PACK], in_=pages[u][:])
 
+        def stage(g, c):
+            return (w3_raw if g == 0 else pair_tiles)[c // 2]
+
         def round_page(u, first, count, on_vector):
             g, t = divmod(u, PACK)
-            raw = w3_raw[1 - g, 1 - first // 2][:].bitcast(BF16).rearrange("p (c u) (m e) -> p c u m e", u=2, e=2)
+            raw = stage(g, first)[:].bitcast(BF16).rearrange("p (c u) (m e) -> p c u m e", u=2, e=2)
             dst = raw[:, first % 2 : first % 2 + count, t // 2, :, t % 2]
             src = pages[u][:, CHUNK * first : CHUNK * (first + count)].rearrange("p (c m) -> p c m", c=count)
             if on_vector:
@@ -274,12 +273,12 @@ def tile_list_tablet_sign_correction_kernel(
         def finish_chunk(g, c, on_vector):
             woven = work.tile([P, CHUNK * PACK], BF16, name="y_woven%d%d" % (g, c), tag="bf", bufs=4, align_bytes=64)
             dst = woven[:].bitcast(F32).rearrange("p (m u) -> p m u", u=2)
-            src = w3_raw[1 - g, 1 - c // 2][:, 2 * (c % 2) : 2 * (c % 2) + 2, :].rearrange("p u m -> p m u")
+            src = stage(g, c)[:, 2 * (c % 2) : 2 * (c % 2) + 2, :].rearrange("p u m -> p m u")
             if on_vector:
                 nc.vector.tensor_copy(dst, src)
             else:
                 nc.scalar.copy(dst, src)
-            codes = work.tile([P, CHUNK], I32, name="y_q%d%d" % (g, c), tag="y_q", bufs=8, align_bytes=64)
+            codes = work.tile([P, CHUNK], I32, name="y_q%d%d" % (g, c), tag="y_q", bufs=6, align_bytes=64)
             nc.vector.quantize_mx(out=codes[:].bitcast(FP8X4), scales=y_sc[g][4 * c : P, :], in_=woven[:])
             nc.sync.dma_start(
                 out=out_1[g].rearrange("p m t -> p (m t)").bitcast(I32)[:, CHUNK * c : CHUNK * (c + 1)], in_=codes[:]
@@ -295,17 +294,21 @@ def tile_list_tablet_sign_correction_kernel(
         products(0, 1, 0)
         take_abs(0)
         add_state(0)
+        weave_w3(0, 0, 1, gd[7].bitcast(BF16))
+        load_w3(1, 0)
+        weave_w3(0, 1, 1, z_woven[1][:, 1024:2048])
+        load_w3(1, 1)
         products(1, 0, 1)
         take_abs(1)
         scatter(0)
         add_state(1)
         products(2, 0, 1)
         scatter(1)
-        weave_w3(1, 0, 0, False, picked[0].bitcast(BF16))
-        weave_w3(1, 0, 1, False, z_woven[1][:, 1024:2048])
         take_abs(2)
-        weave_w3(1, 1, 0, False, mag[0].bitcast(BF16))
-        weave_w3(1, 1, 1, False, base[0].bitcast(BF16))
+        weave_w3(1, 0, 0, gd[6].bitcast(BF16))
+        weave_w3(1, 0, 1, gd[7].bitcast(BF16))
+        weave_w3(1, 1, 0, gd[5].bitcast(BF16))
+        weave_w3(1, 1, 1, z_woven[0][:, 1024:2048])
         add_state(2)
         products(3, 0, 1)
         take_abs(3)
@@ -340,11 +343,10 @@ def tile_list_tablet_sign_correction_kernel(
         store_scales(0)
         take_abs(7)
         scatter(7)
-        round_whole(4)
-        round_whole(5)
-        round_page(6, 0, 2, False)
-        round_page(6, 2, 1, False)
-        round_page(6, 3, 1, True)
+        for u in (4, 5, 6):
+            round_page(u, 0, 2, False)
+            round_page(u, 2, 1, False)
+            round_page(u, 3, 1, True)
         for c in (3, 2, 0, 1):
             round_page(7, c, 1, c == CHUNKS - 1)
         for c in (3, 2, 0, 1):

@@ -52,14 +52,20 @@ def tile_list_tablet_sign_correction_kernel(
         w4_q = [keep.tile([P, CHUNK], I32, name="w4_q%d" % a, align_bytes=64) for a in range(GROUPS)]
         w3_q = {}
         w3_sc = {}
-        for g in range(GROUPS):
-            for a in range(GROUPS):
-                for h in range(2):
-                    w3_q[g, a, h] = keep.tile([P, HALF], I32, name="w3_q%d%d%d" % (g, a, h), align_bytes=64)
-                    if g == 0 and a == 0 and h == 0:
-                        w3_sc[g, a, h] = z_sc[1][4:P, 0:HALF]
-                    else:
-                        w3_sc[g, a, h] = keep.tile([P, HALF], U8, name="w3_sc%d%d%d" % (g, a, h), align_bytes=64)[:]
+        for a in range(GROUPS):
+            for h in range(2):
+                w3_q[0, a, h] = keep.tile([P, HALF], I32, name="w3_q0%d%d" % (a, h), align_bytes=64)[:]
+                if a == 0 and h == 0:
+                    w3_sc[0, a, h] = z_sc[1][4:P, 0:HALF]
+                else:
+                    w3_sc[0, a, h] = keep.tile([P, HALF], U8, name="w3_sc0%d%d" % (a, h), align_bytes=64)[:]
+        w3_q1 = [keep.tile([P, CHUNK], I32, name="w3_q1%d" % a, align_bytes=64) for a in range(GROUPS)]
+        w3_sc1 = [keep.tile([P, CHUNK], U8, name="w3_sc1%d" % a, align_bytes=64) for a in range(GROUPS)]
+        for a in range(GROUPS):
+            for h in range(2):
+                w3_q[1, a, h] = w3_q1[a][:, HALF * h : HALF * (h + 1)]
+                w3_sc[1, a, h] = w3_sc1[a][:, HALF * h : HALF * (h + 1)]
+        last_two = keep.tile([P, 2 * S], F32, name="last_two", align_bytes=64)
         z_woven = [keep.tile([P, S * PACK], BF16, name="z_woven%d" % g, align_bytes=64) for g in range(GROUPS)]
         y_sc = [keep.tile([P, CHUNK], U8, name="y_sc%d" % g, align_bytes=64) for g in range(GROUPS)]
 
@@ -152,9 +158,12 @@ def tile_list_tablet_sign_correction_kernel(
                 draft = bank(PACK * (1 - g) + t, "draft_page%d%d" % (g, t))
                 for jb in range(S // P):
                     nc.tensor.transpose(draft[:, P * jb : P * (jb + 1)], turned[jb][:, t, :], ident[:])
-                scaled = keep.tile([P, S], F32, name="gd%d%d" % (g, t), align_bytes=64)
-                nc.scalar.activation(scaled[:], draft[:], ACT.Copy, scale=gains[:, g, t : t + 1])
-                gd.append(scaled[:])
+                if g == 1 and t >= 2:
+                    scaled = last_two[:, S * (t - 2) : S * (t - 1)]
+                else:
+                    scaled = keep.tile([P, S], F32, name="gd%d%d" % (g, t), align_bytes=64)[:]
+                nc.scalar.activation(scaled, draft[:], ACT.Copy, scale=gains[:, g, t : t + 1])
+                gd.append(scaled)
         for u in range(2, PAGES):
             picked.append(z_woven[0][:].bitcast(F32)[:, 0:S] if u == 7 else gd[u - 2])
 
@@ -182,7 +191,14 @@ def tile_list_tablet_sign_correction_kernel(
                 nc.vector.tensor_copy(dst, src)
             else:
                 nc.scalar.copy(dst, src)
-            nc.vector.quantize_mx(out=w3_q[g, a, h][:].bitcast(FP8X4), scales=w3_sc[g, a, h], in_=woven)
+            nc.vector.quantize_mx(out=w3_q[g, a, h].bitcast(FP8X4), scales=w3_sc[g, a, h], in_=woven)
+
+        def weave_w3_whole(a, woven):
+            nc.scalar.copy(
+                woven.rearrange("p (t m j) -> p m j t", t=PACK, j=PACK),
+                w3_raw[a][:].rearrange("p j (m t) -> p m j t", t=PACK),
+            )
+            nc.vector.quantize_mx(out=w3_q1[a][:].bitcast(FP8X4), scales=w3_sc1[a][:], in_=woven)
 
         def deal_w4(g):
             for a in range(GROUPS):
@@ -245,10 +261,8 @@ def tile_list_tablet_sign_correction_kernel(
             nc.scalar.activation(mag[u], y3[u][:], ACT.Abs)
 
         def add_state(u):
-            if u == 2:
-                base[u] = z_woven[0][:].bitcast(F32)[:, S : 2 * S]
-            elif u == 3:
-                base[u] = gd[5]
+            if u in (2, 3):
+                base[u] = gd[u + 4]
             else:
                 base[u] = work.tile([P, S], F32, name="base%d" % u, tag="tmp", bufs=10)[:]
             nc.vector.tensor_tensor(base[u], y4[u][:], picked[u], ALU.add)
@@ -270,10 +284,21 @@ def tile_list_tablet_sign_correction_kernel(
             else:
                 nc.scalar.copy(dst, src)
 
+        def rounded_rows(c):
+            return w3_raw[c // 2][:].bitcast(BF16)
+
+        def round_rows(u):
+            for first in (0, 2):
+                nc.scalar.copy(rounded_rows(first)[:, u, :], pages[u][:, CHUNK * first : CHUNK * (first + 2)])
+
         def finish_chunk(g, c, on_vector):
             woven = work.tile([P, CHUNK * PACK], BF16, name="y_woven%d%d" % (g, c), tag="bf", bufs=4, align_bytes=64)
-            dst = woven[:].bitcast(F32).rearrange("p (m u) -> p m u", u=2)
-            src = stage(g, c)[:, 2 * (c % 2) : 2 * (c % 2) + 2, :].rearrange("p u m -> p m u")
+            if g == 0:
+                dst = woven[:].rearrange("p (c i t) -> p c t i", i=4, t=PACK)
+                src = rounded_rows(c)[:, :, CHUNK * (c % 2) : CHUNK * (c % 2 + 1)].rearrange("p t (c i) -> p c t i", i=4)
+            else:
+                dst = woven[:].bitcast(F32).rearrange("p (m u) -> p m u", u=2)
+                src = stage(g, c)[:, 2 * (c % 2) : 2 * (c % 2) + 2, :].rearrange("p u m -> p m u")
             if on_vector:
                 nc.vector.tensor_copy(dst, src)
             else:
@@ -305,10 +330,8 @@ def tile_list_tablet_sign_correction_kernel(
         products(2, 0, 1)
         scatter(1)
         take_abs(2)
-        weave_w3(1, 0, 0, gd[6].bitcast(BF16))
-        weave_w3(1, 0, 1, gd[7].bitcast(BF16))
-        weave_w3(1, 1, 0, gd[5].bitcast(BF16))
-        weave_w3(1, 1, 1, z_woven[0][:, 1024:2048])
+        weave_w3_whole(0, z_woven[1][:])
+        weave_w3_whole(1, last_two[:].bitcast(BF16))
         add_state(2)
         products(3, 0, 1)
         take_abs(3)
@@ -325,30 +348,31 @@ def tile_list_tablet_sign_correction_kernel(
             for first in (0, 2):
                 round_page(u, first, 2, False)
 
-        round_whole(0)
-        round_whole(1)
+        round_rows(0)
+        round_rows(1)
         take_abs(4)
         add_state(5)
         scatter(4)
-        round_whole(2)
+        round_rows(2)
         take_abs(5)
         add_state(6)
         scatter(5)
-        round_whole(3)
+        round_rows(3)
         take_abs(6)
         add_state(7)
         scatter(6)
+        take_abs(7)
+        scatter(7)
         for c in range(CHUNKS):
             finish_chunk(0, c, False)
         store_scales(0)
-        take_abs(7)
-        scatter(7)
-        for u in (4, 5, 6):
+        for u in (4, 5):
             round_page(u, 0, 2, False)
             round_page(u, 2, 1, False)
             round_page(u, 3, 1, True)
-        for c in (3, 2, 0, 1):
-            round_page(7, c, 1, c == CHUNKS - 1)
+        for u in (6, 7):
+            round_page(u, 0, 2, False)
+            round_page(u, 2, 2, True)
         for c in (3, 2, 0, 1):
             finish_chunk(1, c, c != 1)
         store_scales(1)

@@ -23,7 +23,7 @@ GROUPS = 2
 PAGES = GROUPS * PACK
 CHUNK = 512
 CHUNKS = T // CHUNK
-HALF = 256
+HALF = S // 2
 
 
 def tile_list_tablet_sign_correction_kernel(
@@ -32,215 +32,275 @@ def tile_list_tablet_sign_correction_kernel(
     nc = tc.nc
     with ExitStack() as ctx:
         keep = ctx.enter_context(tc.tile_pool(name="keep", bufs=1))
-        work = ctx.enter_context(tc.tile_pool(name="work", bufs=1))
         psum = ctx.enter_context(tc.psum_pool(name="psum", bufs=1))
 
-        offsets = keep.tile([P, S // 16], U16, name="offsets")
-        gains = keep.tile([P, GROUPS, PACK], F32, name="gains")
-        pages = [keep.tile([P, T], F32, name="page%d" % u) for u in range(PAGES)]
-        picked = [keep.tile([P, S], F32, name="picked%d" % u, align_bytes=64)[:] for u in range(2)]
-
-        tab_sc = keep.tile([P, GROUPS, T], U8, name="tab_sc", align_bytes=64)
-        w4_sc_raw = keep.tile([P, N], U8, name="w4_sc_raw", align_bytes=64)
-        w1_sc = keep.tile([P, GROUPS, N], U8, name="w1_sc", align_bytes=64)
-        w4_sc = keep.tile([P, N], U8, name="w4_sc", align_bytes=64)
-        ident = keep.tile([P, P], F32, name="ident")
-        v_q = [keep.tile([P, S], I32, name="v_q%d" % a, align_bytes=64) for a in range(GROUPS)]
-        v_sc = [keep.tile([P, S], U8, name="v_sc%d" % a, align_bytes=64) for a in range(GROUPS)]
-        z_q = [keep.tile([P, S], I32, name="z_q%d" % a, align_bytes=64) for a in range(GROUPS)]
-        z_sc = [keep.tile([P, S], U8, name="z_sc%d" % a, align_bytes=64) for a in range(GROUPS)]
-        w4_q = [keep.tile([P, CHUNK], I32, name="w4_q%d" % a, align_bytes=64) for a in range(GROUPS)]
-        w3_q = {}
-        w3_sc = {}
-        for a in range(GROUPS):
-            for h in range(2):
-                w3_q[0, a, h] = keep.tile([P, HALF], I32, name="w3_q0%d%d" % (a, h), align_bytes=64)[:]
-                if a == 0 and h == 0:
-                    w3_sc[0, a, h] = z_sc[1][4:P, 0:HALF]
-                else:
-                    w3_sc[0, a, h] = keep.tile([P, HALF], U8, name="w3_sc0%d%d" % (a, h), align_bytes=64)[:]
-        w3_q1 = [keep.tile([P, CHUNK], I32, name="w3_q1%d" % a, align_bytes=64) for a in range(GROUPS)]
-        w3_sc1 = [keep.tile([P, CHUNK], U8, name="w3_sc1%d" % a, align_bytes=64) for a in range(GROUPS)]
-        for a in range(GROUPS):
-            for h in range(2):
-                w3_q[1, a, h] = w3_q1[a][:, HALF * h : HALF * (h + 1)]
-                w3_sc[1, a, h] = w3_sc1[a][:, HALF * h : HALF * (h + 1)]
-        last_two = keep.tile([P, 2 * S], F32, name="last_two", align_bytes=64)
-        z_woven = [keep.tile([P, S * PACK], BF16, name="z_woven%d" % g, align_bytes=64) for g in range(GROUPS)]
-        y_sc = [keep.tile([P, CHUNK], U8, name="y_sc%d" % g, align_bytes=64) for g in range(GROUPS)]
+        def tile(shape, dtype, name, tag=None, bufs=1):
+            return keep.tile(shape, dtype, name=name, tag=tag or name, bufs=bufs, align_bytes=64)
 
         def bank(b, name):
             return psum.tile([P, S], F32, name=name, tag="bank%d" % b)
 
+        offsets = keep.tile([P, S // 16], U16, name="offsets")
+        gains = [tile([P, PACK], F32, "gains%d" % g) for g in range(GROUPS)]
+        gain_of = [gains[u // PACK][:, u % PACK : u % PACK + 1] for u in range(PAGES)]
+        ident = tile([P, P], F32, "ident")
+        pages = [tile([P, T], F32, "page%d" % u) for u in range(PAGES)]
+        picked = [tile([P, S], F32, "picked%d" % u) for u in range(PAGES)]
+        tab_sc = tile([P, GROUPS, T], U8, "tab_sc", tag="quarter0")
+        w1_sc = tile([P, GROUPS, N], U8, "w1_sc")
+        w4_sc = tile([P, GROUPS, N], U8, "w4_sc")
+
         nc.vector.memset(tab_sc[:].rearrange("p a n -> p (a n)").bitcast(I32), 0)
         nc.gpsimd.memset(w1_sc[:].rearrange("p a n -> p (a n)").bitcast(I32), 0)
-        nc.gpsimd.memset(w4_sc_raw[:].bitcast(I32), 0)
+        nc.gpsimd.memset(w4_sc[:].rearrange("p a n -> p (a n)").bitcast(I32), 0)
         make_identity(nc, ident[:])
 
-        g_rows = gT.rearrange("(g p t) c -> g t p c", g=GROUPS, t=PACK)
-        out_rows = out_0.rearrange("(g p t) c -> g t p c", g=GROUPS, t=PACK)
+        dealt_in = gT[S : 2 * S, :].rearrange("(p t) c -> t p c", t=PACK)
+        dealt_out = out_0[S : 2 * S, :].rearrange("(p t) c -> t p c", t=PACK)
+        page_in = [gT[P * u : P * (u + 1), :] for u in range(PACK)] + [dealt_in[t] for t in range(PACK)]
+        page_out = [out_0[P * u : P * (u + 1), :] for u in range(PACK)] + [dealt_out[t] for t in range(PACK)]
+        w4_cols = w4_words.rearrange("a p n t -> p a (n t)").bitcast(I32)
 
         def load_scales(dst, src):
-            for q in range(4):
+            for r in range(4):
                 nc.sync.dma_start(
-                    out=dst[32 * q : 32 * q + 4, :, :].bitcast(I32),
-                    in_=src[:, 4 * q : 4 * q + 4, :].bitcast(I32).rearrange("a r n -> r a n"),
+                    out=dst[r:P:32, :, :].bitcast(I32),
+                    in_=src[:, r:16:4, :].bitcast(I32).rearrange("a q n -> q a n"),
                 )
 
         def load_table(a):
-            words = work.tile([P, T], I32, name="tab%d" % a, align_bytes=64)
+            words = tile([P, T], I32, "tab%d" % a, tag="half%d" % a)
             nc.sync.dma_start(out=words[:], in_=tab_words[a].rearrange("p n t -> p (n t)").bitcast(I32))
             return words
 
-        w3_raw = [keep.tile([P, PACK, CHUNK], F32, name="w3_raw%d" % a, align_bytes=64) for a in range(GROUPS)]
-        pair_tiles = [keep.tile([P, PACK, CHUNK], F32, name="pairs%d" % a, align_bytes=64) for a in range(2)]
-
-        def load_w3(g, a):
+        def load_w3(raw, a, first, count):
             nc.sync.dma_start(
-                out=w3_raw[a][:],
-                in_=w3[512 * a : 512 * (a + 1), CHUNK * g : CHUNK * (g + 1)].rearrange("(p j) c -> p j c", j=PACK),
+                out=raw, in_=w3[S * a : S * (a + 1), first : first + count].rearrange("(p j) c -> p j c", j=PACK)
             )
 
-        def load_w4(g):
-            raw = work.tile([P, GROUPS, CHUNK], I32, name="w4raw%d" % g, align_bytes=64)
-            nc.sync.dma_start(
-                out=raw[:],
-                in_=w4_words.rearrange("a p n t -> p a (n t)").bitcast(I32)[:, :, CHUNK * g : CHUNK * (g + 1)],
-            )
+        def load_w4(first, count, name):
+            raw = tile([P, GROUPS, count], I32, name)
+            nc.sync.dma_start(out=raw[:], in_=w4_cols[:, :, first : first + count])
             return raw
 
         nc.sync.dma_start(offsets[:], offs)
         tab = [load_table(0)]
         load_scales(tab_sc, tab_scales)
-        w1_q = keep.tile([P, GROUPS, 2 * N], U8, name="w1_q", align_bytes=64)
+        tab.append(load_table(1))
+        w1_q = tile([P, GROUPS, 2 * N], U8, "w1_q", tag="quarter1")
         nc.sync.dma_start(out=w1_q[:].bitcast(I32), in_=w1_words.bitcast(I32).rearrange("a p c -> p a c"))
         load_scales(w1_sc, w1_scales)
-        tab.append(load_table(1))
-        w4_raw = [load_w4(0)]
-        for q in range(4):
-            nc.sync.dma_start(
-                out=w4_sc_raw[32 * q + 4 : 32 * q + 12, :].bitcast(I32),
-                in_=w4_scales[:, 4 * q : 4 * q + 4, :].bitcast(I32),
-            )
         for u in range(PAGES):
-            nc.sync.dma_start(out=pages[u][:], in_=g_rows[u // PACK, u % PACK])
+            nc.sync.dma_start(out=pages[u][:], in_=page_in[u])
             if u == 0:
-                nc.sync.dma_start(out=gains[:], in_=gain.rearrange("(g p t) -> p g t", g=GROUPS, t=PACK))
-        load_w3(0, 0)
-        load_w3(0, 1)
-        w4_raw.append(load_w4(1))
+                with nc.allow_non_contiguous_dma(reason="one gain to a partition and page"):
+                    nc.sync.dma_start(out=gains[0][:], in_=gain[0:S].rearrange("(u p) -> p u", u=PACK))
+                nc.sync.dma_start(out=gains[1][:], in_=gain[S : 2 * S].rearrange("(p t) -> p t", t=PACK))
+            if u == 4:
+                load_scales(w4_sc, w4_scales)
 
-        nc.vector.tensor_copy(v_q[0][:].bitcast(U32), tab[0][:].bitcast(U32).indirect(offsets[:]))
-        for a in range(GROUPS):
-            nc.vector.tensor_copy(v_sc[a][:], tab_sc[:, a, :].indirect(offsets[:]))
-        nc.vector.tensor_copy(v_q[1][:].bitcast(U32), tab[1][:].bitcast(U32).indirect(offsets[:]))
+        v_q = [tile([P, S], I32, "v_q%d" % a) for a in range(GROUPS)]
+        v_sc = [tile([P, S], U8, "v_sc%d" % a) for a in range(GROUPS)]
+        halves = [slice(HALF * h, HALF * (h + 1)) for h in range(2)]
+        half_offsets = [offsets[:, 16 * h : 16 * (h + 1)] for h in range(2)]
 
-        gd = []
-        for g in range(GROUPS):
-            turned = []
-            for jb in range(S // P):
-                cols = slice(P * jb, P * (jb + 1))
-                acc = bank(PACK * g + jb, "draft%d%d" % (g, jb))
-                for a in range(GROUPS):
+        def gather_words(a, h):
+            nc.vector.tensor_copy(v_q[a][:, halves[h]].bitcast(U32), tab[a][:].bitcast(U32).indirect(half_offsets[h]))
+
+        def gather_scales(a, h):
+            nc.vector.tensor_copy(v_sc[a][:, halves[h]], tab_sc[:, a, :].indirect(half_offsets[h]))
+
+        gather_words(0, 0)
+        gather_scales(0, 0)
+        gather_scales(1, 0)
+        gather_words(0, 1)
+        gather_words(1, 0)
+        gather_words(1, 1)
+        gather_scales(0, 1)
+        gather_scales(1, 1)
+
+        def small(name, slot):
+            return tile([P, S], F32, name, tag="small%d" % slot)
+
+        drafts = [bank(b, "draft%d" % b) for b in range(PAGES)]
+        for b in (4, 5, 0, 6, 7, 1, 2, 3):
+            for a in range(GROUPS):
+                cols = slice(P * (b % PACK), P * (b % PACK + 1))
+                if b < PACK:
                     nc.tensor.matmul_mx(
-                        out=acc[:],
-                        lhsT=v_q[a][:, cols].bitcast(FP8X4),
-                        lhsT_scale=v_sc[a][:, cols],
-                        rhs=w1_q[:, a, 1024 * g : 1024 * (g + 1)].bitcast(FP4X4),
-                        rhs_scale=w1_sc[:, a, 512 * g : 512 * (g + 1)],
+                        out=drafts[b][:],
+                        lhsT=w1_q[:, a, 2 * cols.start : 2 * cols.stop].bitcast(FP4X4),
+                        lhsT_scale=w1_sc[:, a, cols],
+                        rhs=v_q[a][:].bitcast(FP8X4),
+                        rhs_scale=v_sc[a][:],
                         start=(a == 0),
                         stop=(a == GROUPS - 1),
                     )
-                draft_t = work.tile([P, PACK, P], F32, name="draft_t%d%d" % (g, jb), tag="tmp", bufs=10)
-                nc.scalar.activation(draft_t[:], acc[:].rearrange("p (m t) -> p t m", t=PACK), ACT.Tanh)
-                turned.append(draft_t)
-            for t in range(PACK):
-                draft = bank(PACK * (1 - g) + t, "draft_page%d%d" % (g, t))
-                for jb in range(S // P):
-                    nc.tensor.transpose(draft[:, P * jb : P * (jb + 1)], turned[jb][:, t, :], ident[:])
-                if g == 1 and t >= 2:
-                    scaled = last_two[:, S * (t - 2) : S * (t - 1)]
                 else:
-                    scaled = keep.tile([P, S], F32, name="gd%d%d" % (g, t), align_bytes=64)[:]
-                nc.scalar.activation(scaled, draft[:], ACT.Copy, scale=gains[:, g, t : t + 1])
-                gd.append(scaled)
-        for u in range(2, PAGES):
-            picked.append(z_woven[0][:].bitcast(F32)[:, 0:S] if u == 7 else gd[u - 2])
+                    nc.tensor.matmul_mx(
+                        out=drafts[b][:],
+                        lhsT=v_q[a][:, cols].bitcast(FP8X4),
+                        lhsT_scale=v_sc[a][:, cols],
+                        rhs=w1_q[:, a, N : 2 * N].bitcast(FP4X4),
+                        rhs_scale=w1_sc[:, a, S : 2 * S],
+                        start=(a == 0),
+                        stop=(a == GROUPS - 1),
+                    )
+        gained = {}
+        turned = {}
 
-        def quantise_z(g):
-            rows = work.tile([P, PACK, S], BF16, name="z_rows%d" % g, tag="bf", bufs=4, align_bytes=64)
-            for t in range(PACK):
-                u = PACK * g + t
-                nc.vector.tensor_copy(picked[u], pages[u][:].indirect(offsets[:]))
-                nc.vector.scalar_tensor_tensor(
-                    rows[:, t, :], picked[u], gains[:, g, t : t + 1], gd[u], ALU.mult, ALU.subtract
-                )
-            dst = z_woven[g][:].rearrange("p (c i t) -> p c t i", i=4, t=PACK)
-            src = rows[:].rearrange("p t (c i) -> p c t i", i=4)
-            if g == 0:
-                nc.scalar.copy(dst, src)
+        def tanh_natural(u):
+            draft = small("draft%d" % u, u)
+            nc.scalar.activation(draft[:], drafts[u][:], ACT.Tanh)
+            gained[u] = small("gained%d" % u, PACK + u)
+            nc.scalar.activation(gained[u][:], draft[:], ACT.Copy, scale=gain_of[u])
+
+        def tanh_turned(jb):
+            turned[jb] = small("turned%d" % jb, 2 * PACK + jb)
+            nc.scalar.activation(
+                turned[jb][:].rearrange("p (t m) -> p t m", t=PACK),
+                drafts[PACK + jb][:].rearrange("p (m t) -> p t m", t=PACK),
+                ACT.Tanh,
+            )
+
+        tanh_turned(0)
+        tanh_turned(1)
+        tanh_natural(0)
+        tanh_turned(2)
+        tanh_turned(3)
+        for u in range(1, PACK):
+            tanh_natural(u)
+        for t in range(PACK):
+            back = bank(PACK + t, "back%d" % t)
+            for jb in range(PACK):
+                nc.tensor.transpose(back[:, P * jb : P * (jb + 1)], turned[jb][:, P * t : P * (t + 1)], ident[:])
+            if t == 1:
+                gained[PACK + t] = tile([P, S], F32, "gained5", tag="z_q0")
             else:
-                nc.scalar.copy(dst[:, :, 0:2, :], src[:, :, 0:2, :])
-                nc.vector.tensor_copy(dst[:, :, 2:4, :], src[:, :, 2:4, :])
-            nc.vector.quantize_mx(out=z_q[g][:].bitcast(FP8X4), scales=z_sc[g][:], in_=z_woven[g][:])
+                gained[PACK + t] = small("gained%d" % (PACK + t), t)
+            nc.scalar.activation(gained[PACK + t][:], back[:], ACT.Copy, scale=gain_of[PACK + t])
 
-        def weave_w3(g, a, h, woven, on_vector=False):
-            dst = woven.rearrange("p (t m j) -> p m j t", t=2, j=PACK)
-            src = w3_raw[a][:].rearrange("p j (m t) -> p m j t", t=PACK)[:, :, :, 2 * h : 2 * h + 2]
-            if on_vector:
-                nc.vector.tensor_copy(dst, src)
-            else:
-                nc.scalar.copy(dst, src)
-            nc.vector.quantize_mx(out=w3_q[g, a, h].bitcast(FP8X4), scales=w3_sc[g, a, h], in_=woven)
+        def gather(u):
+            nc.vector.tensor_copy(picked[u][:], pages[u][:].indirect(offsets[:]))
 
-        def weave_w3_whole(a, woven):
+        z_sc = [tile([P, S], U8, "z_sc%d" % a) for a in range(GROUPS)]
+
+        z_turned = tile([P, PACK, 2, P, 2], BF16, "z_turned", tag="quarter2")
+        for u in range(PACK):
+            gather(u)
+            nc.vector.scalar_tensor_tensor(gained[u][:], picked[u][:], gain_of[u], gained[u][:], ALU.mult, ALU.subtract)
+            acc = bank(u, "z_turn%d" % u)
+            for jb in range(PACK):
+                cols = slice(P * jb, P * (jb + 1))
+                nc.tensor.transpose(acc[:, cols], gained[u][:, cols], ident[:])
             nc.scalar.copy(
-                woven.rearrange("p (t m j) -> p m j t", t=PACK, j=PACK),
-                w3_raw[a][:].rearrange("p j (m t) -> p m j t", t=PACK),
+                z_turned[:, :, :, 32 * u : 32 * (u + 1), :], acc[:].rearrange("p (b q h e) -> p b h q e", b=PACK, h=2, e=2)
             )
-            nc.vector.quantize_mx(out=w3_q1[a][:].bitcast(FP8X4), scales=w3_sc1[a][:], in_=woven)
+        z_woven = [tile([P, S * PACK], BF16, "z_woven0", tag="quarter3"), tile([P, S * PACK], BF16, "z_woven1", tag="quarter5")]
+        z_words = z_turned[:].rearrange("p b h m e -> p b h (m e)").bitcast(F32)
+        for half in range(2):
+            words = bank(half, "z_words%d" % half)
+            for b in range(2):
+                for h in range(2):
+                    nc.tensor.transpose(words[:, P * (2 * b + h) : P * (2 * b + h + 1)], z_words[:, 2 * half + b, h, :], ident[:])
+            nc.scalar.copy(
+                z_woven[0][:].bitcast(F32)[:, S * half : S * (half + 1)].rearrange("p (b j e) -> p b j e", b=2, e=2),
+                words[:].rearrange("p (b e j) -> p b j e", b=2, e=2),
+            )
+        z_q = {}
+        z_rows = tile([P, PACK, S], BF16, "z_rows", tag="quarter4")
+        weave_dst = z_woven[1][:].rearrange("p (c i t) -> p c t i", i=4, t=PACK)
+        weave_src = z_rows[:].rearrange("p t (c i) -> p c t i", i=4)
+        for t in range(PACK - 1):
+            u = PACK + t
+            gather(u)
+            nc.vector.scalar_tensor_tensor(
+                z_rows[:, t, :], picked[u][:], gain_of[u], gained[u][:], ALU.mult, ALU.subtract
+            )
+            if t == 1:
+                z_q[0] = tile([P, S], I32, "z_q0")
+                nc.vector.quantize_mx(out=z_q[0][:].bitcast(FP8X4), scales=z_sc[0][:], in_=z_woven[0][:])
+                nc.scalar.copy(weave_dst[:, :, 0:2, :], weave_src[:, :, 0:2, :])
+        last = PAGES - 1
+        for h in range(2):
+            nc.vector.tensor_copy(picked[last][:, halves[h]], pages[last][:].indirect(half_offsets[h]))
+        for cols in halves:
+            nc.vector.scalar_tensor_tensor(
+                z_rows[:, PACK - 1, cols], picked[last][:, cols], gain_of[last], gained[last][:, cols], ALU.mult, ALU.subtract
+            )
 
-        def deal_w4(g):
+        w3_raw = {}
+        w3_q = {}
+        w3_sc = {}
+        w4_q = {}
+
+        def load_w3_page(u):
+            w3_raw[u] = tile([P, GROUPS, PACK, P], F32, "w3_raw%d" % u, tag="quarter%d" % u if u < 3 else "w3_raw3")
             for a in range(GROUPS):
-                nc.vector.tensor_copy(
-                    out=w4_q[a][:].rearrange("p (t m) -> p m t", t=PACK),
-                    in_=w4_raw[g][:, a, :].rearrange("p (m t) -> p m t", t=PACK),
+                load_w3(w3_raw[u][:, a], a, P * u, P)
+
+        load_w3_page(0)
+        w4_first = load_w4(0, 2 * P, "w4_first")
+        load_w3_page(1)
+        load_w3_page(2)
+        w4_second = load_w4(2 * P, 2 * P, "w4_second")
+        load_w3_page(3)
+        w4_raw = load_w4(S, S, "w4_raw")
+        w3_late = [tile([P, PACK, S], F32, "w3_late%d" % a, tag="half%d" % a) for a in range(GROUPS)]
+        for a in range(GROUPS):
+            load_w3(w3_late[a][:], a, S, S)
+        for u in range(PACK):
+            for a in range(GROUPS):
+                cols = slice(P * (u % 2), P * (u % 2 + 1))
+                w4_q[u, a] = ((w4_first, w4_second)[u // 2][:, a, cols], w4_sc[:, a, P * u : P * (u + 1)])
+
+        w3_woven = {}
+
+        def weave_w3_page(u):
+            w3_woven[u] = tile([P, GROUPS, P * PACK], BF16, "w3_woven%d" % u, tag="w3_woven%d" % u)
+            for a in range(GROUPS):
+                nc.scalar.copy(
+                    w3_woven[u][:, a, :].rearrange("p (c i j) -> p c j i", i=4, j=PACK),
+                    w3_raw[u][:, a].rearrange("p j (c i) -> p c j i", i=4),
                 )
 
-        def y3_pass(acc, u, a):
-            g, t = divmod(u, PACK)
-            cols = slice(P * (t % 2), P * (t % 2 + 1))
-            nc.tensor.matmul_mx(
-                out=acc[:],
-                lhsT=w3_q[g, a, t // 2][:, cols].bitcast(FP8X4),
-                lhsT_scale=w3_sc[g, a, t // 2][:, cols],
-                rhs=z_q[a][:].bitcast(FP8X4),
-                rhs_scale=z_sc[a][:],
-                start=(a == 0),
-                stop=(a == GROUPS - 1),
+        def quantise_w3_page(u):
+            codes = tile([P, GROUPS * P], I32, "w3_codes%d" % u)
+            scales = tile([P, GROUPS * P], U8, "w3_scales%d" % u)
+            nc.vector.quantize_mx(
+                out=codes[:].bitcast(FP8X4), scales=scales[:], in_=w3_woven[u][:].rearrange("p a c -> p (a c)")
+            )
+            for a in range(GROUPS):
+                w3_q[u, a] = (codes[:, P * a : P * (a + 1)], scales[:, P * a : P * (a + 1)])
+
+        def weave_w3_late(a):
+            w3_woven[PACK + a] = tile([P, S * PACK], BF16, "w3_late_woven%d" % a, tag="quarter%d" % (4 + a))
+            nc.scalar.copy(
+                w3_woven[PACK + a][:].rearrange("p (t m j) -> p m j t", t=PACK, j=PACK),
+                w3_late[a][:].rearrange("p j (m t) -> p m j t", t=PACK),
             )
 
-        def y4_pass(acc, u, a):
-            g, t = divmod(u, PACK)
-            nc.tensor.matmul_mx(
-                out=acc[:],
-                lhsT=w4_q[a][:, P * t : P * (t + 1)].bitcast(FP8X4),
-                lhsT_scale=w4_sc[4 + 4 * a : P, P * u : P * (u + 1)],
-                rhs=z_q[a][:].bitcast(FP8X4),
-                rhs_scale=z_sc[a][:],
-                start=(a == 0),
-                stop=(a == GROUPS - 1),
-            )
+        def quantise_w3_late(a):
+            codes = tile([P, S], I32, "w3_late_codes%d" % a)
+            scales = tile([P, S], U8, "w3_late_scales%d" % a)
+            nc.vector.quantize_mx(out=codes[:].bitcast(FP8X4), scales=scales[:], in_=w3_woven[PACK + a][:])
+            for t in range(PACK):
+                w3_q[PACK + t, a] = (codes[:, P * t : P * (t + 1)], scales[:, P * t : P * (t + 1)])
 
-        deal_w4(0)
-        nc.vector.tensor_copy(
-            out=w4_sc[:].rearrange("p (g t m) -> p g m t", g=GROUPS, t=PACK),
-            in_=w4_sc_raw[:].rearrange("p (g m t) -> p g m t", g=GROUPS, t=PACK),
-        )
-        quantise_z(0)
-        quantise_z(1)
-        weave_w3(0, 0, 0, gd[6].bitcast(BF16))
-        weave_w3(0, 1, 0, z_woven[1][:, 0:1024], on_vector=True)
+        def deal_w4():
+            codes = tile([P, GROUPS, S], I32, "w4_dealt")
+            scales = tile([P, GROUPS, S], U8, "w4_dealt_sc")
+            nc.vector.tensor_copy(
+                out=codes[:].rearrange("p a (t m) -> p a m t", t=PACK),
+                in_=w4_raw[:].rearrange("p a (m t) -> p a m t", t=PACK),
+            )
+            nc.vector.tensor_copy(
+                out=scales[:].rearrange("p a (t m) -> p a m t", t=PACK),
+                in_=w4_sc[:, :, S : 2 * S].rearrange("p a (m t) -> p a m t", t=PACK),
+            )
+            for t in range(PACK):
+                for a in range(GROUPS):
+                    w4_q[PACK + t, a] = (codes[:, a, P * t : P * (t + 1)], scales[:, a, P * t : P * (t + 1)])
 
         y3 = {}
         y4 = {}
@@ -249,34 +309,86 @@ def tile_list_tablet_sign_correction_kernel(
             y3[u] = bank(bank3, "y3_%d" % u)
             y4[u] = bank(bank4, "y4_%d" % u)
             for a in range(GROUPS):
-                y3_pass(y3[u], u, a)
-            for a in range(GROUPS):
-                y4_pass(y4[u], u, a)
+                for acc, (codes, scales) in ((y3[u], w3_q[u, a]), (y4[u], w4_q[u, a])):
+                    nc.tensor.matmul_mx(
+                        out=acc[:],
+                        lhsT=codes.bitcast(FP8X4),
+                        lhsT_scale=scales,
+                        rhs=z_q[a][:].bitcast(FP8X4),
+                        rhs_scale=z_sc[a][:],
+                        start=(a == 0),
+                        stop=(a == GROUPS - 1),
+                    )
 
-        mag = {}
+        size = {}
         base = {}
 
         def take_abs(u):
-            mag[u] = work.tile([P, S], F32, name="mag%d" % u, tag="tmp", bufs=10)[:]
-            nc.scalar.activation(mag[u], y3[u][:], ACT.Abs)
+            if u in (2, 3):
+                size[u] = tile([P, S], F32, "size%d" % u, tag="half0" if u == 2 else "quarter4")
+            else:
+                size[u] = small("size%d" % u, u)
+            nc.scalar.activation(size[u][:], y3[u][:], ACT.Abs)
 
         def add_state(u):
-            if u in (2, 3):
-                base[u] = gd[u + 4]
+            if u < 2:
+                base[u] = tile([P, S], F32, "base%d" % u, tag="w3_woven%d" % (u + 2))
+            elif u == 2:
+                base[u] = tile([P, S], F32, "base%d" % u, tag="quarter5")
             else:
-                base[u] = work.tile([P, S], F32, name="base%d" % u, tag="tmp", bufs=10)[:]
-            nc.vector.tensor_tensor(base[u], y4[u][:], picked[u], ALU.add)
+                base[u] = small("base%d" % u, (3, 8, 9, 10, 0)[u - 3])
+            nc.vector.tensor_tensor(base[u][:], y4[u][:], picked[u][:], ALU.add)
 
         def scatter(u):
-            nc.vector.tensor_tensor(pages[u][:].indirect(offsets[:]), base[u], mag[u], ALU.add)
-            nc.sync.dma_start(out=out_rows[u // PACK, u % PACK], in_=pages[u][:])
+            nc.vector.tensor_tensor(pages[u][:].indirect(offsets[:]), base[u][:], size[u][:], ALU.add)
+            nc.sync.dma_start(out=page_out[u], in_=pages[u][:])
 
-        def stage(g, c):
-            return (w3_raw if g == 0 else pair_tiles)[c // 2]
+        y_sc = [tile([P, CHUNK], U8, "y_sc%d" % g) for g in range(GROUPS)]
+        codes_out = [out_1[g].rearrange("p m t -> p (m t)").bitcast(I32) for g in range(GROUPS)]
+        y_turned = {}
+        y_woven = {}
+
+        def turn_page(u, banks):
+            if u != 2:
+                whole = tile([P, PACK, 2, P, 2], BF16, "y_turned%d" % u, tag="half1" if u == 0 else "y_turned%d" % u)
+                y_turned[u] = [whole[:, 0:2], whole[:, 2:4]]
+            else:
+                y_turned[u] = [tile([P, 2, 2, P, 2], BF16, "y_turned2%d" % a, tag="half%d" % a)[:] for a in range(2)]
+            for k in range(PACK):
+                acc = bank(banks[k], "turn%d%d" % (u, k))
+                for q in range(CHUNKS):
+                    first = CHUNK * q + P * k
+                    nc.tensor.transpose(acc[:, P * q : P * (q + 1)], pages[u][:, first : first + P], ident[:])
+                nc.scalar.copy(y_turned[u][k // 2][:, k % 2], acc[:].rearrange("p (m h e) -> p h m e", h=2, e=2))
+
+        def turn_back(u, banks):
+            y_woven[u] = tile([P, CHUNK * PACK], BF16, "y_woven%d" % u, tag="y_woven", bufs=5)
+            for half in range(2):
+                words = y_turned[u][half].rearrange("p k h m e -> p k h (m e)").bitcast(F32)
+                acc = bank(banks[half], "back%d%d" % (u, half))
+                for b in range(2):
+                    for h in range(2):
+                        nc.tensor.transpose(
+                            acc[:, P * (2 * b + h) : P * (2 * b + h + 1)], words[:, b, h, :], ident[:]
+                        )
+                nc.scalar.copy(
+                    y_woven[u][:].bitcast(F32)[:, S * half : S * (half + 1)].rearrange("p (b c h) -> p b c h", b=2, h=2),
+                    acc[:].rearrange("p (b h c) -> p b c h", b=2, h=2),
+                )
+
+        def quantise_page(u):
+            codes = tile([P, CHUNK], I32, "y_codes%d" % u, tag="y_codes", bufs=6)
+            nc.vector.quantize_mx(out=codes[:].bitcast(FP8X4), scales=y_sc[0][4 * u : P, :], in_=y_woven[u][:])
+            for q in range(CHUNKS):
+                nc.sync.dma_start(
+                    out=codes_out[0][32 * u : 32 * (u + 1), CHUNK * q : CHUNK * (q + 1)], in_=codes[32 * q : 32 * (q + 1), :]
+                )
+
+        pairs = []
 
         def round_page(u, first, count, on_vector):
-            g, t = divmod(u, PACK)
-            raw = stage(g, first)[:].bitcast(BF16).rearrange("p (c u) (m e) -> p c u m e", u=2, e=2)
+            t = u - PACK
+            raw = pairs[first // 2][:].bitcast(BF16).rearrange("p (c h) (m e) -> p c h m e", h=2, e=2)
             dst = raw[:, first % 2 : first % 2 + count, t // 2, :, t % 2]
             src = pages[u][:, CHUNK * first : CHUNK * (first + count)].rearrange("p (c m) -> p c m", c=count)
             if on_vector:
@@ -284,95 +396,140 @@ def tile_list_tablet_sign_correction_kernel(
             else:
                 nc.scalar.copy(dst, src)
 
-        def rounded_rows(c):
-            return w3_raw[c // 2][:].bitcast(BF16)
+        joined = {}
 
-        def round_rows(u):
-            for first in (0, 2):
-                nc.scalar.copy(rounded_rows(first)[:, u, :], pages[u][:, CHUNK * first : CHUNK * (first + 2)])
-
-        def finish_chunk(g, c, on_vector):
-            woven = work.tile([P, CHUNK * PACK], BF16, name="y_woven%d%d" % (g, c), tag="bf", bufs=4, align_bytes=64)
-            if g == 0:
-                dst = woven[:].rearrange("p (c i t) -> p c t i", i=4, t=PACK)
-                src = rounded_rows(c)[:, :, CHUNK * (c % 2) : CHUNK * (c % 2 + 1)].rearrange("p t (c i) -> p c t i", i=4)
-            else:
-                dst = woven[:].bitcast(F32).rearrange("p (m u) -> p m u", u=2)
-                src = stage(g, c)[:, 2 * (c % 2) : 2 * (c % 2) + 2, :].rearrange("p u m -> p m u")
+        def join_chunk(c, on_vector):
+            joined[c] = tile([P, CHUNK * PACK], BF16, "y_joined%d" % c, tag="y_woven", bufs=5)
+            dst = joined[c][:].bitcast(F32).rearrange("p (m h) -> p m h", h=2)
+            src = pairs[c // 2][:, 2 * (c % 2) : 2 * (c % 2) + 2, :].rearrange("p h m -> p m h")
             if on_vector:
                 nc.vector.tensor_copy(dst, src)
             else:
                 nc.scalar.copy(dst, src)
-            codes = work.tile([P, CHUNK], I32, name="y_q%d%d" % (g, c), tag="y_q", bufs=6, align_bytes=64)
-            nc.vector.quantize_mx(out=codes[:].bitcast(FP8X4), scales=y_sc[g][4 * c : P, :], in_=woven[:])
-            nc.sync.dma_start(
-                out=out_1[g].rearrange("p m t -> p (m t)").bitcast(I32)[:, CHUNK * c : CHUNK * (c + 1)], in_=codes[:]
-            )
+
+        def quantise_chunk(c):
+            codes = tile([P, CHUNK], I32, "y_chunk%d" % c, tag="y_codes", bufs=6)
+            nc.vector.quantize_mx(out=codes[:].bitcast(FP8X4), scales=y_sc[1][4 * c : P, :], in_=joined[c][:])
+            nc.sync.dma_start(out=codes_out[1][:, CHUNK * c : CHUNK * (c + 1)], in_=codes[:])
 
         def store_scales(g):
             for q in range(4):
-                nc.sync.dma_start(
-                    out=out_2[g, 4 * q : 4 * q + 4, :].bitcast(I32).rearrange("r (c m) -> c r m", c=CHUNKS),
-                    in_=y_sc[g][32 * q : 32 * q + 16, :].bitcast(I32),
-                )
+                if g == 0:
+                    dst = out_2[0, :, CHUNK * q : CHUNK * (q + 1)].bitcast(I32)
+                else:
+                    dst = out_2[1, 4 * q : 4 * q + 4, :].bitcast(I32).rearrange("r (c m) -> c r m", c=CHUNKS)
+                nc.sync.dma_start(out=dst, in_=y_sc[g][32 * q : 32 * q + 16, :].bitcast(I32))
 
-        products(0, 1, 0)
-        take_abs(0)
-        add_state(0)
-        weave_w3(0, 0, 1, gd[7].bitcast(BF16))
-        load_w3(1, 0)
-        weave_w3(0, 1, 1, z_woven[1][:, 1024:2048])
-        load_w3(1, 1)
-        products(1, 0, 1)
+        weave_w3_page(0)
+        quantise_w3_page(0)
+        for h in range(2):
+            lines = slice(64 * h, 64 * (h + 1))
+            nc.vector.tensor_copy(weave_dst[:, lines, 2:4, :], weave_src[:, lines, 2:4, :])
+        z_q[1] = tile([P, S], I32, "z_q1", tag="w3_woven0")
+        for h in range(2):
+            nc.vector.quantize_mx(
+                out=z_q[1][:, halves[h]].bitcast(FP8X4),
+                scales=z_sc[1][:, halves[h]],
+                in_=z_woven[1][:, PACK * HALF * h : PACK * HALF * (h + 1)],
+            )
+        first3 = [bank(b, "first3_%d" % b) for b in (0, 4)]
+        first4 = [bank(b, "first4_%d" % b) for b in (2, 5)]
+
+        def half_pass(acc, weights, a, h):
+            codes, scales = weights[0, a]
+            nc.tensor.matmul_mx(
+                out=acc[h][:, 0:HALF],
+                lhsT=codes.bitcast(FP8X4),
+                lhsT_scale=scales,
+                rhs=z_q[a][:, halves[h]].bitcast(FP8X4),
+                rhs_scale=z_sc[a][:, halves[h]],
+                start=(a == 0),
+                stop=(a == GROUPS - 1),
+            )
+
+        for acc, weights in ((first4, w4_q), (first3, w3_q)):
+            for h in range(2):
+                half_pass(acc, weights, 0, h)
+        for h in range(2):
+            half_pass(first3, w3_q, 1, h)
+            half_pass(first4, w4_q, 1, h)
+        weave_w3_page(1)
+        quantise_w3_page(1)
+        size[0] = tile([P, S], F32, "size0", tag="quarter1")
+        base[0] = tile([P, S], F32, "base0", tag="w3_woven1")
+        for h in range(2):
+            nc.scalar.activation(size[0][:, halves[h]], first3[h][:, 0:HALF], ACT.Abs)
+        products(1, 1, 3)
+        for h in range(2):
+            nc.vector.tensor_tensor(base[0][:, halves[h]], first4[h][:, 0:HALF], picked[0][:, halves[h]], ALU.add)
+            nc.vector.tensor_tensor(
+                pages[0][:].indirect(half_offsets[h]), base[0][:, halves[h]], size[0][:, halves[h]], ALU.add
+            )
+        nc.sync.dma_start(out=page_out[0], in_=pages[0][:])
         take_abs(1)
-        scatter(0)
+        weave_w3_page(2)
+        weave_w3_page(3)
+        quantise_w3_page(2)
+        quantise_w3_page(3)
+        products(2, 0, 2)
         add_state(1)
-        products(2, 0, 1)
+        products(3, 1, 3)
         scatter(1)
+        weave_w3_late(0)
         take_abs(2)
-        weave_w3_whole(0, z_woven[1][:])
-        weave_w3_whole(1, last_two[:].bitcast(BF16))
+        weave_w3_late(1)
+        deal_w4()
+        quantise_w3_late(0)
+        quantise_w3_late(1)
         add_state(2)
-        products(3, 0, 1)
-        take_abs(3)
-        deal_w4(1)
-        add_state(3)
-        for u in range(PACK, PAGES - 1):
-            products(u, 2 * (u - PACK) + 2, 2 * (u - PACK) + 3)
-        products(PAGES - 1, 0, 1)
         scatter(2)
-        add_state(4)
+        turn_page(0, (4, 5, 6, 7))
+        take_abs(3)
+        add_state(3)
         scatter(3)
-
-        def round_whole(u):
-            for first in (0, 2):
-                round_page(u, first, 2, False)
-
-        round_rows(0)
-        round_rows(1)
+        turn_page(1, (4, 5, 6, 7))
+        products(4, 1, 0)
         take_abs(4)
-        add_state(5)
+        add_state(4)
         scatter(4)
-        round_rows(2)
+        turn_back(0, (2, 4))
+        products(5, 7, 1)
         take_abs(5)
-        add_state(6)
+        add_state(5)
         scatter(5)
-        round_rows(3)
+        turn_back(1, (5, 3))
+        products(6, 6, 7)
+        turn_page(2, (2, 4, 5, 3))
         take_abs(6)
-        add_state(7)
+        add_state(6)
         scatter(6)
+        turn_back(2, (2, 4))
+        pairs.extend(tile([P, PACK, CHUNK], F32, "pairs%d" % a, tag="half%d" % a) for a in range(2))
+        round_page(4, 0, 2, False)
+        round_page(4, 2, 2, False)
+        products(7, 6, 5)
         take_abs(7)
+        add_state(7)
         scatter(7)
-        for c in range(CHUNKS):
-            finish_chunk(0, c, False)
+        turn_page(3, (3, 2, 4, 6))
+        round_page(5, 0, 2, False)
+        turn_back(3, (3, 0))
+        round_page(5, 2, 2, False)
+        for u in range(PACK):
+            quantise_page(u)
         store_scales(0)
-        for u in (4, 5):
-            round_page(u, 0, 2, False)
-            round_page(u, 2, 1, False)
-            round_page(u, 3, 1, True)
-        for u in (6, 7):
-            round_page(u, 0, 2, False)
-            round_page(u, 2, 2, True)
-        for c in (3, 2, 0, 1):
-            finish_chunk(1, c, c != 1)
+        round_page(6, 0, 2, False)
+        round_page(6, 2, 1, False)
+        round_page(6, 3, 1, True)
+        round_page(7, 3, 1, True)
+        for c in range(3):
+            round_page(7, c, 1, False)
+        join_chunk(3, True)
+        join_chunk(0, True)
+        quantise_chunk(3)
+        quantise_chunk(0)
+        join_chunk(1, True)
+        quantise_chunk(1)
+        join_chunk(2, False)
+        quantise_chunk(2)
         store_scales(1)

@@ -276,31 +276,48 @@ def tile_list_tablet_sign_correction_kernel(
         def weave_w3_late(a):
             w3_woven[PACK + a] = tile([P, S * PACK], BF16, "w3_late_woven%d" % a, tag="quarter%d" % (4 + a))
             nc.scalar.copy(
-                w3_woven[PACK + a][:].rearrange("p (t m j) -> p m j t", t=PACK, j=PACK),
-                w3_late[a][:].rearrange("p j (m t) -> p m j t", t=PACK),
+                w3_woven[PACK + a][:].rearrange("p (c i j) -> p c j i", i=4, j=PACK),
+                w3_late[a][:].rearrange("p j (c i) -> p c j i", i=4),
             )
 
         def quantise_w3_late(a):
             codes = tile([P, S], I32, "w3_late_codes%d" % a)
             scales = tile([P, S], U8, "w3_late_scales%d" % a)
             nc.vector.quantize_mx(out=codes[:].bitcast(FP8X4), scales=scales[:], in_=w3_woven[PACK + a][:])
-            for t in range(PACK):
-                w3_q[PACK + t, a] = (codes[:, P * t : P * (t + 1)], scales[:, P * t : P * (t + 1)])
+            w3_late_q[a] = (codes[:], scales[:])
 
-        def deal_w4():
-            codes = tile([P, GROUPS, S], I32, "w4_dealt")
-            scales = tile([P, GROUPS, S], U8, "w4_dealt_sc")
-            nc.vector.tensor_copy(
-                out=codes[:].rearrange("p a (t m) -> p a m t", t=PACK),
-                in_=w4_raw[:].rearrange("p a (m t) -> p a m t", t=PACK),
-            )
-            nc.vector.tensor_copy(
-                out=scales[:].rearrange("p a (t m) -> p a m t", t=PACK),
-                in_=w4_sc[:, :, S : 2 * S].rearrange("p a (m t) -> p a m t", t=PACK),
-            )
-            for t in range(PACK):
-                for a in range(GROUPS):
-                    w4_q[PACK + t, a] = (codes[:, a, P * t : P * (t + 1)], scales[:, a, P * t : P * (t + 1)])
+        w3_late_q = {}
+        w4_late_q = {a: (w4_raw[:, a, :], w4_sc[:, a, S : 2 * S]) for a in range(GROUPS)}
+
+        def turned_products(weights, banks, func, tag):
+            out = tile([P, PACK, PACK, P], F32, "turned_" + tag, tag=tag)
+            accs = [bank(b, "turned_%s%d" % (tag, b)) for b in banks]
+            for a in range(GROUPS):
+                codes, scales = weights[a]
+                for jb in range(PACK):
+                    cols = slice(P * jb, P * (jb + 1))
+                    nc.tensor.matmul_mx(
+                        out=accs[jb][:],
+                        lhsT=z_q[a][:, cols].bitcast(FP8X4),
+                        lhsT_scale=z_sc[a][:, cols],
+                        rhs=codes.bitcast(FP8X4),
+                        rhs_scale=scales,
+                        start=(a == 0),
+                        stop=(a == GROUPS - 1),
+                    )
+            for jb in range(PACK):
+                nc.scalar.activation(out[:, jb], accs[jb][:].rearrange("p (m t) -> p t m", t=PACK), func)
+            return out
+
+        def sum_turned(u, b, sizes, rests):
+            acc = bank(b, "sum%d" % u)
+            for jb in range(PACK):
+                cols = slice(P * jb, P * (jb + 1))
+                nc.tensor.matmul(acc[:, cols], rests[:, jb, u - PACK], ident[:], start=True, stop=False, is_transpose=True)
+                nc.tensor.matmul(acc[:, cols], sizes[:, jb, u - PACK], ident[:], start=False, stop=True, is_transpose=True)
+            size[u] = small("sum%d" % u, u + 1)
+            base[u] = picked[u]
+            nc.scalar.copy(size[u][:], acc[:])
 
         y3 = {}
         y4 = {}
@@ -324,10 +341,10 @@ def tile_list_tablet_sign_correction_kernel(
         base = {}
 
         def take_abs(u):
-            if u in (2, 3):
-                size[u] = tile([P, S], F32, "size%d" % u, tag="half0" if u == 2 else "quarter4")
+            if u == 2:
+                size[u] = tile([P, S], F32, "size2", tag="quarter4")
             else:
-                size[u] = small("size%d" % u, u)
+                size[u] = small("size%d" % u, u + 1)
             nc.scalar.activation(size[u][:], y3[u][:], ACT.Abs)
 
         def add_state(u):
@@ -336,7 +353,7 @@ def tile_list_tablet_sign_correction_kernel(
             elif u == 2:
                 base[u] = tile([P, S], F32, "base%d" % u, tag="quarter5")
             else:
-                base[u] = small("base%d" % u, (3, 8, 9, 10, 0)[u - 3])
+                base[u] = small("base%d" % u, u)
             nc.vector.tensor_tensor(base[u][:], y4[u][:], picked[u][:], ALU.add)
 
         def scatter(u):
@@ -350,7 +367,7 @@ def tile_list_tablet_sign_correction_kernel(
 
         def turn_page(u, banks):
             if u != 2:
-                whole = tile([P, PACK, 2, P, 2], BF16, "y_turned%d" % u, tag="half1" if u == 0 else "y_turned%d" % u)
+                whole = tile([P, PACK, 2, P, 2], BF16, "y_turned%d" % u, tag="y_turned%d" % (u % 2))
                 y_turned[u] = [whole[:, 0:2], whole[:, 2:4]]
             else:
                 y_turned[u] = [tile([P, 2, 2, P, 2], BF16, "y_turned2%d" % a, tag="half%d" % a)[:] for a in range(2)]
@@ -473,63 +490,49 @@ def tile_list_tablet_sign_correction_kernel(
         quantise_w3_page(3)
         products(2, 0, 2)
         add_state(1)
-        products(3, 1, 3)
         scatter(1)
         weave_w3_late(0)
-        take_abs(2)
         weave_w3_late(1)
-        deal_w4()
         quantise_w3_late(0)
+        take_abs(2)
+        products(3, 0, 3)
         quantise_w3_late(1)
         add_state(2)
         scatter(2)
-        turn_page(0, (4, 5, 6, 7))
         take_abs(3)
         add_state(3)
         scatter(3)
-        turn_page(1, (4, 5, 6, 7))
-        products(4, 1, 0)
-        take_abs(4)
-        add_state(4)
-        scatter(4)
-        turn_back(0, (2, 4))
-        products(5, 7, 1)
-        take_abs(5)
-        add_state(5)
-        scatter(5)
-        turn_back(1, (5, 3))
-        products(6, 6, 7)
-        turn_page(2, (2, 4, 5, 3))
-        take_abs(6)
-        add_state(6)
-        scatter(6)
-        turn_back(2, (2, 4))
+        rests = turned_products(w4_late_q, (4, 5, 6, 7), ACT.Copy, "half1")
+        sizes = turned_products(w3_late_q, (1, 2, 4, 5), ACT.Abs, "half0")
+        for u, b in ((4, 0), (5, 6), (6, 7), (7, 3)):
+            sum_turned(u, b, sizes, rests)
+            scatter(u)
+        turn_page(0, (1, 2, 4, 5))
+        turn_page(1, (0, 6, 7, 3))
+        turn_back(0, (1, 2))
+        turn_back(1, (4, 5))
+        turn_page(2, (0, 6, 7, 3))
+        turn_page(3, (1, 2, 4, 5))
+        turn_back(2, (0, 6))
+        turn_back(3, (7, 3))
+        for u in range(2):
+            quantise_page(u)
         pairs.extend(tile([P, PACK, CHUNK], F32, "pairs%d" % a, tag="half%d" % a) for a in range(2))
-        round_page(4, 0, 2, False)
-        round_page(4, 2, 2, False)
-        products(7, 6, 5)
-        take_abs(7)
-        add_state(7)
-        scatter(7)
-        turn_page(3, (3, 2, 4, 6))
-        round_page(5, 0, 2, False)
-        turn_back(3, (3, 0))
-        round_page(5, 2, 2, False)
-        for u in range(PACK):
+        for u in (4, 5):
+            round_page(u, 0, 2, True)
+            round_page(u, 2, 2, True)
+        for u in range(2, PACK):
             quantise_page(u)
         store_scales(0)
-        round_page(6, 0, 2, False)
-        round_page(6, 2, 1, False)
-        round_page(6, 3, 1, True)
-        round_page(7, 3, 1, True)
-        for c in range(3):
-            round_page(7, c, 1, False)
+        for u in (6, 7):
+            round_page(u, 2, 2, False)
+            round_page(u, 0, 2, False)
         join_chunk(3, True)
-        join_chunk(0, True)
+        join_chunk(2, True)
         quantise_chunk(3)
-        quantise_chunk(0)
-        join_chunk(1, True)
-        quantise_chunk(1)
-        join_chunk(2, False)
         quantise_chunk(2)
+        join_chunk(0, False)
+        quantise_chunk(0)
+        join_chunk(1, False)
+        quantise_chunk(1)
         store_scales(1)

@@ -235,16 +235,20 @@ def tile_list_tablet_sign_correction_kernel(
         w4_q = {}
 
         def load_w3_page(u):
-            w3_raw[u] = tile([P, GROUPS, PACK, P], F32, "w3_raw%d" % u, tag="quarter%d" % u if u < 3 else "w3_raw3")
+            raw = tile([P, GROUPS, PACK, P], F32, "w3_raw%d" % u, tag="quarter%d" % u)
             for a in range(GROUPS):
-                load_w3(w3_raw[u][:, a], a, P * u, P)
+                w3_raw[u, a] = raw[:, a]
+                load_w3(w3_raw[u, a], a, P * u, P)
 
         load_w3_page(0)
         w4_first = load_w4(0, 2 * P, "w4_first")
         load_w3_page(1)
-        load_w3_page(2)
+        for a, tag in enumerate(("quarter2", "w3_raw3")):
+            raw = tile([P, PACK, 2 * P], F32, "w3_pair%d" % a, tag=tag)
+            load_w3(raw[:], a, 2 * P, 2 * P)
+            for u in range(2):
+                w3_raw[2 + u, a] = raw[:, :, P * u : P * (u + 1)]
         w4_second = load_w4(2 * P, 2 * P, "w4_second")
-        load_w3_page(3)
         w4_raw = load_w4(S, S, "w4_raw")
         w3_late = [tile([P, PACK, S], F32, "w3_late%d" % a, tag="half%d" % a) for a in range(GROUPS)]
         for a in range(GROUPS):
@@ -261,7 +265,7 @@ def tile_list_tablet_sign_correction_kernel(
             for a in range(GROUPS):
                 nc.scalar.copy(
                     w3_woven[u][:, a, :].rearrange("p (c i j) -> p c j i", i=4, j=PACK),
-                    w3_raw[u][:, a].rearrange("p j (c i) -> p c j i", i=4),
+                    w3_raw[u, a].rearrange("p j (c i) -> p c j i", i=4),
                 )
 
         def quantise_w3_page(u):
@@ -311,10 +315,16 @@ def tile_list_tablet_sign_correction_kernel(
 
         def sum_turned(u, b, sizes, rests):
             acc = bank(b, "sum%d" % u)
-            for jb in range(PACK):
-                cols = slice(P * jb, P * (jb + 1))
-                nc.tensor.matmul(acc[:, cols], rests[:, jb, u - PACK], ident[:], start=True, stop=False, is_transpose=True)
-                nc.tensor.matmul(acc[:, cols], sizes[:, jb, u - PACK], ident[:], start=False, stop=True, is_transpose=True)
+            for term, first, last in ((rests, 0, None), (sizes, None, PACK - 1)):
+                for jb in range(PACK):
+                    nc.tensor.matmul(
+                        acc[:, P * jb : P * (jb + 1)],
+                        term[:, jb, u - PACK],
+                        ident[:],
+                        start=(jb == first),
+                        stop=(jb == last),
+                        is_transpose=True,
+                    )
             size[u] = small("sum%d" % u, u + 1)
             base[u] = picked[u]
             nc.scalar.copy(size[u][:], acc[:])

@@ -51,6 +51,8 @@ def tile_list_tablet_sign_correction_kernel(
         w4_sc = tile([P, GROUPS, N], U8, "w4_sc")
 
         nc.vector.memset(tab_sc[:].rearrange("p a n -> p (a n)").bitcast(I32), 0)
+        gain_rows = tile([P, P], F32, "gain_rows")
+        nc.gpsimd.memset(gain_rows[:], 0.0)
         nc.gpsimd.memset(w1_sc[:].rearrange("p a n -> p (a n)").bitcast(I32), 0)
         nc.gpsimd.memset(w4_sc[:].rearrange("p a n -> p (a n)").bitcast(I32), 0)
         make_identity(nc, ident[:])
@@ -89,12 +91,11 @@ def tile_list_tablet_sign_correction_kernel(
         tab.append(load_table(1))
         w1_q = tile([P, GROUPS, 2 * N], U8, "w1_q", tag="quarter1")
         nc.sync.dma_start(out=w1_q[:].bitcast(I32), in_=w1_words.bitcast(I32).rearrange("a p c -> p a c"))
+        nc.sync.dma_start(out=gain_rows[0:PACK, :], in_=gain[0:S].rearrange("(u i) -> u i", u=PACK))
         load_scales(w1_sc, w1_scales)
         for u in range(PAGES):
             nc.sync.dma_start(out=pages[u][:], in_=page_in[u])
             if u == 0:
-                with nc.allow_non_contiguous_dma(reason="one gain to a partition and page"):
-                    nc.sync.dma_start(out=gains[0][:], in_=gain[0:S].rearrange("(u p) -> p u", u=PACK))
                 nc.sync.dma_start(out=gains[1][:], in_=gain[S : 2 * S].rearrange("(p t) -> p t", t=PACK))
             if u == 4:
                 load_scales(w4_sc, w4_scales)
@@ -121,6 +122,10 @@ def tile_list_tablet_sign_correction_kernel(
 
         def small(name, slot):
             return tile([P, S], F32, name, tag="small%d" % slot)
+
+        gain_cols = bank(3, "gain_cols")
+        nc.tensor.transpose(gain_cols[:, 0:P], gain_rows[:], ident[:])
+        nc.vector.tensor_copy(gains[0][:], gain_cols[:, 0:PACK])
 
         drafts = [bank(b, "draft%d" % b) for b in range(PAGES)]
         for b in (4, 5, 0, 6, 7, 1, 2, 3):
@@ -372,80 +377,66 @@ def tile_list_tablet_sign_correction_kernel(
 
         y_sc = [tile([P, CHUNK], U8, "y_sc%d" % g) for g in range(GROUPS)]
         codes_out = [out_1[g].rearrange("p m t -> p (m t)").bitcast(I32) for g in range(GROUPS)]
-        y_turned = {}
-        y_woven = {}
+        pairs = []
+        y_turned = []
+        joined = {}
 
         def turn_page(u, banks):
-            if u != 2:
-                whole = tile([P, PACK, 2, P, 2], BF16, "y_turned%d" % u, tag="y_turned%d" % (u % 2))
-                y_turned[u] = [whole[:, 0:2], whole[:, 2:4]]
-            else:
-                y_turned[u] = [tile([P, 2, 2, P, 2], BF16, "y_turned2%d" % a, tag="half%d" % a)[:] for a in range(2)]
-            for k in range(PACK):
-                acc = bank(banks[k], "turn%d%d" % (u, k))
-                for q in range(CHUNKS):
-                    first = CHUNK * q + P * k
-                    nc.tensor.transpose(acc[:, P * q : P * (q + 1)], pages[u][:, first : first + P], ident[:])
-                nc.scalar.copy(y_turned[u][k // 2][:, k % 2], acc[:].rearrange("p (m h e) -> p h m e", h=2, e=2))
+            for c in range(CHUNKS):
+                acc = bank(banks[c], "turn%d%d" % (u, c))
+                for k in range(PACK):
+                    first = CHUNK * c + P * k
+                    nc.tensor.transpose(acc[:, P * k : P * (k + 1)], pages[u][:, first : first + P], ident[:])
+                nc.scalar.copy(
+                    y_turned[c][:, :, :, 32 * u : 32 * (u + 1), :],
+                    acc[:].rearrange("p (k q h e) -> p k h q e", k=PACK, h=2, e=2),
+                )
 
-        def turn_back(u, banks):
-            y_woven[u] = tile([P, CHUNK * PACK], BF16, "y_woven%d" % u, tag="y_woven", bufs=5)
+        def turn_back(c, banks):
+            joined[0, c] = tile([P, CHUNK * PACK], BF16, "y_woven%d" % c, tag="y_woven", bufs=6)
+            words = y_turned[c].rearrange("p k h m e -> p k h (m e)").bitcast(F32)
             for half in range(2):
-                words = y_turned[u][half].rearrange("p k h m e -> p k h (m e)").bitcast(F32)
-                acc = bank(banks[half], "back%d%d" % (u, half))
+                acc = bank(banks[half], "back%d%d" % (c, half))
                 for b in range(2):
                     for h in range(2):
                         nc.tensor.transpose(
-                            acc[:, P * (2 * b + h) : P * (2 * b + h + 1)], words[:, b, h, :], ident[:]
+                            acc[:, P * (2 * b + h) : P * (2 * b + h + 1)], words[:, 2 * half + b, h, :], ident[:]
                         )
                 nc.scalar.copy(
-                    y_woven[u][:].bitcast(F32)[:, S * half : S * (half + 1)].rearrange("p (b c h) -> p b c h", b=2, h=2),
+                    joined[0, c][:].bitcast(F32)[:, S * half : S * (half + 1)].rearrange("p (b c h) -> p b c h", b=2, h=2),
                     acc[:].rearrange("p (b h c) -> p b c h", b=2, h=2),
                 )
 
-        def quantise_page(u):
-            codes = tile([P, CHUNK], I32, "y_codes%d" % u, tag="y_codes", bufs=6)
-            nc.vector.quantize_mx(out=codes[:].bitcast(FP8X4), scales=y_sc[0][4 * u : P, :], in_=y_woven[u][:])
-            for q in range(CHUNKS):
-                nc.sync.dma_start(
-                    out=codes_out[0][32 * u : 32 * (u + 1), CHUNK * q : CHUNK * (q + 1)], in_=codes[32 * q : 32 * (q + 1), :]
-                )
-
-        pairs = []
-
         def round_page(u, first, count, on_vector):
             t = u - PACK
-            raw = pairs[first // 2][:].bitcast(BF16).rearrange("p (c h) (m e) -> p c h m e", h=2, e=2)
-            dst = raw[:, first % 2 : first % 2 + count, t // 2, :, t % 2]
+            raw = pairs[first // 2][:].bitcast(BF16).rearrange("p (h c) (m e) -> p h c m e", h=2, e=2)
+            dst = raw[:, t // 2, first % 2 : first % 2 + count, :, t % 2]
             src = pages[u][:, CHUNK * first : CHUNK * (first + count)].rearrange("p (c m) -> p c m", c=count)
             if on_vector:
                 nc.vector.tensor_copy(dst, src)
             else:
                 nc.scalar.copy(dst, src)
 
-        joined = {}
-
         def join_chunk(c, on_vector):
-            joined[c] = tile([P, CHUNK * PACK], BF16, "y_joined%d" % c, tag="y_woven", bufs=5)
-            dst = joined[c][:].bitcast(F32).rearrange("p (m h) -> p m h", h=2)
-            src = pairs[c // 2][:, 2 * (c % 2) : 2 * (c % 2) + 2, :].rearrange("p h m -> p m h")
+            joined[1, c] = tile([P, CHUNK * PACK], BF16, "y_joined%d" % c, tag="y_woven", bufs=6)
+            dst = joined[1, c][:].bitcast(F32).rearrange("p (m h) -> p m h", h=2)
+            src = pairs[c // 2][:, c % 2 : PACK : 2, :].rearrange("p h m -> p m h")
             if on_vector:
                 nc.vector.tensor_copy(dst, src)
             else:
                 nc.scalar.copy(dst, src)
 
-        def quantise_chunk(c):
-            codes = tile([P, CHUNK], I32, "y_chunk%d" % c, tag="y_codes", bufs=6)
-            nc.vector.quantize_mx(out=codes[:].bitcast(FP8X4), scales=y_sc[1][4 * c : P, :], in_=joined[c][:])
-            nc.sync.dma_start(out=codes_out[1][:, CHUNK * c : CHUNK * (c + 1)], in_=codes[:])
+        def quantise_chunk(g, c):
+            codes = tile([P, CHUNK], I32, "y_chunk%d%d" % (g, c), tag="y_codes", bufs=6)
+            nc.vector.quantize_mx(out=codes[:].bitcast(FP8X4), scales=y_sc[g][4 * c : P, :], in_=joined[g, c][:])
+            nc.sync.dma_start(out=codes_out[g][:, CHUNK * c : CHUNK * (c + 1)], in_=codes[:])
 
         def store_scales(g):
             for q in range(4):
-                if g == 0:
-                    dst = out_2[0, :, CHUNK * q : CHUNK * (q + 1)].bitcast(I32)
-                else:
-                    dst = out_2[1, 4 * q : 4 * q + 4, :].bitcast(I32).rearrange("r (c m) -> c r m", c=CHUNKS)
-                nc.sync.dma_start(out=dst, in_=y_sc[g][32 * q : 32 * q + 16, :].bitcast(I32))
+                nc.sync.dma_start(
+                    out=out_2[g, 4 * q : 4 * q + 4, :].bitcast(I32).rearrange("r (c m) -> c r m", c=CHUNKS),
+                    in_=y_sc[g][32 * q : 32 * q + 16, :].bitcast(I32),
+                )
 
         weave_w3_page(0)
         quantise_w3_page(0)
@@ -517,32 +508,32 @@ def tile_list_tablet_sign_correction_kernel(
         for u, b in ((4, 0), (5, 6), (6, 7), (7, 3)):
             sum_turned(u, b, sizes, rests)
             scatter(u)
+        pairs.extend(tile([P, PACK, CHUNK], F32, "pairs%d" % a, tag="half%d" % a) for a in range(2))
+        y_turned.extend(tile([P, PACK, 2, P, 2], BF16, "y_turned%d" % c)[:] for c in range(2))
+        for a in range(2):
+            upper = pairs[a][:, 2:4, :].rearrange("p r m -> p (r m)").bitcast(BF16)
+            y_turned.append(upper.rearrange("p (k h m e) -> p k h m e", k=PACK, h=2, e=2))
         turn_page(0, (1, 2, 4, 5))
         turn_page(1, (0, 6, 7, 3))
-        turn_back(0, (1, 2))
-        turn_back(1, (4, 5))
-        turn_page(2, (0, 6, 7, 3))
-        turn_page(3, (1, 2, 4, 5))
-        turn_back(2, (0, 6))
-        turn_back(3, (7, 3))
-        for u in range(2):
-            quantise_page(u)
-        pairs.extend(tile([P, PACK, CHUNK], F32, "pairs%d" % a, tag="half%d" % a) for a in range(2))
+        turn_page(2, (1, 2, 4, 5))
+        turn_page(3, (0, 6, 7, 3))
+        for c, banks in enumerate(((1, 2), (4, 5), (0, 6), (7, 3))):
+            turn_back(c, banks)
         for u in (4, 5):
             round_page(u, 0, 2, True)
             round_page(u, 2, 2, True)
-        for u in range(2, PACK):
-            quantise_page(u)
+        for c in range(CHUNKS):
+            quantise_chunk(0, c)
         store_scales(0)
-        for u in (6, 7):
-            round_page(u, 2, 2, False)
-            round_page(u, 0, 2, False)
-        join_chunk(3, True)
-        join_chunk(2, True)
-        quantise_chunk(3)
-        quantise_chunk(2)
-        join_chunk(0, False)
-        quantise_chunk(0)
-        join_chunk(1, False)
-        quantise_chunk(1)
+        for first in (0, 2):
+            for u in (6, 7):
+                round_page(u, first, 2, False)
+        join_chunk(0, True)
+        join_chunk(1, True)
+        quantise_chunk(1, 0)
+        quantise_chunk(1, 1)
+        join_chunk(2, False)
+        quantise_chunk(1, 2)
+        join_chunk(3, False)
+        quantise_chunk(1, 3)
         store_scales(1)

@@ -426,6 +426,13 @@ def tile_list_tablet_sign_correction_kernel(
             else:
                 nc.scalar.copy(dst, src)
 
+        def weave_chunk(c):
+            joined[1, c] = tile([P, CHUNK * PACK], BF16, "y_joined%d" % c, tag="y_woven", bufs=6)
+            nc.scalar.copy(
+                joined[1, c][:].rearrange("p (c i t) -> p c t i", i=4, t=PACK),
+                wide[c][:].rearrange("p t (c i) -> p c t i", i=4),
+            )
+
         def quantise_chunk(g, c):
             codes = tile([P, CHUNK], I32, "y_chunk%d%d" % (g, c), tag="y_codes", bufs=6)
             nc.vector.quantize_mx(out=codes[:].bitcast(FP8X4), scales=y_sc[g][4 * c : P, :], in_=joined[g, c][:])
@@ -507,33 +514,33 @@ def tile_list_tablet_sign_correction_kernel(
         sizes = turned_products(w3_late_q, (1, 2, 4, 5), ACT.Abs, "half0")
         for u, b in ((4, 0), (5, 6), (6, 7), (7, 3)):
             sum_turned(u, b, sizes, rests)
-            scatter(u)
-        pairs.extend(tile([P, PACK, CHUNK], F32, "pairs%d" % a, tag="half%d" % a) for a in range(2))
-        y_turned.extend(tile([P, PACK, 2, P, 2], BF16, "y_turned%d" % c)[:] for c in range(2))
+        wide = {2: tile([P, PACK, CHUNK], F32, "wide2"), 3: tile([P, PACK, CHUNK], F32, "wide3", tag="half1")}
+        for u in range(PACK, PAGES):
+            nc.vector.tensor_tensor(pages[u][:].indirect(offsets[:]), base[u][:], size[u][:], ALU.add)
+            for c in wide:
+                nc.sync.dma_start(out=wide[c][:, u - PACK, :], in_=pages[u][:, CHUNK * c : CHUNK * (c + 1)])
+            nc.sync.dma_start(out=page_out[u], in_=pages[u][:])
+        pairs.append(tile([P, PACK, CHUNK], F32, "pairs", tag="half0"))
+        y_turned.extend(tile([P, PACK, 2, P, 2], BF16, "y_turned%d" % c, tag="quarter%d" % (2 * c))[:] for c in range(2))
         for a in range(2):
-            upper = pairs[a][:, 2:4, :].rearrange("p r m -> p (r m)").bitcast(BF16)
-            y_turned.append(upper.rearrange("p (k h m e) -> p k h m e", k=PACK, h=2, e=2))
+            part = pairs[0][:, 2 * a : 2 * a + 2, :].rearrange("p r m -> p (r m)").bitcast(BF16)
+            y_turned.append(part.rearrange("p (k h m e) -> p k h m e", k=PACK, h=2, e=2))
         turn_page(0, (1, 2, 4, 5))
         turn_page(1, (0, 6, 7, 3))
         turn_page(2, (1, 2, 4, 5))
         turn_page(3, (0, 6, 7, 3))
         for c, banks in enumerate(((1, 2), (4, 5), (0, 6), (7, 3))):
             turn_back(c, banks)
-        for u in (4, 5):
-            round_page(u, 0, 2, True)
-            round_page(u, 2, 2, True)
         for c in range(CHUNKS):
             quantise_chunk(0, c)
         store_scales(0)
-        for first in (0, 2):
-            for u in (6, 7):
-                round_page(u, first, 2, False)
+        for u in range(PACK, PAGES):
+            round_page(u, 0, 1, True)
+            round_page(u, 1, 1, False)
         join_chunk(0, True)
+        weave_chunk(2)
+        weave_chunk(3)
         join_chunk(1, True)
-        quantise_chunk(1, 0)
-        quantise_chunk(1, 1)
-        join_chunk(2, False)
-        quantise_chunk(1, 2)
-        join_chunk(3, False)
-        quantise_chunk(1, 3)
+        for c in range(CHUNKS):
+            quantise_chunk(1, c)
         store_scales(1)

@@ -3,7 +3,7 @@ from contextlib import ExitStack
 import concourse.mybir as mybir
 from concourse.masks import make_identity
 
-K, N, T, S = 1024, 1024, 2048, 512
+N, T, S = 1024, 2048, 512
 FLOPS = 3 * 2 * 1024 * 1024 * 512
 
 F32 = mybir.dt.float32
@@ -24,6 +24,8 @@ PAGES = GROUPS * PACK
 CHUNK = 512
 CHUNKS = T // CHUNK
 HALF = S // 2
+LIST_ROWS = 16
+RING = 6
 
 
 def tile_list_tablet_sign_correction_kernel(
@@ -37,10 +39,59 @@ def tile_list_tablet_sign_correction_kernel(
         def tile(shape, dtype, name, tag=None, bufs=1):
             return keep.tile(shape, dtype, name=name, tag=tag or name, bufs=bufs, align_bytes=64)
 
+        def small(name, slot):
+            return tile([P, S], F32, name, tag="small%d" % slot)
+
         def bank(b, name):
             return psum.tile([P, S], F32, name=name, tag="bank%d" % b)
 
-        offsets = keep.tile([P, S // 16], U16, name="offsets")
+        def copy_on(on_vector, dst, src):
+            if on_vector:
+                nc.vector.tensor_copy(dst, src)
+            else:
+                nc.scalar.copy(dst, src)
+
+        def block(i):
+            return slice(P * i, P * (i + 1))
+
+        def mx_pass(acc, stationary, moving, a):
+            nc.tensor.matmul_mx(
+                out=acc,
+                lhsT=stationary[0],
+                lhsT_scale=stationary[1],
+                rhs=moving[0],
+                rhs_scale=moving[1],
+                start=(a == 0),
+                stop=(a == GROUPS - 1),
+            )
+
+        def weave_views(woven, rows):
+            return (
+                woven.rearrange("p (c i t) -> p c t i", i=4, t=PACK),
+                rows.rearrange("p t (c i) -> p c t i", i=4),
+            )
+
+        def turn_pairs_back(words, woven, banks, name):
+            for half in range(2):
+                acc = bank(banks[half], "%s%d" % (name, half))
+                for k in range(2):
+                    for h in range(2):
+                        nc.tensor.transpose(acc[:, block(2 * k + h)], words[:, 2 * half + k, h, :], ident[:])
+                nc.scalar.copy(
+                    woven[:].bitcast(F32)[:, S * half : S * (half + 1)].rearrange("p (k c h) -> p k c h", k=2, h=2),
+                    acc[:].rearrange("p (k h c) -> p k c h", k=2, h=2),
+                )
+
+        def round_turned(turned, u, acc):
+            nc.scalar.copy(
+                turned[:, :, :, 32 * u : 32 * (u + 1), :],
+                acc[:].rearrange("p (k q h e) -> p k h q e", k=PACK, h=2, e=2),
+            )
+
+        def as_words(turned):
+            return turned.rearrange("p k h m e -> p k h (m e)").bitcast(F32)
+
+        offsets = keep.tile([P, S // LIST_ROWS], U16, name="offsets")
         gains = [tile([P, PACK], F32, "gains%d" % g) for g in range(GROUPS)]
         gain_of = [gains[u // PACK][:, u % PACK : u % PACK + 1] for u in range(PAGES)]
         ident = tile([P, P], F32, "ident")
@@ -59,8 +110,8 @@ def tile_list_tablet_sign_correction_kernel(
 
         dealt_in = gT[S : 2 * S, :].rearrange("(p t) c -> t p c", t=PACK)
         dealt_out = out_0[S : 2 * S, :].rearrange("(p t) c -> t p c", t=PACK)
-        page_in = [gT[P * u : P * (u + 1), :] for u in range(PACK)] + [dealt_in[t] for t in range(PACK)]
-        page_out = [out_0[P * u : P * (u + 1), :] for u in range(PACK)] + [dealt_out[t] for t in range(PACK)]
+        page_in = [gT[block(u), :] for u in range(PACK)] + [dealt_in[t] for t in range(PACK)]
+        page_out = [out_0[block(u), :] for u in range(PACK)] + [dealt_out[t] for t in range(PACK)]
         w4_cols = w4_words.rearrange("a p n t -> p a (n t)").bitcast(I32)
 
         def load_scales(dst, src):
@@ -77,7 +128,7 @@ def tile_list_tablet_sign_correction_kernel(
 
         def load_w3(raw, a, first, count):
             nc.sync.dma_start(
-                out=raw, in_=w3[S * a : S * (a + 1), first : first + count].rearrange("(p j) c -> p j c", j=PACK)
+                out=raw, in_=w3[S * a : S * (a + 1), first : first + count].rearrange("(p t) c -> p t c", t=PACK)
             )
 
         def load_w4(first, count, name):
@@ -97,62 +148,46 @@ def tile_list_tablet_sign_correction_kernel(
             nc.sync.dma_start(out=pages[u][:], in_=page_in[u])
             if u == 0:
                 nc.sync.dma_start(out=gains[1][:], in_=gain[S : 2 * S].rearrange("(p t) -> p t", t=PACK))
-            if u == 4:
+            if u == PACK:
                 load_scales(w4_sc, w4_scales)
 
         v_q = [tile([P, S], I32, "v_q%d" % a) for a in range(GROUPS)]
         v_sc = [tile([P, S], U8, "v_sc%d" % a) for a in range(GROUPS)]
         halves = [slice(HALF * h, HALF * (h + 1)) for h in range(2)]
-        half_offsets = [offsets[:, 16 * h : 16 * (h + 1)] for h in range(2)]
+        half_offsets = [offsets[:, HALF // LIST_ROWS * h : HALF // LIST_ROWS * (h + 1)] for h in range(2)]
 
         def gather_words(a, h):
             nc.vector.tensor_copy(v_q[a][:, halves[h]].bitcast(U32), tab[a][:].bitcast(U32).indirect(half_offsets[h]))
 
-        def gather_scales(a, h):
-            nc.vector.tensor_copy(v_sc[a][:, halves[h]], tab_sc[:, a, :].indirect(half_offsets[h]))
+        def gather_scales(h):
+            for a in range(GROUPS):
+                nc.vector.tensor_copy(v_sc[a][:, halves[h]], tab_sc[:, a, :].indirect(half_offsets[h]))
 
         gather_words(0, 0)
-        gather_scales(0, 0)
-        gather_scales(1, 0)
+        gather_scales(0)
         gather_words(0, 1)
         gather_words(1, 0)
         gather_words(1, 1)
-        gather_scales(0, 1)
-        gather_scales(1, 1)
-
-        def small(name, slot):
-            return tile([P, S], F32, name, tag="small%d" % slot)
+        gather_scales(1)
 
         gain_cols = bank(3, "gain_cols")
         nc.tensor.transpose(gain_cols[:, 0:P], gain_rows[:], ident[:])
         nc.vector.tensor_copy(gains[0][:], gain_cols[:, 0:PACK])
 
         drafts = [bank(b, "draft%d" % b) for b in range(PAGES)]
-        for b in (4, 5, 0, 6, 7, 1, 2, 3):
+
+        def draft_natural(u):
             for a in range(GROUPS):
-                cols = slice(P * (b % PACK), P * (b % PACK + 1))
-                if b < PACK:
-                    nc.tensor.matmul_mx(
-                        out=drafts[b][:],
-                        lhsT=w1_q[:, a, 2 * cols.start : 2 * cols.stop].bitcast(FP4X4),
-                        lhsT_scale=w1_sc[:, a, cols],
-                        rhs=v_q[a][:].bitcast(FP8X4),
-                        rhs_scale=v_sc[a][:],
-                        start=(a == 0),
-                        stop=(a == GROUPS - 1),
-                    )
-                else:
-                    nc.tensor.matmul_mx(
-                        out=drafts[b][:],
-                        lhsT=v_q[a][:, cols].bitcast(FP8X4),
-                        lhsT_scale=v_sc[a][:, cols],
-                        rhs=w1_q[:, a, N : 2 * N].bitcast(FP4X4),
-                        rhs_scale=w1_sc[:, a, S : 2 * S],
-                        start=(a == 0),
-                        stop=(a == GROUPS - 1),
-                    )
+                w1_cols = (w1_q[:, a, 2 * P * u : 2 * P * (u + 1)].bitcast(FP4X4), w1_sc[:, a, block(u)])
+                mx_pass(drafts[u][:], w1_cols, (v_q[a][:].bitcast(FP8X4), v_sc[a][:]), a)
+
+        def draft_turned(jb):
+            for a in range(GROUPS):
+                w1_cols = (w1_q[:, a, N : 2 * N].bitcast(FP4X4), w1_sc[:, a, S : 2 * S])
+                mx_pass(drafts[PACK + jb][:], (v_q[a][:, block(jb)].bitcast(FP8X4), v_sc[a][:, block(jb)]), w1_cols, a)
+
         gained = {}
-        turned = {}
+        draft_t = {}
 
         def tanh_natural(u):
             draft = small("draft%d" % u, u)
@@ -161,82 +196,69 @@ def tile_list_tablet_sign_correction_kernel(
             nc.scalar.activation(gained[u][:], draft[:], ACT.Copy, scale=gain_of[u])
 
         def tanh_turned(jb):
-            turned[jb] = small("turned%d" % jb, 2 * PACK + jb)
+            draft_t[jb] = small("draft_t%d" % jb, 2 * PACK + jb)
             nc.scalar.activation(
-                turned[jb][:].rearrange("p (t m) -> p t m", t=PACK),
+                draft_t[jb][:].rearrange("p (t m) -> p t m", t=PACK),
                 drafts[PACK + jb][:].rearrange("p (m t) -> p t m", t=PACK),
                 ACT.Tanh,
             )
 
-        tanh_turned(0)
-        tanh_turned(1)
-        tanh_natural(0)
-        tanh_turned(2)
-        tanh_turned(3)
-        for u in range(1, PACK):
-            tanh_natural(u)
+        for natural, turned in ((draft_natural, draft_turned), (tanh_natural, tanh_turned)):
+            turned(0)
+            turned(1)
+            natural(0)
+            turned(2)
+            turned(3)
+            for u in range(1, PACK):
+                natural(u)
         for t in range(PACK):
-            back = bank(PACK + t, "back%d" % t)
+            u = PACK + t
+            back = bank(u, "draft_back%d" % t)
             for jb in range(PACK):
-                nc.tensor.transpose(back[:, P * jb : P * (jb + 1)], turned[jb][:, P * t : P * (t + 1)], ident[:])
-            if t == 1:
-                gained[PACK + t] = tile([P, S], F32, "gained5", tag="z_q0")
-            else:
-                gained[PACK + t] = small("gained%d" % (PACK + t), t)
-            nc.scalar.activation(gained[PACK + t][:], back[:], ACT.Copy, scale=gain_of[PACK + t])
+                nc.tensor.transpose(back[:, block(jb)], draft_t[jb][:, block(t)], ident[:])
+            gained[u] = tile([P, S], F32, "gained5", tag="z_q0") if t == 1 else small("gained%d" % u, t)
+            nc.scalar.activation(gained[u][:], back[:], ACT.Copy, scale=gain_of[u])
 
         def gather(u):
             nc.vector.tensor_copy(picked[u][:], pages[u][:].indirect(offsets[:]))
 
-        z_sc = [tile([P, S], U8, "z_sc%d" % a) for a in range(GROUPS)]
+        def form_z(out, u, cols):
+            nc.vector.scalar_tensor_tensor(out, picked[u][:, cols], gain_of[u], gained[u][:, cols], ALU.mult, ALU.subtract)
 
+        whole = slice(0, S)
+        z_sc = [tile([P, S], U8, "z_sc%d" % a) for a in range(GROUPS)]
         z_turned = tile([P, PACK, 2, P, 2], BF16, "z_turned", tag="quarter2")
         for u in range(PACK):
             gather(u)
-            nc.vector.scalar_tensor_tensor(gained[u][:], picked[u][:], gain_of[u], gained[u][:], ALU.mult, ALU.subtract)
+            form_z(gained[u][:], u, whole)
             acc = bank(u, "z_turn%d" % u)
             for jb in range(PACK):
-                cols = slice(P * jb, P * (jb + 1))
-                nc.tensor.transpose(acc[:, cols], gained[u][:, cols], ident[:])
-            nc.scalar.copy(
-                z_turned[:, :, :, 32 * u : 32 * (u + 1), :], acc[:].rearrange("p (b q h e) -> p b h q e", b=PACK, h=2, e=2)
-            )
-        z_woven = [tile([P, S * PACK], BF16, "z_woven0", tag="quarter3"), tile([P, S * PACK], BF16, "z_woven1", tag="quarter5")]
-        z_words = z_turned[:].rearrange("p b h m e -> p b h (m e)").bitcast(F32)
-        for half in range(2):
-            words = bank(half, "z_words%d" % half)
-            for b in range(2):
-                for h in range(2):
-                    nc.tensor.transpose(words[:, P * (2 * b + h) : P * (2 * b + h + 1)], z_words[:, 2 * half + b, h, :], ident[:])
-            nc.scalar.copy(
-                z_woven[0][:].bitcast(F32)[:, S * half : S * (half + 1)].rearrange("p (b j e) -> p b j e", b=2, e=2),
-                words[:].rearrange("p (b e j) -> p b j e", b=2, e=2),
-            )
+                nc.tensor.transpose(acc[:, block(jb)], gained[u][:, block(jb)], ident[:])
+            round_turned(z_turned[:], u, acc)
+        z_woven = [tile([P, S * PACK], BF16, "z_woven%d" % a, tag="quarter%d" % (3 + 2 * a)) for a in range(GROUPS)]
+        turn_pairs_back(as_words(z_turned[:]), z_woven[0], (0, 1), "z_back")
+
         z_q = {}
         z_rows = tile([P, PACK, S], BF16, "z_rows", tag="quarter4")
-        weave_dst = z_woven[1][:].rearrange("p (c i t) -> p c t i", i=4, t=PACK)
-        weave_src = z_rows[:].rearrange("p t (c i) -> p c t i", i=4)
+        z_weave_dst, z_weave_src = weave_views(z_woven[1][:], z_rows[:])
         for t in range(PACK - 1):
-            u = PACK + t
-            gather(u)
-            nc.vector.scalar_tensor_tensor(
-                z_rows[:, t, :], picked[u][:], gain_of[u], gained[u][:], ALU.mult, ALU.subtract
-            )
+            gather(PACK + t)
+            form_z(z_rows[:, t, :], PACK + t, whole)
             if t == 1:
                 z_q[0] = tile([P, S], I32, "z_q0")
                 nc.vector.quantize_mx(out=z_q[0][:].bitcast(FP8X4), scales=z_sc[0][:], in_=z_woven[0][:])
-                nc.scalar.copy(weave_dst[:, :, 0:2, :], weave_src[:, :, 0:2, :])
+                nc.scalar.copy(z_weave_dst[:, :, 0:2, :], z_weave_src[:, :, 0:2, :])
         last = PAGES - 1
         for h in range(2):
             nc.vector.tensor_copy(picked[last][:, halves[h]], pages[last][:].indirect(half_offsets[h]))
         for cols in halves:
-            nc.vector.scalar_tensor_tensor(
-                z_rows[:, PACK - 1, cols], picked[last][:, cols], gain_of[last], gained[last][:, cols], ALU.mult, ALU.subtract
-            )
+            form_z(z_rows[:, PACK - 1, cols], last, cols)
+
+        def z_operand(a, cols):
+            return z_q[a][:, cols].bitcast(FP8X4), z_sc[a][:, cols]
 
         w3_raw = {}
         w3_q = {}
-        w3_sc = {}
         w4_q = {}
 
         def load_w3_page(u):
@@ -246,32 +268,31 @@ def tile_list_tablet_sign_correction_kernel(
                 load_w3(w3_raw[u, a], a, P * u, P)
 
         load_w3_page(0)
-        w4_first = load_w4(0, 2 * P, "w4_first")
+        w4_natural = [load_w4(0, 2 * P, "w4_first")]
         load_w3_page(1)
-        for a, tag in enumerate(("quarter2", "w3_raw3")):
+        for a, tag in enumerate(("quarter2", "w3_pair1")):
             raw = tile([P, PACK, 2 * P], F32, "w3_pair%d" % a, tag=tag)
             load_w3(raw[:], a, 2 * P, 2 * P)
             for u in range(2):
-                w3_raw[2 + u, a] = raw[:, :, P * u : P * (u + 1)]
-        w4_second = load_w4(2 * P, 2 * P, "w4_second")
-        w4_raw = load_w4(S, S, "w4_raw")
+                w3_raw[2 + u, a] = raw[:, :, block(u)]
+        w4_natural.append(load_w4(2 * P, 2 * P, "w4_second"))
+        w4_late = load_w4(S, S, "w4_late")
         w3_late = [tile([P, PACK, S], F32, "w3_late%d" % a, tag="half%d" % a) for a in range(GROUPS)]
         for a in range(GROUPS):
             load_w3(w3_late[a][:], a, S, S)
         for u in range(PACK):
             for a in range(GROUPS):
-                cols = slice(P * (u % 2), P * (u % 2 + 1))
-                w4_q[u, a] = ((w4_first, w4_second)[u // 2][:, a, cols], w4_sc[:, a, P * u : P * (u + 1)])
+                w4_q[u, a] = (w4_natural[u // 2][:, a, block(u % 2)].bitcast(FP8X4), w4_sc[:, a, block(u)])
+        w4_late_q = [(w4_late[:, a, :].bitcast(FP8X4), w4_sc[:, a, S : 2 * S]) for a in range(GROUPS)]
 
         w3_woven = {}
+        w3_late_woven = {}
+        w3_late_q = {}
 
         def weave_w3_page(u):
-            w3_woven[u] = tile([P, GROUPS, P * PACK], BF16, "w3_woven%d" % u, tag="w3_woven%d" % u)
+            w3_woven[u] = tile([P, GROUPS, P * PACK], BF16, "w3_woven%d" % u)
             for a in range(GROUPS):
-                nc.scalar.copy(
-                    w3_woven[u][:, a, :].rearrange("p (c i j) -> p c j i", i=4, j=PACK),
-                    w3_raw[u, a].rearrange("p j (c i) -> p c j i", i=4),
-                )
+                nc.scalar.copy(*weave_views(w3_woven[u][:, a, :], w3_raw[u, a]))
 
         def quantise_w3_page(u):
             codes = tile([P, GROUPS * P], I32, "w3_codes%d" % u)
@@ -280,162 +301,162 @@ def tile_list_tablet_sign_correction_kernel(
                 out=codes[:].bitcast(FP8X4), scales=scales[:], in_=w3_woven[u][:].rearrange("p a c -> p (a c)")
             )
             for a in range(GROUPS):
-                w3_q[u, a] = (codes[:, P * a : P * (a + 1)], scales[:, P * a : P * (a + 1)])
+                w3_q[u, a] = (codes[:, block(a)].bitcast(FP8X4), scales[:, block(a)])
 
         def weave_w3_late(a):
-            w3_woven[PACK + a] = tile([P, S * PACK], BF16, "w3_late_woven%d" % a, tag="quarter%d" % (4 + a))
-            nc.scalar.copy(
-                w3_woven[PACK + a][:].rearrange("p (c i j) -> p c j i", i=4, j=PACK),
-                w3_late[a][:].rearrange("p j (c i) -> p c j i", i=4),
-            )
+            w3_late_woven[a] = tile([P, S * PACK], BF16, "w3_late_woven%d" % a, tag="quarter%d" % (4 + a))
+            nc.scalar.copy(*weave_views(w3_late_woven[a][:], w3_late[a][:]))
 
         def quantise_w3_late(a):
             codes = tile([P, S], I32, "w3_late_codes%d" % a)
             scales = tile([P, S], U8, "w3_late_scales%d" % a)
-            nc.vector.quantize_mx(out=codes[:].bitcast(FP8X4), scales=scales[:], in_=w3_woven[PACK + a][:])
-            w3_late_q[a] = (codes[:], scales[:])
-
-        w3_late_q = {}
-        w4_late_q = {a: (w4_raw[:, a, :], w4_sc[:, a, S : 2 * S]) for a in range(GROUPS)}
-
-        def turned_products(weights, banks, func, tag):
-            out = tile([P, PACK, PACK, P], F32, "turned_" + tag, tag=tag)
-            accs = [bank(b, "turned_%s%d" % (tag, b)) for b in banks]
-            for a in range(GROUPS):
-                codes, scales = weights[a]
-                for jb in range(PACK):
-                    cols = slice(P * jb, P * (jb + 1))
-                    nc.tensor.matmul_mx(
-                        out=accs[jb][:],
-                        lhsT=z_q[a][:, cols].bitcast(FP8X4),
-                        lhsT_scale=z_sc[a][:, cols],
-                        rhs=codes.bitcast(FP8X4),
-                        rhs_scale=scales,
-                        start=(a == 0),
-                        stop=(a == GROUPS - 1),
-                    )
-            for jb in range(PACK):
-                nc.scalar.activation(out[:, jb], accs[jb][:].rearrange("p (m t) -> p t m", t=PACK), func)
-            return out
-
-        def sum_turned(u, b, sizes, rests):
-            acc = bank(b, "sum%d" % u)
-            for term, first, last in ((rests, 0, None), (sizes, None, PACK - 1)):
-                for jb in range(PACK):
-                    nc.tensor.matmul(
-                        acc[:, P * jb : P * (jb + 1)],
-                        term[:, jb, u - PACK],
-                        ident[:],
-                        start=(jb == first),
-                        stop=(jb == last),
-                        is_transpose=True,
-                    )
-            size[u] = small("sum%d" % u, u + 1)
-            base[u] = picked[u]
-            nc.scalar.copy(size[u][:], acc[:])
+            nc.vector.quantize_mx(out=codes[:].bitcast(FP8X4), scales=scales[:], in_=w3_late_woven[a][:])
+            w3_late_q[a] = (codes[:].bitcast(FP8X4), scales[:])
 
         y3 = {}
         y4 = {}
+        size = {}
+        base = {}
 
         def products(u, bank3, bank4):
             y3[u] = bank(bank3, "y3_%d" % u)
             y4[u] = bank(bank4, "y4_%d" % u)
             for a in range(GROUPS):
-                for acc, (codes, scales) in ((y3[u], w3_q[u, a]), (y4[u], w4_q[u, a])):
-                    nc.tensor.matmul_mx(
-                        out=acc[:],
-                        lhsT=codes.bitcast(FP8X4),
-                        lhsT_scale=scales,
-                        rhs=z_q[a][:].bitcast(FP8X4),
-                        rhs_scale=z_sc[a][:],
-                        start=(a == 0),
-                        stop=(a == GROUPS - 1),
-                    )
+                mx_pass(y3[u][:], w3_q[u, a], z_operand(a, whole), a)
+                mx_pass(y4[u][:], w4_q[u, a], z_operand(a, whole), a)
 
-        size = {}
-        base = {}
+        def take_abs(u, out):
+            size[u] = out
+            nc.scalar.activation(out[:], y3[u][:], ACT.Abs)
 
-        def take_abs(u):
-            if u == 2:
-                size[u] = tile([P, S], F32, "size2", tag="quarter4")
-            else:
-                size[u] = small("size%d" % u, u + 1)
-            nc.scalar.activation(size[u][:], y3[u][:], ACT.Abs)
+        def add_state(u, out):
+            base[u] = out
+            nc.vector.tensor_tensor(out[:], y4[u][:], picked[u][:], ALU.add)
 
-        def add_state(u):
-            if u < 2:
-                base[u] = tile([P, S], F32, "base%d" % u, tag="w3_woven%d" % (u + 2))
-            elif u == 2:
-                base[u] = tile([P, S], F32, "base%d" % u, tag="quarter5")
-            else:
-                base[u] = small("base%d" % u, u)
-            nc.vector.tensor_tensor(base[u][:], y4[u][:], picked[u][:], ALU.add)
+        def scatter(u, first, second):
+            nc.vector.tensor_tensor(pages[u][:].indirect(offsets[:]), first[:], second[:], ALU.add)
 
-        def scatter(u):
-            nc.vector.tensor_tensor(pages[u][:].indirect(offsets[:]), base[u][:], size[u][:], ALU.add)
+        def store_page(u):
             nc.sync.dma_start(out=page_out[u], in_=pages[u][:])
 
         y_sc = [tile([P, CHUNK], U8, "y_sc%d" % g) for g in range(GROUPS)]
-        codes_out = [out_1[g].rearrange("p m t -> p (m t)").bitcast(I32) for g in range(GROUPS)]
-        pairs = []
-        y_turned = []
-        joined = {}
 
-        def turn_page(u, banks):
-            for c in range(CHUNKS):
-                acc = bank(banks[c], "turn%d%d" % (u, c))
-                for k in range(PACK):
-                    first = CHUNK * c + P * k
-                    nc.tensor.transpose(acc[:, P * k : P * (k + 1)], pages[u][:, first : first + P], ident[:])
-                nc.scalar.copy(
-                    y_turned[c][:, :, :, 32 * u : 32 * (u + 1), :],
-                    acc[:].rearrange("p (k q h e) -> p k h q e", k=PACK, h=2, e=2),
-                )
-
-        def turn_back(c, banks):
-            joined[0, c] = tile([P, CHUNK * PACK], BF16, "y_woven%d" % c, tag="y_woven", bufs=6)
-            words = y_turned[c].rearrange("p k h m e -> p k h (m e)").bitcast(F32)
-            for half in range(2):
-                acc = bank(banks[half], "back%d%d" % (c, half))
-                for b in range(2):
-                    for h in range(2):
-                        nc.tensor.transpose(
-                            acc[:, P * (2 * b + h) : P * (2 * b + h + 1)], words[:, 2 * half + b, h, :], ident[:]
-                        )
-                nc.scalar.copy(
-                    joined[0, c][:].bitcast(F32)[:, S * half : S * (half + 1)].rearrange("p (b c h) -> p b c h", b=2, h=2),
-                    acc[:].rearrange("p (b h c) -> p b c h", b=2, h=2),
-                )
-
-        def round_page(u, first, count, on_vector):
-            t = u - PACK
-            raw = pairs[first // 2][:].bitcast(BF16).rearrange("p (h c) (m e) -> p h c m e", h=2, e=2)
-            dst = raw[:, t // 2, first % 2 : first % 2 + count, :, t % 2]
-            src = pages[u][:, CHUNK * first : CHUNK * (first + count)].rearrange("p (c m) -> p c m", c=count)
-            if on_vector:
-                nc.vector.tensor_copy(dst, src)
-            else:
-                nc.scalar.copy(dst, src)
-
-        def join_chunk(c, on_vector):
-            joined[1, c] = tile([P, CHUNK * PACK], BF16, "y_joined%d" % c, tag="y_woven", bufs=6)
-            dst = joined[1, c][:].bitcast(F32).rearrange("p (m h) -> p m h", h=2)
-            src = pairs[c // 2][:, c % 2 : PACK : 2, :].rearrange("p h m -> p m h")
-            if on_vector:
-                nc.vector.tensor_copy(dst, src)
-            else:
-                nc.scalar.copy(dst, src)
-
-        def weave_chunk(c):
-            joined[1, c] = tile([P, CHUNK * PACK], BF16, "y_joined%d" % c, tag="y_woven", bufs=6)
-            nc.scalar.copy(
-                joined[1, c][:].rearrange("p (c i t) -> p c t i", i=4, t=PACK),
-                wide[c][:].rearrange("p t (c i) -> p c t i", i=4),
+        weave_w3_page(0)
+        quantise_w3_page(0)
+        for h in range(2):
+            fours = slice(HALF // 4 * h, HALF // 4 * (h + 1))
+            nc.vector.tensor_copy(z_weave_dst[:, fours, 2:4, :], z_weave_src[:, fours, 2:4, :])
+        z_q[1] = tile([P, S], I32, "z_q1", tag="w3_woven0")
+        for h in range(2):
+            nc.vector.quantize_mx(
+                out=z_q[1][:, halves[h]].bitcast(FP8X4),
+                scales=z_sc[1][:, halves[h]],
+                in_=z_woven[1][:, PACK * HALF * h : PACK * HALF * (h + 1)],
             )
+        y3_half = [bank(b, "y3_half%d" % b)[:, 0:HALF] for b in (0, 4)]
+        y4_half = [bank(b, "y4_half%d" % b)[:, 0:HALF] for b in (2, 5)]
+        for accs, weights in ((y4_half, w4_q), (y3_half, w3_q)):
+            for h in range(2):
+                mx_pass(accs[h], weights[0, 0], z_operand(0, halves[h]), 0)
+        for h in range(2):
+            mx_pass(y3_half[h], w3_q[0, 1], z_operand(1, halves[h]), 1)
+            mx_pass(y4_half[h], w4_q[0, 1], z_operand(1, halves[h]), 1)
+        weave_w3_page(1)
+        quantise_w3_page(1)
+        size[0] = tile([P, S], F32, "size0", tag="quarter1")
+        base[0] = tile([P, S], F32, "base0", tag="w3_woven1")
+        for h in range(2):
+            nc.scalar.activation(size[0][:, halves[h]], y3_half[h], ACT.Abs)
+        products(1, 1, 3)
+        for h in range(2):
+            nc.vector.tensor_tensor(base[0][:, halves[h]], y4_half[h], picked[0][:, halves[h]], ALU.add)
+            nc.vector.tensor_tensor(
+                pages[0][:].indirect(half_offsets[h]), base[0][:, halves[h]], size[0][:, halves[h]], ALU.add
+            )
+        store_page(0)
+
+        take_abs(1, small("size1", 2))
+        pair_woven = tile([P, 2, GROUPS, P * PACK], BF16, "w3_pair_woven")
+        for u in range(2):
+            for a in range(GROUPS):
+                nc.scalar.copy(*weave_views(pair_woven[:, u, a, :], w3_raw[2 + u, a]))
+        pair_codes = tile([P, 2, GROUPS, P], I32, "w3_pair_codes")
+        pair_scales = tile([P, 2, GROUPS, P], U8, "w3_pair_scales")
+        nc.vector.quantize_mx(
+            out=pair_codes[:].rearrange("p u a c -> p (u a c)").bitcast(FP8X4),
+            scales=pair_scales[:].rearrange("p u a c -> p (u a c)"),
+            in_=pair_woven[:].rearrange("p u a c -> p (u a c)"),
+        )
+        for u in range(2):
+            for a in range(GROUPS):
+                w3_q[2 + u, a] = (pair_codes[:, u, a, :].bitcast(FP8X4), pair_scales[:, u, a, :])
+        products(2, 0, 2)
+        add_state(1, tile([P, S], F32, "base1", tag="w3_pair_woven"))
+        scatter(1, base[1], size[1])
+        store_page(1)
+        weave_w3_late(0)
+        weave_w3_late(1)
+        quantise_w3_late(0)
+        take_abs(2, tile([P, S], F32, "size2", tag="quarter4"))
+        products(3, 0, 3)
+        quantise_w3_late(1)
+        add_state(2, tile([P, S], F32, "base2", tag="quarter5"))
+        scatter(2, base[2], size[2])
+        store_page(2)
+        take_abs(3, small("size3", 4))
+        add_state(3, small("base3", 3))
+        scatter(3, base[3], size[3])
+        store_page(3)
+
+        def turned_products(weights, banks, func, slot):
+            out = tile([P, PACK, PACK, P], F32, "turned_" + slot, tag=slot)
+            accs = [bank(b, "turned_%s%d" % (slot, b)) for b in banks]
+            for a in range(GROUPS):
+                for jb in range(PACK):
+                    mx_pass(accs[jb][:], z_operand(a, block(jb)), weights[a], a)
+            for jb in range(PACK):
+                nc.scalar.activation(out[:, jb], accs[jb][:].rearrange("p (m t) -> p t m", t=PACK), func)
+            return out
+
+        def sum_turned(t, b):
+            acc = bank(b, "sum%d" % t)
+            for term, first, final in ((y4_t, 0, None), (size_t, None, PACK - 1)):
+                for jb in range(PACK):
+                    nc.tensor.matmul(
+                        acc[:, block(jb)], term[:, jb, t], ident[:], start=(jb == first), stop=(jb == final), is_transpose=True
+                    )
+            out = small("sum%d" % t, PACK + 1 + t)
+            nc.scalar.copy(out[:], acc[:])
+            return out
+
+        set_a, set_b = (1, 2, 4, 5), (0, 6, 7, 3)
+        y4_t = turned_products(w4_late_q, (4, 5, 6, 7), ACT.Copy, "half1")
+        size_t = turned_products(w3_late_q, set_a, ACT.Abs, "half0")
+        sums = [sum_turned(t, set_b[t]) for t in range(PACK)]
+
+        wide = {2: tile([P, PACK, CHUNK], F32, "wide2"), 3: tile([P, PACK, CHUNK], F32, "wide3", tag="half1")}
+        for t in range(PACK):
+            u = PACK + t
+            scatter(u, picked[u], sums[t])
+            for c in wide:
+                nc.sync.dma_start(out=wide[c][:, t, :], in_=pages[u][:, CHUNK * c : CHUNK * (c + 1)])
+            store_page(u)
+
+        pairs = tile([P, PACK, CHUNK], F32, "pairs", tag="half0")
+        y_turned = [tile([P, PACK, 2, P, 2], BF16, "y_turned%d" % c, tag="quarter%d" % (2 * c))[:] for c in range(2)]
+        for h in range(2):
+            part = pairs[:, 2 * h : 2 * h + 2, :].rearrange("p r m -> p (r m)").bitcast(BF16)
+            y_turned.append(part.rearrange("p (k h m e) -> p k h m e", k=PACK, h=2, e=2))
+        y_woven = {}
+        codes_out = [out_1[g].rearrange("p m t -> p (m t)").bitcast(I32) for g in range(GROUPS)]
+
+        def new_woven(g, c):
+            y_woven[g, c] = tile([P, CHUNK * PACK], BF16, "y_woven%d%d" % (g, c), tag="y_woven", bufs=RING)
+            return y_woven[g, c]
 
         def quantise_chunk(g, c):
-            codes = tile([P, CHUNK], I32, "y_chunk%d%d" % (g, c), tag="y_codes", bufs=6)
-            nc.vector.quantize_mx(out=codes[:].bitcast(FP8X4), scales=y_sc[g][4 * c : P, :], in_=joined[g, c][:])
+            codes = tile([P, CHUNK], I32, "y_codes%d%d" % (g, c), tag="y_codes", bufs=RING)
+            nc.vector.quantize_mx(out=codes[:].bitcast(FP8X4), scales=y_sc[g][4 * c : P, :], in_=y_woven[g, c][:])
             nc.sync.dma_start(out=codes_out[g][:, CHUNK * c : CHUNK * (c + 1)], in_=codes[:])
 
         def store_scales(g):
@@ -445,102 +466,43 @@ def tile_list_tablet_sign_correction_kernel(
                     in_=y_sc[g][32 * q : 32 * q + 16, :].bitcast(I32),
                 )
 
-        weave_w3_page(0)
-        quantise_w3_page(0)
-        for h in range(2):
-            lines = slice(64 * h, 64 * (h + 1))
-            nc.vector.tensor_copy(weave_dst[:, lines, 2:4, :], weave_src[:, lines, 2:4, :])
-        z_q[1] = tile([P, S], I32, "z_q1", tag="w3_woven0")
-        for h in range(2):
-            nc.vector.quantize_mx(
-                out=z_q[1][:, halves[h]].bitcast(FP8X4),
-                scales=z_sc[1][:, halves[h]],
-                in_=z_woven[1][:, PACK * HALF * h : PACK * HALF * (h + 1)],
-            )
-        first3 = [bank(b, "first3_%d" % b) for b in (0, 4)]
-        first4 = [bank(b, "first4_%d" % b) for b in (2, 5)]
-
-        def half_pass(acc, weights, a, h):
-            codes, scales = weights[0, a]
-            nc.tensor.matmul_mx(
-                out=acc[h][:, 0:HALF],
-                lhsT=codes.bitcast(FP8X4),
-                lhsT_scale=scales,
-                rhs=z_q[a][:, halves[h]].bitcast(FP8X4),
-                rhs_scale=z_sc[a][:, halves[h]],
-                start=(a == 0),
-                stop=(a == GROUPS - 1),
-            )
-
-        for acc, weights in ((first4, w4_q), (first3, w3_q)):
-            for h in range(2):
-                half_pass(acc, weights, 0, h)
-        for h in range(2):
-            half_pass(first3, w3_q, 1, h)
-            half_pass(first4, w4_q, 1, h)
-        weave_w3_page(1)
-        quantise_w3_page(1)
-        size[0] = tile([P, S], F32, "size0", tag="quarter1")
-        base[0] = tile([P, S], F32, "base0", tag="w3_woven1")
-        for h in range(2):
-            nc.scalar.activation(size[0][:, halves[h]], first3[h][:, 0:HALF], ACT.Abs)
-        products(1, 1, 3)
-        for h in range(2):
-            nc.vector.tensor_tensor(base[0][:, halves[h]], first4[h][:, 0:HALF], picked[0][:, halves[h]], ALU.add)
-            nc.vector.tensor_tensor(
-                pages[0][:].indirect(half_offsets[h]), base[0][:, halves[h]], size[0][:, halves[h]], ALU.add
-            )
-        nc.sync.dma_start(out=page_out[0], in_=pages[0][:])
-        take_abs(1)
-        weave_w3_page(2)
-        weave_w3_page(3)
-        quantise_w3_page(2)
-        quantise_w3_page(3)
-        products(2, 0, 2)
-        add_state(1)
-        scatter(1)
-        weave_w3_late(0)
-        weave_w3_late(1)
-        quantise_w3_late(0)
-        take_abs(2)
-        products(3, 0, 3)
-        quantise_w3_late(1)
-        add_state(2)
-        scatter(2)
-        take_abs(3)
-        add_state(3)
-        scatter(3)
-        rests = turned_products(w4_late_q, (4, 5, 6, 7), ACT.Copy, "half1")
-        sizes = turned_products(w3_late_q, (1, 2, 4, 5), ACT.Abs, "half0")
-        for u, b in ((4, 0), (5, 6), (6, 7), (7, 3)):
-            sum_turned(u, b, sizes, rests)
-        wide = {2: tile([P, PACK, CHUNK], F32, "wide2"), 3: tile([P, PACK, CHUNK], F32, "wide3", tag="half1")}
-        for u in range(PACK, PAGES):
-            nc.vector.tensor_tensor(pages[u][:].indirect(offsets[:]), base[u][:], size[u][:], ALU.add)
-            for c in wide:
-                nc.sync.dma_start(out=wide[c][:, u - PACK, :], in_=pages[u][:, CHUNK * c : CHUNK * (c + 1)])
-            nc.sync.dma_start(out=page_out[u], in_=pages[u][:])
-        pairs.append(tile([P, PACK, CHUNK], F32, "pairs", tag="half0"))
-        y_turned.extend(tile([P, PACK, 2, P, 2], BF16, "y_turned%d" % c, tag="quarter%d" % (2 * c))[:] for c in range(2))
-        for a in range(2):
-            part = pairs[0][:, 2 * a : 2 * a + 2, :].rearrange("p r m -> p (r m)").bitcast(BF16)
-            y_turned.append(part.rearrange("p (k h m e) -> p k h m e", k=PACK, h=2, e=2))
-        turn_page(0, (1, 2, 4, 5))
-        turn_page(1, (0, 6, 7, 3))
-        turn_page(2, (1, 2, 4, 5))
-        turn_page(3, (0, 6, 7, 3))
-        for c, banks in enumerate(((1, 2), (4, 5), (0, 6), (7, 3))):
-            turn_back(c, banks)
+        for u in range(PACK):
+            for c in range(CHUNKS):
+                acc = bank((set_a, set_b)[u % 2][c], "turn%d%d" % (u, c))
+                for k in range(PACK):
+                    nc.tensor.transpose(acc[:, block(k)], pages[u][:, block(PACK * c + k)], ident[:])
+                round_turned(y_turned[c], u, acc)
+        both_sets = set_a + set_b
+        for c in range(CHUNKS):
+            turn_pairs_back(as_words(y_turned[c]), new_woven(0, c), both_sets[2 * c : 2 * c + 2], "back%d" % c)
         for c in range(CHUNKS):
             quantise_chunk(0, c)
         store_scales(0)
-        for u in range(PACK, PAGES):
-            round_page(u, 0, 1, True)
-            round_page(u, 1, 1, False)
-        join_chunk(0, True)
-        weave_chunk(2)
-        weave_chunk(3)
-        join_chunk(1, True)
-        for c in range(CHUNKS):
+
+        pair_values = pairs[:].bitcast(BF16).rearrange("p (h c) (m e) -> p h c m e", h=2, e=2)
+        for t in range(PACK):
+            for c in range(2):
+                src = pages[PACK + t][:, CHUNK * c : CHUNK * (c + 1)].rearrange("p (c m) -> p c m", c=1)
+                copy_on(c == 0, pair_values[:, t // 2, c : c + 1, :, t % 2], src)
+
+        def join_chunk(c):
+            nc.vector.tensor_copy(
+                new_woven(1, c)[:].bitcast(F32).rearrange("p (m h) -> p m h", h=2),
+                pairs[:, c:PACK:2, :].rearrange("p h m -> p m h"),
+            )
+
+        join_chunk(0)
+        nc.scalar.copy(*weave_views(new_woven(1, 2)[:], wide[2][:]))
+        last_woven = new_woven(1, 3)
+        column_halves = [slice(CHUNK // 2 * h, CHUNK // 2 * (h + 1)) for h in range(2)]
+        woven_halves = [last_woven[:, PACK * cols.start : PACK * cols.stop] for cols in column_halves]
+        for h in range(2):
+            nc.scalar.copy(*weave_views(woven_halves[h], wide[3][:, :, column_halves[h]]))
+        join_chunk(1)
+        for c in range(CHUNKS - 1):
             quantise_chunk(1, c)
+        last_codes = tile([P, CHUNK], I32, "y_codes13", tag="y_codes", bufs=RING)
+        for h, cols in enumerate(column_halves):
+            nc.vector.quantize_mx(out=last_codes[:, cols].bitcast(FP8X4), scales=y_sc[1][12:P, cols], in_=woven_halves[h])
+            nc.sync.dma_start(out=codes_out[1][:, 3 * CHUNK + cols.start : 3 * CHUNK + cols.stop], in_=last_codes[:, cols])
         store_scales(1)

@@ -442,11 +442,9 @@ def tile_list_tablet_sign_correction_kernel(
                 nc.sync.dma_start(out=wide[c][:, t, :], in_=pages[u][:, CHUNK * c : CHUNK * (c + 1)])
             store_page(u)
 
-        pairs = tile([P, PACK, CHUNK], F32, "pairs", tag="half0")
+        late_turned = tile([P, 2, PACK, 2, P, 2], BF16, "y_turned23", tag="half0")
         y_turned = [tile([P, PACK, 2, P, 2], BF16, "y_turned%d" % c, tag="quarter%d" % (2 * c))[:] for c in range(2)]
-        for h in range(2):
-            part = pairs[:, 2 * h : 2 * h + 2, :].rearrange("p r m -> p (r m)").bitcast(BF16)
-            y_turned.append(part.rearrange("p (k h m e) -> p k h m e", k=PACK, h=2, e=2))
+        y_turned.extend(late_turned[:, c] for c in range(2))
         y_woven = {}
         codes_out = [out_1[g].rearrange("p m t -> p (m t)").bitcast(I32) for g in range(GROUPS)]
 
@@ -454,10 +452,12 @@ def tile_list_tablet_sign_correction_kernel(
             y_woven[g, c] = tile([P, CHUNK * PACK], BF16, "y_woven%d%d" % (g, c), tag="y_woven", bufs=RING)
             return y_woven[g, c]
 
-        def quantise_chunk(g, c):
-            codes = tile([P, CHUNK], I32, "y_codes%d%d" % (g, c), tag="y_codes", bufs=RING)
+        def quantise_chunk(g, c, codes):
             nc.vector.quantize_mx(out=codes[:].bitcast(FP8X4), scales=y_sc[g][4 * c : P, :], in_=y_woven[g, c][:])
             nc.sync.dma_start(out=codes_out[g][:, CHUNK * c : CHUNK * (c + 1)], in_=codes[:])
+
+        def ring_codes(g, c):
+            return tile([P, CHUNK], I32, "y_codes%d%d" % (g, c), tag="y_codes", bufs=RING)
 
         def store_scales(g):
             for q in range(4):
@@ -476,33 +476,36 @@ def tile_list_tablet_sign_correction_kernel(
         for c in range(CHUNKS):
             turn_pairs_back(as_words(y_turned[c]), new_woven(0, c), both_sets[2 * c : 2 * c + 2], "back%d" % c)
         for c in range(CHUNKS):
-            quantise_chunk(0, c)
+            quantise_chunk(0, c, ring_codes(0, c))
         store_scales(0)
 
-        pair_values = pairs[:].bitcast(BF16).rearrange("p (h c) (m e) -> p h c m e", h=2, e=2)
-        for t in range(PACK):
+        dealt_turned = [tile([P, PACK, 2, P, 2], BF16, "dealt_turned%d" % c, tag="quarter%d" % (2 * c)) for c in range(2)]
+        for h in range(2):
             for c in range(2):
-                src = pages[PACK + t][:, CHUNK * c : CHUNK * (c + 1)].rearrange("p (c m) -> p c m", c=1)
-                copy_on(c == 0, pair_values[:, t // 2, c : c + 1, :, t % 2], src)
+                for half in range(2):
+                    acc = bank((set_a, set_b)[h][2 * c + half], "pair%d%d%d" % (h, c, half))
+                    for k in range(2):
+                        for e in range(2):
+                            cols = block(PACK * c + 2 * half + k)
+                            nc.tensor.transpose(acc[:, block(2 * k + e)], pages[PACK + 2 * h + e][:, cols], ident[:])
+                    nc.scalar.copy(
+                        dealt_turned[c][:, 2 * half : 2 * half + 2, h, :, :],
+                        acc[:].rearrange("p (k e m) -> p k m e", k=2, e=2),
+                    )
+        for c in range(2):
+            turn_pairs_back(as_words(dealt_turned[c][:]), new_woven(1, c), set_a[2 * c : 2 * c + 2], "dealt_back%d" % c)
 
-        def join_chunk(c):
-            nc.vector.tensor_copy(
-                new_woven(1, c)[:].bitcast(F32).rearrange("p (m h) -> p m h", h=2),
-                pairs[:, c:PACK:2, :].rearrange("p h m -> p m h"),
-            )
-
-        join_chunk(0)
-        nc.scalar.copy(*weave_views(new_woven(1, 2)[:], wide[2][:]))
-        last_woven = new_woven(1, 3)
+        nc.vector.tensor_copy(*weave_views(new_woven(1, 3)[:], wide[3][:]))
+        quantise_chunk(1, 3, ring_codes(1, 3))
+        quantise_chunk(1, 0, tile([P, CHUNK], I32, "y_codes10", tag="half1"))
+        last_woven = new_woven(1, 2)
         column_halves = [slice(CHUNK // 2 * h, CHUNK // 2 * (h + 1)) for h in range(2)]
         woven_halves = [last_woven[:, PACK * cols.start : PACK * cols.stop] for cols in column_halves]
         for h in range(2):
-            nc.scalar.copy(*weave_views(woven_halves[h], wide[3][:, :, column_halves[h]]))
-        join_chunk(1)
-        for c in range(CHUNKS - 1):
-            quantise_chunk(1, c)
-        last_codes = tile([P, CHUNK], I32, "y_codes13", tag="y_codes", bufs=RING)
+            copy_on(h == 0, *weave_views(woven_halves[h], wide[2][:, :, column_halves[h]]))
+        quantise_chunk(1, 1, ring_codes(1, 1))
+        last_codes = ring_codes(1, 2)
         for h, cols in enumerate(column_halves):
-            nc.vector.quantize_mx(out=last_codes[:, cols].bitcast(FP8X4), scales=y_sc[1][12:P, cols], in_=woven_halves[h])
-            nc.sync.dma_start(out=codes_out[1][:, 3 * CHUNK + cols.start : 3 * CHUNK + cols.stop], in_=last_codes[:, cols])
+            nc.vector.quantize_mx(out=last_codes[:, cols].bitcast(FP8X4), scales=y_sc[1][8:P, cols], in_=woven_halves[h])
+            nc.sync.dma_start(out=codes_out[1][:, 2 * CHUNK + cols.start : 2 * CHUNK + cols.stop], in_=last_codes[:, cols])
         store_scales(1)

@@ -142,8 +142,8 @@ def tile_list_tablet_sign_correction_kernel(
         tab.append(load_table(1))
         w1_q = tile([P, GROUPS, 2 * N], U8, "w1_q", tag="quarter1")
         nc.sync.dma_start(out=w1_q[:].bitcast(I32), in_=w1_words.bitcast(I32).rearrange("a p c -> p a c"))
-        nc.sync.dma_start(out=gain_rows[0:PACK, :], in_=gain[0:S].rearrange("(u i) -> u i", u=PACK))
         load_scales(w1_sc, w1_scales)
+        nc.sync.dma_start(out=gain_rows[0:PACK, :], in_=gain[0:S].rearrange("(u i) -> u i", u=PACK))
         for u in range(PAGES):
             nc.sync.dma_start(out=pages[u][:], in_=page_in[u])
             if u == 0:
@@ -187,6 +187,7 @@ def tile_list_tablet_sign_correction_kernel(
                 mx_pass(drafts[PACK + jb][:], (v_q[a][:, block(jb)].bitcast(FP8X4), v_sc[a][:, block(jb)]), w1_cols, a)
 
         gained = {}
+        gained_halves = {}
         draft_t = {}
 
         def tanh_natural(u):
@@ -204,55 +205,81 @@ def tile_list_tablet_sign_correction_kernel(
             )
 
         for natural, turned in ((draft_natural, draft_turned), (tanh_natural, tanh_turned)):
-            turned(0)
-            turned(1)
-            natural(0)
-            turned(2)
-            turned(3)
-            for u in range(1, PACK):
-                natural(u)
+            for h in range(2):
+                natural(h)
+                turned(2 * h)
+                turned(2 * h + 1)
+            natural(2)
+            natural(3)
+        draft_back = {}
         for t in range(PACK):
             u = PACK + t
             back = bank(u, "draft_back%d" % t)
+            draft_back[u] = back
             for jb in range(PACK):
                 nc.tensor.transpose(back[:, block(jb)], draft_t[jb][:, block(t)], ident[:])
-            gained[u] = tile([P, S], F32, "gained5", tag="z_q0") if t == 1 else small("gained%d" % u, t)
-            nc.scalar.activation(gained[u][:], back[:], ACT.Copy, scale=gain_of[u])
+            if t >= 2:
+                continue
+            if t == 1:
+                gained_halves[u] = [tile([P, HALF], F32, "gained5a", tag="z_q0")[:], small("gained5b", t)[:, 0:HALF]]
+                for h in range(2):
+                    nc.scalar.activation(gained_halves[u][h], back[:, halves[h]], ACT.Copy, scale=gain_of[u])
+            else:
+                gained[u] = small("gained%d" % u, t)
+                nc.scalar.activation(gained[u][:], back[:], ACT.Copy, scale=gain_of[u])
+        for u in gained:
+            gained_halves[u] = [gained[u][:, cols] for cols in halves]
 
         def gather(u):
-            nc.vector.tensor_copy(picked[u][:], pages[u][:].indirect(offsets[:]))
+            for h in range(2):
+                nc.vector.tensor_copy(picked[u][:, halves[h]], pages[u][:].indirect(half_offsets[h]))
 
-        def form_z(out, u, cols):
-            nc.vector.scalar_tensor_tensor(out, picked[u][:, cols], gain_of[u], gained[u][:, cols], ALU.mult, ALU.subtract)
+        def form_z(out, u, h):
+            nc.vector.scalar_tensor_tensor(out, picked[u][:, halves[h]], gain_of[u], gained_halves[u][h], ALU.mult, ALU.subtract)
 
         whole = slice(0, S)
         z_sc = [tile([P, S], U8, "z_sc%d" % a) for a in range(GROUPS)]
         z_turned = tile([P, PACK, 2, P, 2], BF16, "z_turned", tag="quarter2")
         for u in range(PACK):
             gather(u)
-            form_z(gained[u][:], u, whole)
-            acc = bank(u, "z_turn%d" % u)
-            for jb in range(PACK):
-                nc.tensor.transpose(acc[:, block(jb)], gained[u][:, block(jb)], ident[:])
-            round_turned(z_turned[:], u, acc)
+            for h in range(2):
+                form_z(gained_halves[u][h], u, h)
+            if u < PACK - 1:
+                acc = bank(u, "z_turn%d" % u)
+                for jb in range(PACK):
+                    nc.tensor.transpose(acc[:, block(jb)], gained[u][:, block(jb)], ident[:])
+                round_turned(z_turned[:], u, acc)
+            else:
+                for h in range(2):
+                    acc = bank(u - h, "z_turn%d%d" % (u, h))
+                    for k in range(2):
+                        nc.tensor.transpose(acc[:, block(k)], gained[u][:, block(2 * h + k)], ident[:])
+                    nc.scalar.copy(
+                        z_turned[:, 2 * h : 2 * h + 2, :, 32 * u : 32 * (u + 1), :],
+                        acc[:, 0:HALF].rearrange("p (k q h e) -> p k h q e", k=2, h=2, e=2),
+                    )
         z_woven = [tile([P, S * PACK], BF16, "z_woven%d" % a, tag="quarter%d" % (3 + 2 * a)) for a in range(GROUPS)]
         turn_pairs_back(as_words(z_turned[:]), z_woven[0], (0, 1), "z_back")
+        late_gained = tile([P, 2, S], F32, "late_gained", tag="quarter2")
+        for i, u in enumerate((PAGES - 2, PAGES - 1)):
+            nc.scalar.activation(late_gained[:, i, :], draft_back[u][:], ACT.Copy, scale=gain_of[u])
+            gained_halves[u] = [late_gained[:, i, cols] for cols in halves]
 
         z_q = {}
         z_rows = tile([P, PACK, S], BF16, "z_rows", tag="quarter4")
         z_weave_dst, z_weave_src = weave_views(z_woven[1][:], z_rows[:])
         for t in range(PACK - 1):
             gather(PACK + t)
-            form_z(z_rows[:, t, :], PACK + t, whole)
+            for h in range(2):
+                form_z(z_rows[:, t, halves[h]], PACK + t, h)
             if t == 1:
                 z_q[0] = tile([P, S], I32, "z_q0")
                 nc.vector.quantize_mx(out=z_q[0][:].bitcast(FP8X4), scales=z_sc[0][:], in_=z_woven[0][:])
                 nc.scalar.copy(z_weave_dst[:, :, 0:2, :], z_weave_src[:, :, 0:2, :])
         last = PAGES - 1
+        gather(last)
         for h in range(2):
-            nc.vector.tensor_copy(picked[last][:, halves[h]], pages[last][:].indirect(half_offsets[h]))
-        for cols in halves:
-            form_z(z_rows[:, PACK - 1, cols], last, cols)
+            form_z(z_rows[:, PACK - 1, halves[h]], last, h)
 
         def z_operand(a, cols):
             return z_q[a][:, cols].bitcast(FP8X4), z_sc[a][:, cols]
@@ -270,7 +297,7 @@ def tile_list_tablet_sign_correction_kernel(
         load_w3_page(0)
         w4_natural = [load_w4(0, 2 * P, "w4_first")]
         load_w3_page(1)
-        for a, tag in enumerate(("quarter2", "w3_pair1")):
+        for a, tag in enumerate(("small7", "w3_pair1")):
             raw = tile([P, PACK, 2 * P], F32, "w3_pair%d" % a, tag=tag)
             load_w3(raw[:], a, 2 * P, 2 * P)
             for u in range(2):
@@ -488,7 +515,8 @@ def tile_list_tablet_sign_correction_kernel(
                         for e in range(2):
                             cols = block(PACK * c + 2 * half + k)
                             nc.tensor.transpose(acc[:, block(2 * k + e)], pages[PACK + 2 * h + e][:, cols], ident[:])
-                    nc.scalar.copy(
+                    copy_on(
+                        h == 1 and c == 1,
                         dealt_turned[c][:, 2 * half : 2 * half + 2, h, :, :],
                         acc[:].rearrange("p (k e m) -> p k m e", k=2, e=2),
                     )
@@ -501,8 +529,9 @@ def tile_list_tablet_sign_correction_kernel(
         last_woven = new_woven(1, 2)
         column_halves = [slice(CHUNK // 2 * h, CHUNK // 2 * (h + 1)) for h in range(2)]
         woven_halves = [last_woven[:, PACK * cols.start : PACK * cols.stop] for cols in column_halves]
-        for h in range(2):
-            copy_on(h == 0, *weave_views(woven_halves[h], wide[2][:, :, column_halves[h]]))
+        for first, count in ((0, P), (P, P), (2 * P, 2 * P)):
+            cols = slice(first, first + count)
+            copy_on(first == 0, *weave_views(last_woven[:, PACK * cols.start : PACK * cols.stop], wide[2][:, :, cols]))
         quantise_chunk(1, 1, ring_codes(1, 1))
         last_codes = ring_codes(1, 2)
         for h, cols in enumerate(column_halves):

@@ -515,8 +515,7 @@ def tile_list_tablet_sign_correction_kernel(
                         for e in range(2):
                             cols = block(PACK * c + 2 * half + k)
                             nc.tensor.transpose(acc[:, block(2 * k + e)], pages[PACK + 2 * h + e][:, cols], ident[:])
-                    copy_on(
-                        h == 1 and c == 1,
+                    nc.scalar.copy(
                         dealt_turned[c][:, 2 * half : 2 * half + 2, h, :, :],
                         acc[:].rearrange("p (k e m) -> p k m e", k=2, e=2),
                     )

@@ -97,14 +97,14 @@ def tile_list_tablet_sign_correction_kernel(
         ident = tile([P, P], F32, "ident")
         pages = [tile([P, T], F32, "page%d" % u) for u in range(PAGES)]
         picked = [tile([P, S], F32, "picked%d" % u) for u in range(PAGES)]
-        tab_sc = tile([P, GROUPS, T], U8, "tab_sc", tag="quarter0")
+        tab_sc = tile([P, T], U8, "tab_sc", tag="quarter0")
+        v_sc = tile([P, GROUPS, S], U8, "v_sc")
         w1_sc = tile([P, GROUPS, N], U8, "w1_sc")
         w4_sc = tile([P, GROUPS, N], U8, "w4_sc")
 
-        nc.vector.memset(tab_sc[:].rearrange("p a n -> p (a n)").bitcast(I32), 0)
-        gain_rows = tile([P, P], F32, "gain_rows")
-        nc.gpsimd.memset(gain_rows[:], 0.0)
-        nc.gpsimd.memset(w1_sc[:].rearrange("p a n -> p (a n)").bitcast(I32), 0)
+        nc.vector.memset(tab_sc[:].bitcast(I32), 0)
+        nc.vector.memset(w1_sc[:].rearrange("p a n -> p (a n)").bitcast(I32), 0)
+        nc.vector.memset(v_sc[:].rearrange("p a n -> p (a n)").bitcast(I32), 0)
         nc.gpsimd.memset(w4_sc[:].rearrange("p a n -> p (a n)").bitcast(I32), 0)
         make_identity(nc, ident[:])
 
@@ -114,8 +114,8 @@ def tile_list_tablet_sign_correction_kernel(
         page_out = [out_0[block(u), :] for u in range(PACK)] + [dealt_out[t] for t in range(PACK)]
         w4_cols = w4_words.rearrange("a p n t -> p a (n t)").bitcast(I32)
 
-        def load_scales(dst, src):
-            for r in range(4):
+        def load_scales(dst, src, rows=range(4)):
+            for r in rows:
                 nc.sync.dma_start(
                     out=dst[r:P:32, :, :].bitcast(I32),
                     in_=src[:, r:16:4, :].bitcast(I32).rearrange("a q n -> q a n"),
@@ -137,13 +137,22 @@ def tile_list_tablet_sign_correction_kernel(
             return raw
 
         nc.sync.dma_start(offsets[:], offs)
+        with nc.allow_non_contiguous_dma(reason="one gain a partition and page"):
+            nc.sync.dma_start(out=gains[0][:], in_=gain[0:S].rearrange("(u p) -> p u", u=PACK))
+        for a in range(GROUPS):
+            nc.sync.dma_start(out=tab_sc[4 * a : P : 8, :].bitcast(I32), in_=tab_scales[a].bitcast(I32))
         tab = [load_table(0)]
-        load_scales(tab_sc, tab_scales)
+        load_scales(w1_sc, w1_scales, (0, 1, 2))
         tab.append(load_table(1))
+        load_scales(w1_sc, w1_scales, (3,))
+        spread_sc = tile([P, S], U8, "spread_sc")
+        nc.vector.tensor_copy(spread_sc[:], tab_sc[:].indirect(offsets[:]))
+        for q in range(4):
+            nc.sync.dma_start(
+                out=v_sc[32 * q : 32 * q + 4, :, :].bitcast(I32), in_=spread_sc[32 * q : 32 * q + 32 : 4, :].bitcast(I32)
+            )
         w1_q = tile([P, GROUPS, 2 * N], U8, "w1_q", tag="quarter1")
         nc.sync.dma_start(out=w1_q[:].bitcast(I32), in_=w1_words.bitcast(I32).rearrange("a p c -> p a c"))
-        load_scales(w1_sc, w1_scales)
-        nc.sync.dma_start(out=gain_rows[0:PACK, :], in_=gain[0:S].rearrange("(u i) -> u i", u=PACK))
         for u in range(PAGES):
             nc.sync.dma_start(out=pages[u][:], in_=page_in[u])
             if u == 0:
@@ -152,39 +161,27 @@ def tile_list_tablet_sign_correction_kernel(
                 load_scales(w4_sc, w4_scales)
 
         v_q = [tile([P, S], I32, "v_q%d" % a) for a in range(GROUPS)]
-        v_sc = [tile([P, S], U8, "v_sc%d" % a) for a in range(GROUPS)]
         halves = [slice(HALF * h, HALF * (h + 1)) for h in range(2)]
         half_offsets = [offsets[:, HALF // LIST_ROWS * h : HALF // LIST_ROWS * (h + 1)] for h in range(2)]
 
         def gather_words(a, h):
             nc.vector.tensor_copy(v_q[a][:, halves[h]].bitcast(U32), tab[a][:].bitcast(U32).indirect(half_offsets[h]))
 
-        def gather_scales(h):
-            for a in range(GROUPS):
-                nc.vector.tensor_copy(v_sc[a][:, halves[h]], tab_sc[:, a, :].indirect(half_offsets[h]))
-
-        gather_words(0, 0)
-        gather_scales(0)
-        gather_words(0, 1)
-        gather_words(1, 0)
-        gather_words(1, 1)
-        gather_scales(1)
-
-        gain_cols = bank(3, "gain_cols")
-        nc.tensor.transpose(gain_cols[:, 0:P], gain_rows[:], ident[:])
-        nc.vector.tensor_copy(gains[0][:], gain_cols[:, 0:PACK])
+        for a in range(GROUPS):
+            for h in range(2):
+                gather_words(a, h)
 
         drafts = [bank(b, "draft%d" % b) for b in range(PAGES)]
 
         def draft_natural(u):
             for a in range(GROUPS):
                 w1_cols = (w1_q[:, a, 2 * P * u : 2 * P * (u + 1)].bitcast(FP4X4), w1_sc[:, a, block(u)])
-                mx_pass(drafts[u][:], w1_cols, (v_q[a][:].bitcast(FP8X4), v_sc[a][:]), a)
+                mx_pass(drafts[u][:], w1_cols, (v_q[a][:].bitcast(FP8X4), v_sc[:, a, :]), a)
 
         def draft_turned(jb):
             for a in range(GROUPS):
                 w1_cols = (w1_q[:, a, N : 2 * N].bitcast(FP4X4), w1_sc[:, a, S : 2 * S])
-                mx_pass(drafts[PACK + jb][:], (v_q[a][:, block(jb)].bitcast(FP8X4), v_sc[a][:, block(jb)]), w1_cols, a)
+                mx_pass(drafts[PACK + jb][:], (v_q[a][:, block(jb)].bitcast(FP8X4), v_sc[:, a, block(jb)]), w1_cols, a)
 
         gained = {}
         gained_halves = {}

@@ -137,11 +137,12 @@ def tile_list_tablet_sign_correction_kernel(
             return raw
 
         nc.sync.dma_start(offsets[:], offs)
-        with nc.allow_non_contiguous_dma(reason="one gain a partition and page"):
-            nc.sync.dma_start(out=gains[0][:], in_=gain[0:S].rearrange("(u p) -> p u", u=PACK))
+        tab = [tile([P, T], I32, "tab0", tag="half0")]
+        first_words = tab_words[0].rearrange("p n t -> p (n t)").bitcast(I32)
+        nc.sync.dma_start(out=tab[0][:, 0 : T // 2], in_=first_words[:, 0 : T // 2])
         for a in range(GROUPS):
             nc.sync.dma_start(out=tab_sc[4 * a : P : 8, :].bitcast(I32), in_=tab_scales[a].bitcast(I32))
-        tab = [load_table(0)]
+        nc.sync.dma_start(out=tab[0][:, T // 2 : T], in_=first_words[:, T // 2 : T])
         load_scales(w1_sc, w1_scales, (0, 1, 2))
         tab.append(load_table(1))
         load_scales(w1_sc, w1_scales, (3,))
@@ -156,6 +157,9 @@ def tile_list_tablet_sign_correction_kernel(
         for u in range(PAGES):
             nc.sync.dma_start(out=pages[u][:], in_=page_in[u])
             if u == 0:
+                with nc.allow_non_contiguous_dma(reason="one gain a partition and page"):
+                    nc.sync.dma_start(out=gains[0][:], in_=gain[0:S].rearrange("(u p) -> p u", u=PACK))
+            if u == 1:
                 nc.sync.dma_start(out=gains[1][:], in_=gain[S : 2 * S].rearrange("(p t) -> p t", t=PACK))
             if u == PACK:
                 load_scales(w4_sc, w4_scales)

from contextlib import ExitStack

import concourse.mybir as mybir
from concourse.masks import make_identity

N, T, S = 1024, 2048, 512
FLOPS = 3 * 2 * 1024 * 1024 * 512

F32 = mybir.dt.float32
BF16 = mybir.dt.bfloat16
I32 = mybir.dt.int32
U32 = mybir.dt.uint32
U16 = mybir.dt.uint16
U8 = mybir.dt.uint8
FP8X4 = mybir.dt.float8_e4m3fn_x4
FP4X4 = mybir.dt.float4_e2m1fn_x4
ACT = mybir.ActivationFunctionType
ALU = mybir.AluOpType

P = 128
PACK = 4
GROUPS = 2
PAGES = GROUPS * PACK
CHUNK = 512
CHUNKS = T // CHUNK
HALF = S // 2
LIST_ROWS = 16
RING = 6


def tile_list_tablet_sign_correction_kernel(
    tc, tab_words, tab_scales, w1_words, w1_scales, w3, w4_words, w4_scales, gain, gT, offs, out_0, out_1, out_2
):
    nc = tc.nc
    with ExitStack() as ctx:
        keep = ctx.enter_context(tc.tile_pool(name="keep", bufs=1))
        psum = ctx.enter_context(tc.psum_pool(name="psum", bufs=1))

        def tile(shape, dtype, name, tag=None, bufs=1):
            return keep.tile(shape, dtype, name=name, tag=tag or name, bufs=bufs, align_bytes=64)

        def small(name, slot):
            return tile([P, S], F32, name, tag="small%d" % slot)

        def bank(b, name):
            return psum.tile([P, S], F32, name=name, tag="bank%d" % b)

        def copy_on(on_vector, dst, src):
            if on_vector:
                nc.vector.tensor_copy(dst, src)
            else:
                nc.scalar.copy(dst, src)

        def block(i):
            return slice(P * i, P * (i + 1))

        def mx_pass(acc, stationary, moving, a):
            nc.tensor.matmul_mx(
                out=acc,
                lhsT=stationary[0],
                lhsT_scale=stationary[1],
                rhs=moving[0],
                rhs_scale=moving[1],
                start=(a == 0),
                stop=(a == GROUPS - 1),
            )

        def weave_views(woven, rows):
            return (
                woven.rearrange("p (c i t) -> p c t i", i=4, t=PACK),
                rows.rearrange("p t (c i) -> p c t i", i=4),
            )

        def turn_pairs_back(words, woven, banks, name):
            for half in range(2):
                acc = bank(banks[half], "%s%d" % (name, half))
                for k in range(2):
                    for h in range(2):
                        nc.tensor.transpose(acc[:, block(2 * k + h)], words[:, 2 * half + k, h, :], ident[:])
                nc.scalar.copy(
                    woven[:].bitcast(F32)[:, S * half : S * (half + 1)].rearrange("p (k c h) -> p k c h", k=2, h=2),
                    acc[:].rearrange("p (k h c) -> p k c h", k=2, h=2),
                )

        def round_turned(turned, u, acc):
            nc.scalar.copy(
                turned[:, :, :, 32 * u : 32 * (u + 1), :],
                acc[:].rearrange("p (k q h e) -> p k h q e", k=PACK, h=2, e=2),
            )

        def as_words(turned):
            return turned.rearrange("p k h m e -> p k h (m e)").bitcast(F32)

        offsets = keep.tile([P, S // LIST_ROWS], U16, name="offsets")
        gains = [tile([P, PACK], F32, "gains%d" % g) for g in range(GROUPS)]
        gain_of = [gains[u // PACK][:, u % PACK : u % PACK + 1] for u in range(PAGES)]
        ident = tile([P, P], F32, "ident")
        pages = [tile([P, T], F32, "page%d" % u) for u in range(PAGES)]
        picked = [tile([P, S], F32, "picked%d" % u) for u in range(PAGES)]
        tab_sc = tile([P, T], U8, "tab_sc", tag="quarter0")
        v_sc = tile([P, GROUPS, S], U8, "v_sc")
        w1_sc = tile([P, GROUPS, N], U8, "w1_sc")
        w4_sc = tile([P, GROUPS, N], U8, "w4_sc")

        nc.vector.memset(tab_sc[:].bitcast(I32), 0)
        nc.vector.memset(w1_sc[:].rearrange("p a n -> p (a n)").bitcast(I32), 0)
        nc.vector.memset(v_sc[:].rearrange("p a n -> p (a n)").bitcast(I32), 0)
        nc.gpsimd.memset(w4_sc[:].rearrange("p a n -> p (a n)").bitcast(I32), 0)
        make_identity(nc, ident[:])

        dealt_in = gT[S : 2 * S, :].rearrange("(p t) c -> t p c", t=PACK)
        dealt_out = out_0[S : 2 * S, :].rearrange("(p t) c -> t p c", t=PACK)
        page_in = [gT[block(u), :] for u in range(PACK)] + [dealt_in[t] for t in range(PACK)]
        page_out = [out_0[block(u), :] for u in range(PACK)] + [dealt_out[t] for t in range(PACK)]
        w4_cols = w4_words.rearrange("a p n t -> p a (n t)").bitcast(I32)

        def load_scales(dst, src, rows=range(4)):
            for r in rows:
                nc.sync.dma_start(
                    out=dst[r:P:32, :, :].bitcast(I32),
                    in_=src[:, r:16:4, :].bitcast(I32).rearrange("a q n -> q a n"),
                )

        def load_table(a):
            words = tile([P, T], I32, "tab%d" % a, tag="half%d" % a)
            nc.sync.dma_start(out=words[:], in_=tab_words[a].rearrange("p n t -> p (n t)").bitcast(I32))
            return words

        def load_w3(raw, a, first, count):
            nc.sync.dma_start(
                out=raw, in_=w3[S * a : S * (a + 1), first : first + count].rearrange("(p t) c -> p t c", t=PACK)
            )

        def load_w4(first, count, name):
            raw = tile([P, GROUPS, count], I32, name)
            nc.sync.dma_start(out=raw[:], in_=w4_cols[:, :, first : first + count])
            return raw

        nc.sync.dma_start(offsets[:], offs)
        tab = [tile([P, T], I32, "tab0", tag="half0")]
        first_words = tab_words[0].rearrange("p n t -> p (n t)").bitcast(I32)
        nc.sync.dma_start(out=tab[0][:, 0 : T // 2], in_=first_words[:, 0 : T // 2])
        for a in range(GROUPS):
            nc.sync.dma_start(out=tab_sc[4 * a : P : 8, :].bitcast(I32), in_=tab_scales[a].bitcast(I32))
        nc.sync.dma_start(out=tab[0][:, T // 2 : T], in_=first_words[:, T // 2 : T])
        load_scales(w1_sc, w1_scales, (0, 1, 2))
        tab.append(load_table(1))
        load_scales(w1_sc, w1_scales, (3,))
        spread_sc = tile([P, S], U8, "spread_sc")
        nc.vector.tensor_copy(spread_sc[:], tab_sc[:].indirect(offsets[:]))
        for q in range(4):
            nc.sync.dma_start(
                out=v_sc[32 * q : 32 * q + 4, :, :].bitcast(I32), in_=spread_sc[32 * q : 32 * q + 32 : 4, :].bitcast(I32)
            )
        w1_q = tile([P, GROUPS, 2 * N], U8, "w1_q", tag="quarter1")
        nc.sync.dma_start(out=w1_q[:].bitcast(I32), in_=w1_words.bitcast(I32).rearrange("a p c -> p a c"))
        for u in range(PAGES):
            nc.sync.dma_start(out=pages[u][:], in_=page_in[u])
            if u == 0:
                with nc.allow_non_contiguous_dma(reason="one gain a partition and page"):
                    nc.sync.dma_start(out=gains[0][:], in_=gain[0:S].rearrange("(u p) -> p u", u=PACK))
            if u == 1:
                nc.sync.dma_start(out=gains[1][:], in_=gain[S : 2 * S].rearrange("(p t) -> p t", t=PACK))
            if u == PACK:
                load_scales(w4_sc, w4_scales)

        v_q = [tile([P, S], I32, "v_q%d" % a) for a in range(GROUPS)]
        halves = [slice(HALF * h, HALF * (h + 1)) for h in range(2)]
        half_offsets = [offsets[:, HALF // LIST_ROWS * h : HALF // LIST_ROWS * (h + 1)] for h in range(2)]

        def gather_words(a, h):
            nc.vector.tensor_copy(v_q[a][:, halves[h]].bitcast(U32), tab[a][:].bitcast(U32).indirect(half_offsets[h]))

        for a in range(GROUPS):
            for h in range(2):
                gather_words(a, h)

        drafts = [bank(b, "draft%d" % b) for b in range(PAGES)]

        def draft_natural(u):
            for a in range(GROUPS):
                w1_cols = (w1_q[:, a, 2 * P * u : 2 * P * (u + 1)].bitcast(FP4X4), w1_sc[:, a, block(u)])
                mx_pass(drafts[u][:], w1_cols, (v_q[a][:].bitcast(FP8X4), v_sc[:, a, :]), a)

        def draft_turned(jb):
            for a in range(GROUPS):
                w1_cols = (w1_q[:, a, N : 2 * N].bitcast(FP4X4), w1_sc[:, a, S : 2 * S])
                mx_pass(drafts[PACK + jb][:], (v_q[a][:, block(jb)].bitcast(FP8X4), v_sc[:, a, block(jb)]), w1_cols, a)

        gained = {}
        gained_halves = {}
        draft_t = {}

        def tanh_natural(u):
            draft = small("draft%d" % u, u)
            nc.scalar.activation(draft[:], drafts[u][:], ACT.Tanh)
            gained[u] = small("gained%d" % u, PACK + u)
            nc.scalar.activation(gained[u][:], draft[:], ACT.Copy, scale=gain_of[u])

        def tanh_turned(jb):
            draft_t[jb] = small("draft_t%d" % jb, 2 * PACK + jb)
            nc.scalar.activation(
                draft_t[jb][:].rearrange("p (t m) -> p t m", t=PACK),
                drafts[PACK + jb][:].rearrange("p (m t) -> p t m", t=PACK),
                ACT.Tanh,
            )

        for natural, turned in ((draft_natural, draft_turned), (tanh_natural, tanh_turned)):
            for h in range(2):
                natural(h)
                turned(2 * h)
                turned(2 * h + 1)
            natural(2)
            natural(3)
        draft_back = {}
        for t in range(PACK):
            u = PACK + t
            back = bank(u, "draft_back%d" % t)
            draft_back[u] = back
            for jb in range(PACK):
                nc.tensor.transpose(back[:, block(jb)], draft_t[jb][:, block(t)], ident[:])
            if t >= 2:
                continue
            if t == 1:
                gained_halves[u] = [tile([P, HALF], F32, "gained5a", tag="z_q0")[:], small("gained5b", t)[:, 0:HALF]]
                for h in range(2):
                    nc.scalar.activation(gained_halves[u][h], back[:, halves[h]], ACT.Copy, scale=gain_of[u])
            else:
                gained[u] = small("gained%d" % u, t)
                nc.scalar.activation(gained[u][:], back[:], ACT.Copy, scale=gain_of[u])
        for u in gained:
            gained_halves[u] = [gained[u][:, cols] for cols in halves]

        def gather(u):
            for h in range(2):
                nc.vector.tensor_copy(picked[u][:, halves[h]], pages[u][:].indirect(half_offsets[h]))

        def form_z(out, u, h):
            nc.vector.scalar_tensor_tensor(out, picked[u][:, halves[h]], gain_of[u], gained_halves[u][h], ALU.mult, ALU.subtract)

        whole = slice(0, S)
        z_sc = [tile([P, S], U8, "z_sc%d" % a) for a in range(GROUPS)]
        z_turned = tile([P, PACK, 2, P, 2], BF16, "z_turned", tag="quarter2")
        for u in range(PACK):
            gather(u)
            for h in range(2):
                form_z(gained_halves[u][h], u, h)
            if u < PACK - 1:
                acc = bank(u, "z_turn%d" % u)
                for jb in range(PACK):
                    nc.tensor.transpose(acc[:, block(jb)], gained[u][:, block(jb)], ident[:])
                round_turned(z_turned[:], u, acc)
            else:
                for h in range(2):
                    acc = bank(u - h, "z_turn%d%d" % (u, h))
                    for k in range(2):
                        nc.tensor.transpose(acc[:, block(k)], gained[u][:, block(2 * h + k)], ident[:])
                    nc.scalar.copy(
                        z_turned[:, 2 * h : 2 * h + 2, :, 32 * u : 32 * (u + 1), :],
                        acc[:, 0:HALF].rearrange("p (k q h e) -> p k h q e", k=2, h=2, e=2),
                    )
        z_woven = [tile([P, S * PACK], BF16, "z_woven%d" % a, tag="quarter%d" % (3 + 2 * a)) for a in range(GROUPS)]
        turn_pairs_back(as_words(z_turned[:]), z_woven[0], (0, 1), "z_back")
        late_gained = tile([P, 2, S], F32, "late_gained", tag="quarter2")
        for i, u in enumerate((PAGES - 2, PAGES - 1)):
            nc.scalar.activation(late_gained[:, i, :], draft_back[u][:], ACT.Copy, scale=gain_of[u])
            gained_halves[u] = [late_gained[:, i, cols] for cols in halves]

        z_q = {}
        z_rows = tile([P, PACK, S], BF16, "z_rows", tag="quarter4")
        z_weave_dst, z_weave_src = weave_views(z_woven[1][:], z_rows[:])
        for t in range(PACK - 1):
            gather(PACK + t)
            for h in range(2):
                form_z(z_rows[:, t, halves[h]], PACK + t, h)
            if t == 1:
                z_q[0] = tile([P, S], I32, "z_q0")
                nc.vector.quantize_mx(out=z_q[0][:].bitcast(FP8X4), scales=z_sc[0][:], in_=z_woven[0][:])
                nc.scalar.copy(z_weave_dst[:, :, 0:2, :], z_weave_src[:, :, 0:2, :])
        last = PAGES - 1
        gather(last)
        for h in range(2):
            form_z(z_rows[:, PACK - 1, halves[h]], last, h)

        def z_operand(a, cols):
            return z_q[a][:, cols].bitcast(FP8X4), z_sc[a][:, cols]

        w3_raw = {}
        w3_q = {}
        w4_q = {}

        def load_w3_page(u):
            raw = tile([P, GROUPS, PACK, P], F32, "w3_raw%d" % u, tag="quarter%d" % u)
            for a in range(GROUPS):
                w3_raw[u, a] = raw[:, a]
                load_w3(w3_raw[u, a], a, P * u, P)

        load_w3_page(0)
        w4_natural = [load_w4(0, 2 * P, "w4_first")]
        load_w3_page(1)
        for a, tag in enumerate(("small7", "w3_pair1")):
            raw = tile([P, PACK, 2 * P], F32, "w3_pair%d" % a, tag=tag)
            load_w3(raw[:], a, 2 * P, 2 * P)
            for u in range(2):
                w3_raw[2 + u, a] = raw[:, :, block(u)]
        w4_natural.append(load_w4(2 * P, 2 * P, "w4_second"))
        w4_late = load_w4(S, S, "w4_late")
        w3_late = [tile([P, PACK, S], F32, "w3_late%d" % a, tag="half%d" % a) for a in range(GROUPS)]
        for a in range(GROUPS):
            load_w3(w3_late[a][:], a, S, S)
        for u in range(PACK):
            for a in range(GROUPS):
                w4_q[u, a] = (w4_natural[u // 2][:, a, block(u % 2)].bitcast(FP8X4), w4_sc[:, a, block(u)])
        w4_late_q = [(w4_late[:, a, :].bitcast(FP8X4), w4_sc[:, a, S : 2 * S]) for a in range(GROUPS)]

        w3_woven = {}
        w3_late_woven = {}
        w3_late_q = {}

        def weave_w3_page(u):
            w3_woven[u] = tile([P, GROUPS, P * PACK], BF16, "w3_woven%d" % u)
            for a in range(GROUPS):
                nc.scalar.copy(*weave_views(w3_woven[u][:, a, :], w3_raw[u, a]))

        def quantise_w3_page(u):
            codes = tile([P, GROUPS * P], I32, "w3_codes%d" % u)
            scales = tile([P, GROUPS * P], U8, "w3_scales%d" % u)
            nc.vector.quantize_mx(
                out=codes[:].bitcast(FP8X4), scales=scales[:], in_=w3_woven[u][:].rearrange("p a c -> p (a c)")
            )
            for a in range(GROUPS):
                w3_q[u, a] = (codes[:, block(a)].bitcast(FP8X4), scales[:, block(a)])

        def weave_w3_late(a):
            w3_late_woven[a] = tile([P, S * PACK], BF16, "w3_late_woven%d" % a, tag="quarter%d" % (4 + a))
            nc.scalar.copy(*weave_views(w3_late_woven[a][:], w3_late[a][:]))

        def quantise_w3_late(a):
            codes = tile([P, S], I32, "w3_late_codes%d" % a)
            scales = tile([P, S], U8, "w3_late_scales%d" % a)
            nc.vector.quantize_mx(out=codes[:].bitcast(FP8X4), scales=scales[:], in_=w3_late_woven[a][:])
            w3_late_q[a] = (codes[:].bitcast(FP8X4), scales[:])

        y3 = {}
        y4 = {}
        size = {}
        base = {}

        def products(u, bank3, bank4):
            y3[u] = bank(bank3, "y3_%d" % u)
            y4[u] = bank(bank4, "y4_%d" % u)
            for a in range(GROUPS):
                mx_pass(y3[u][:], w3_q[u, a], z_operand(a, whole), a)
                mx_pass(y4[u][:], w4_q[u, a], z_operand(a, whole), a)

        def take_abs(u, out):
            size[u] = out
            nc.scalar.activation(out[:], y3[u][:], ACT.Abs)

        def add_state(u, out):
            base[u] = out
            nc.vector.tensor_tensor(out[:], y4[u][:], picked[u][:], ALU.add)

        def scatter(u, first, second):
            nc.vector.tensor_tensor(pages[u][:].indirect(offsets[:]), first[:], second[:], ALU.add)

        def store_page(u):
            nc.sync.dma_start(out=page_out[u], in_=pages[u][:])

        y_sc = [tile([P, CHUNK], U8, "y_sc%d" % g) for g in range(GROUPS)]

        weave_w3_page(0)
        quantise_w3_page(0)
        for h in range(2):
            fours = slice(HALF // 4 * h, HALF // 4 * (h + 1))
            nc.vector.tensor_copy(z_weave_dst[:, fours, 2:4, :], z_weave_src[:, fours, 2:4, :])
        z_q[1] = tile([P, S], I32, "z_q1", tag="w3_woven0")
        for h in range(2):
            nc.vector.quantize_mx(
                out=z_q[1][:, halves[h]].bitcast(FP8X4),
                scales=z_sc[1][:, halves[h]],
                in_=z_woven[1][:, PACK * HALF * h : PACK * HALF * (h + 1)],
            )
        y3_half = [bank(b, "y3_half%d" % b)[:, 0:HALF] for b in (0, 4)]
        y4_half = [bank(b, "y4_half%d" % b)[:, 0:HALF] for b in (2, 5)]
        for accs, weights in ((y4_half, w4_q), (y3_half, w3_q)):
            for h in range(2):
                mx_pass(accs[h], weights[0, 0], z_operand(0, halves[h]), 0)
        for h in range(2):
            mx_pass(y3_half[h], w3_q[0, 1], z_operand(1, halves[h]), 1)
            mx_pass(y4_half[h], w4_q[0, 1], z_operand(1, halves[h]), 1)
        weave_w3_page(1)
        quantise_w3_page(1)
        size[0] = tile([P, S], F32, "size0", tag="quarter1")
        base[0] = tile([P, S], F32, "base0", tag="w3_woven1")
        for h in range(2):
            nc.scalar.activation(size[0][:, halves[h]], y3_half[h], ACT.Abs)
        products(1, 1, 3)
        for h in range(2):
            nc.vector.tensor_tensor(base[0][:, halves[h]], y4_half[h], picked[0][:, halves[h]], ALU.add)
            nc.vector.tensor_tensor(
                pages[0][:].indirect(half_offsets[h]), base[0][:, halves[h]], size[0][:, halves[h]], ALU.add
            )
        store_page(0)

        take_abs(1, small("size1", 2))
        pair_woven = tile([P, 2, GROUPS, P * PACK], BF16, "w3_pair_woven")
        for u in range(2):
            for a in range(GROUPS):
                nc.scalar.copy(*weave_views(pair_woven[:, u, a, :], w3_raw[2 + u, a]))
        pair_codes = tile([P, 2, GROUPS, P], I32, "w3_pair_codes")
        pair_scales = tile([P, 2, GROUPS, P], U8, "w3_pair_scales")
        nc.vector.quantize_mx(
            out=pair_codes[:].rearrange("p u a c -> p (u a c)").bitcast(FP8X4),
            scales=pair_scales[:].rearrange("p u a c -> p (u a c)"),
            in_=pair_woven[:].rearrange("p u a c -> p (u a c)"),
        )
        for u in range(2):
            for a in range(GROUPS):
                w3_q[2 + u, a] = (pair_codes[:, u, a, :].bitcast(FP8X4), pair_scales[:, u, a, :])
        products(2, 0, 2)
        add_state(1, tile([P, S], F32, "base1", tag="w3_pair_woven"))
        scatter(1, base[1], size[1])
        store_page(1)
        weave_w3_late(0)
        weave_w3_late(1)
        quantise_w3_late(0)
        take_abs(2, tile([P, S], F32, "size2", tag="quarter4"))
        products(3, 0, 3)
        quantise_w3_late(1)
        add_state(2, tile([P, S], F32, "base2", tag="quarter5"))
        scatter(2, base[2], size[2])
        store_page(2)
        take_abs(3, small("size3", 4))
        add_state(3, small("base3", 3))
        scatter(3, base[3], size[3])
        store_page(3)

        def turned_products(weights, banks, func, slot):
            out = tile([P, PACK, PACK, P], F32, "turned_" + slot, tag=slot)
            accs = [bank(b, "turned_%s%d" % (slot, b)) for b in banks]
            for a in range(GROUPS):
                for jb in range(PACK):
                    mx_pass(accs[jb][:], z_operand(a, block(jb)), weights[a], a)
            for jb in range(PACK):
                nc.scalar.activation(out[:, jb], accs[jb][:].rearrange("p (m t) -> p t m", t=PACK), func)
            return out

        def sum_turned(t, b):
            acc = bank(b, "sum%d" % t)
            for term, first, final in ((y4_t, 0, None), (size_t, None, PACK - 1)):
                for jb in range(PACK):
                    nc.tensor.matmul(
                        acc[:, block(jb)], term[:, jb, t], ident[:], start=(jb == first), stop=(jb == final), is_transpose=True
                    )
            out = small("sum%d" % t, PACK + 1 + t)
            nc.scalar.copy(out[:], acc[:])
            return out

        set_a, set_b = (1, 2, 4, 5), (0, 6, 7, 3)
        y4_t = turned_products(w4_late_q, (4, 5, 6, 7), ACT.Copy, "half1")
        size_t = turned_products(w3_late_q, set_a, ACT.Abs, "half0")
        sums = [sum_turned(t, set_b[t]) for t in range(PACK)]

        wide = {2: tile([P, PACK, CHUNK], F32, "wide2"), 3: tile([P, PACK, CHUNK], F32, "wide3", tag="half1")}
        for t in range(PACK):
            u = PACK + t
            scatter(u, picked[u], sums[t])
            for c in wide:
                nc.sync.dma_start(out=wide[c][:, t, :], in_=pages[u][:, CHUNK * c : CHUNK * (c + 1)])
            store_page(u)

        late_turned = tile([P, 2, PACK, 2, P, 2], BF16, "y_turned23", tag="half0")
        y_turned = [tile([P, PACK, 2, P, 2], BF16, "y_turned%d" % c, tag="quarter%d" % (2 * c))[:] for c in range(2)]
        y_turned.extend(late_turned[:, c] for c in range(2))
        y_woven = {}
        codes_out = [out_1[g].rearrange("p m t -> p (m t)").bitcast(I32) for g in range(GROUPS)]

        def new_woven(g, c):
            y_woven[g, c] = tile([P, CHUNK * PACK], BF16, "y_woven%d%d" % (g, c), tag="y_woven", bufs=RING)
            return y_woven[g, c]

        def quantise_chunk(g, c, codes):
            nc.vector.quantize_mx(out=codes[:].bitcast(FP8X4), scales=y_sc[g][4 * c : P, :], in_=y_woven[g, c][:])
            nc.sync.dma_start(out=codes_out[g][:, CHUNK * c : CHUNK * (c + 1)], in_=codes[:])

        def ring_codes(g, c):
            return tile([P, CHUNK], I32, "y_codes%d%d" % (g, c), tag="y_codes", bufs=RING)

        def store_scales(g):
            for q in range(4):
                nc.sync.dma_start(
                    out=out_2[g, 4 * q : 4 * q + 4, :].bitcast(I32).rearrange("r (c m) -> c r m", c=CHUNKS),
                    in_=y_sc[g][32 * q : 32 * q + 16, :].bitcast(I32),
                )

        for u in range(PACK):
            for c in range(CHUNKS):
                acc = bank((set_a, set_b)[u % 2][c], "turn%d%d" % (u, c))
                for k in range(PACK):
                    nc.tensor.transpose(acc[:, block(k)], pages[u][:, block(PACK * c + k)], ident[:])
                round_turned(y_turned[c], u, acc)
        both_sets = set_a + set_b
        for c in range(CHUNKS):
            turn_pairs_back(as_words(y_turned[c]), new_woven(0, c), both_sets[2 * c : 2 * c + 2], "back%d" % c)
        for c in range(CHUNKS):
            quantise_chunk(0, c, ring_codes(0, c))
        store_scales(0)

        dealt_turned = [tile([P, PACK, 2, P, 2], BF16, "dealt_turned%d" % c, tag="quarter%d" % (2 * c)) for c in range(2)]
        for h in range(2):
            for c in range(2):
                for half in range(2):
                    acc = bank((set_a, set_b)[h][2 * c + half], "pair%d%d%d" % (h, c, half))
                    for k in range(2):
                        for e in range(2):
                            cols = block(PACK * c + 2 * half + k)
                            nc.tensor.transpose(acc[:, block(2 * k + e)], pages[PACK + 2 * h + e][:, cols], ident[:])
                    nc.scalar.copy(
                        dealt_turned[c][:, 2 * half : 2 * half + 2, h, :, :],
                        acc[:].rearrange("p (k e m) -> p k m e", k=2, e=2),
                    )
        for c in range(2):
            turn_pairs_back(as_words(dealt_turned[c][:]), new_woven(1, c), set_a[2 * c : 2 * c + 2], "dealt_back%d" % c)

        nc.vector.tensor_copy(*weave_views(new_woven(1, 3)[:], wide[3][:]))
        quantise_chunk(1, 3, ring_codes(1, 3))
        quantise_chunk(1, 0, tile([P, CHUNK], I32, "y_codes10", tag="half1"))
        last_woven = new_woven(1, 2)
        column_halves = [slice(CHUNK // 2 * h, CHUNK // 2 * (h + 1)) for h in range(2)]
        woven_halves = [last_woven[:, PACK * cols.start : PACK * cols.stop] for cols in column_halves]
        for first, count in ((0, P), (P, P), (2 * P, 2 * P)):
            cols = slice(first, first + count)
            copy_on(first == 0, *weave_views(last_woven[:, PACK * cols.start : PACK * cols.stop], wide[2][:, :, cols]))
        quantise_chunk(1, 1, ring_codes(1, 1))
        last_codes = ring_codes(1, 2)
        for h, cols in enumerate(column_halves):
            nc.vector.quantize_mx(out=last_codes[:, cols].bitcast(FP8X4), scales=y_sc[1][8:P, cols], in_=woven_halves[h])
            nc.sync.dma_start(out=codes_out[1][:, 2 * CHUNK + cols.start : 2 * CHUNK + cols.stop], in_=last_codes[:, cols])
        store_scales(1)
